import numpy as np
import ml_dtypes


def mxq(x, axis, fmt="e4m3"):
    dtype, down = {"e4m3": (ml_dtypes.float8_e4m3fn, 7), "e5m2": (ml_dtypes.float8_e5m2, 14)}[fmt]
    v = np.moveaxis(np.asarray(x, np.float32).astype(ml_dtypes.bfloat16).astype(np.float64), axis, -1)
    blocks = v.reshape(v.shape[:-1] + (-1, 32))
    amax = np.abs(blocks).max(-1, keepdims=True)
    byte = np.maximum(np.where(amax > 0, np.frexp(amax)[1] - 1 + 127, 0) - down, 1)
    scale = np.exp2(byte - 127.0)
    codes = (blocks / scale).astype(np.float32).astype(dtype).astype(np.float64)
    return np.moveaxis((codes * scale).reshape(v.shape), -1, axis)


WIDE = False


def mx_kscale(k):
    if not WIDE:
        return np.ones(k)
    levels = np.array([10, -10, 5, -5, 0])
    if k % 512:
        return np.exp2(np.random.permutation(np.resize(levels, k // 32))).repeat(32)
    a = np.empty((k // 512, 16))
    for p in range(k // 512):
        a[p, :8] = np.random.permutation(np.resize(levels, 8))
        for g in range(8):
            far = levels[np.abs(levels - a[p, g]) >= 10]
            a[p, g + 8] = far[np.random.randint(len(far))]
    return np.exp2(a.ravel()).repeat(32)


def f64(x):
    return np.asarray(x).astype(np.float64)


def striped(idx):
    return np.tile(idx.reshape(-1, 16).T, (8, 1)).astype(np.uint16)


def unstriped(offs):
    return offs[:16].T.reshape(-1).astype(np.int64)


E2M1 = np.array([0.0, 0.5, 1.0, 1.5, 2.0, 3.0, 4.0, 6.0, -0.0, -0.5, -1.0, -1.5, -2.0, -3.0, -4.0, -6.0])


def pack_weight(w, fmt):
    k, n = w.shape
    w = f64(np.asarray(w, np.float32).astype(ml_dtypes.bfloat16)).reshape(k // 32, 32, n)
    amax = np.abs(w).max(1)
    if fmt == "e4m3":
        byte = np.frexp(amax)[1] - 1 + 127 - 7
    else:
        mant, ex = np.frexp(amax / 6.0)
        byte = np.where(mant > 0.5, ex, ex - 1) + 127
    byte = np.clip(np.where(amax > 0, byte, 1), 1, 254)
    scaled = (w * np.exp2(127.0 - byte)[:, None, :]).reshape(k, n).astype(np.float32)
    by_word = np.ascontiguousarray(scaled.reshape(k // 512, 128, 4, n).transpose(0, 1, 3, 2))
    if fmt == "e4m3":
        words = by_word.astype(ml_dtypes.float8_e4m3fn).view(np.uint8)
    else:
        c = by_word.astype(ml_dtypes.float4_e2m1fn).view(np.uint8) & 0xF
        words = (c[..., 0::2] | (c[..., 1::2] << 4)).reshape(k // 512, 128, 2 * n)
    return np.ascontiguousarray(words), np.ascontiguousarray(byte.astype(np.uint8).reshape(k // 512, 16, n))


def unpack_weight(words, scales, fmt):
    g, _, n = scales.shape
    words = np.ascontiguousarray(words).reshape(g, 128, n, -1)
    if fmt == "e4m3":
        vals = words.view(ml_dtypes.float8_e4m3fn).astype(np.float64)
    else:
        nib = np.empty((g, 128, n, 4), np.uint8)
        nib[..., 0::2] = words & 0xF
        nib[..., 1::2] = words >> 4
        vals = E2M1[nib]
    vals = vals * np.repeat(np.exp2(scales.astype(np.float64) - 127.0), 8, axis=1)[..., None]
    return vals.transpose(0, 1, 3, 2).reshape(g * 512, n)


def gelu(v):
    return 0.5 * v * (1.0 + np.tanh(np.sqrt(2.0 / np.pi) * (v + 0.044715 * v**3)))


K, H, T, S, P = 1536, 1024, 4096, 1024, 512


def setup_inputs():
    n = np.random.standard_normal
    s = mx_kscale(K)[:, None]
    u = mx_kscale(H)[:, None]
    tab_words, tab_scales = pack_weight(n((K, T)) * s, "e4m3")
    w2_words, w2_scales = pack_weight(2.0 * n((H, H)) / np.sqrt(H) / u, "e2m1")
    return {
        "tab_words": tab_words, "tab_scales": tab_scales,
        "offs": striped(np.random.permutation(T)[:S]),
        "pos1": striped(np.random.permutation(S)[:P]),
        "pos2": striped(np.random.permutation(S)[:P]),
        "w1": (1.2 * n((K, H)) / np.sqrt(K) / s).astype(np.float32),
        "gain": (np.random.uniform(0.6, 1.6, H) * u[:, 0]).astype(np.float32),
        "w2_words": w2_words, "w2_scales": w2_scales,
    }


def reference(tab_words, tab_scales, offs, pos1, pos2, w1, gain, w2_words, w2_scales):
    v = unpack_weight(tab_words, tab_scales, "e4m3")[:, unstriped(offs)]
    h = mxq(f64(w1), 0, "e4m3").T @ v
    x = h[:, unstriped(pos1)]
    ge = 0.5 * x * (1.0 + np.tanh(np.sqrt(2.0 / np.pi) * (x + 0.044715 * x ** 3)))
    z = mxq(ge * f64(gain)[:, None], 0, "e4m3")
    w2 = unpack_weight(w2_words, w2_scales, "e2m1")
    y = w2.T @ z
    gate = 1.0 / (1.0 + np.exp(-y))
    return gate * h[:, unstriped(pos2)]

@@ -1,0 +1,212 @@
+from contextlib import ExitStack
+
+import concourse.mybir as mybir
+
+K, H, T, S, M = 1536, 1024, 4096, 1024, 512
+FLOPS = 2 * K * H * S + 2 * H * H * M
+
+F32 = mybir.dt.float32
+BF16 = mybir.dt.bfloat16
+I32 = mybir.dt.int32
+U32 = mybir.dt.uint32
+U16 = mybir.dt.uint16
+U8 = mybir.dt.uint8
+FP8X4 = mybir.dt.float8_e4m3fn_x4
+FP4X4 = mybir.dt.float4_e2m1fn_x4
+ACT = mybir.ActivationFunctionType
+MULT = mybir.AluOpType.mult
+
+P = 128
+PACK = 4
+KP = K // (P * PACK)
+HP = H // (P * PACK)
+TILES = H // P
+BANK = 512
+CW = 256
+CHUNKS = H // CW
+W1_LOADS = [(0, 256), (256, 256), (512, 512)]
+
+
+def tile_list_citation_chain_gate_kernel(tc, tab_words, tab_scales, offs, pos1, pos2, w1, gain, w2_words, w2_scales, out):
+    nc = tc.nc
+    with ExitStack() as ctx:
+        keep = ctx.enter_context(tc.tile_pool(name="keep", bufs=1))
+        ring = ctx.enter_context(tc.tile_pool(name="ring", bufs=3))
+        psum = ctx.enter_context(tc.psum_pool(name="psum", bufs=8))
+
+        offs_sb = keep.tile([P, S // 16], U16, name="offs_sb")
+        pos1_sb = keep.tile([P, M // 16], U16, name="pos1_sb")
+        pos2_sb = keep.tile([P, M // 16], U16, name="pos2_sb")
+        tab = [keep.tile([P, T], I32, name=f"tab{a}", align_bytes=64) for a in range(KP)]
+        tab_sc = keep.tile([P, T], U8, name="tab_sc")
+        w1_raw = {}
+        for n0, width in W1_LOADS:
+            for a in range(KP):
+                w1_raw[n0, a] = keep.tile([P, PACK, width], F32, name=f"w1_raw{n0}_{a}")
+        gain_sb = keep.tile([P, TILES], F32, name="gain_sb")
+        w2_w = keep.tile([P, HP, 2 * H], U8, name="w2_w", align_bytes=64)
+        w2_s = keep.tile([P, HP, H], U8, name="w2_s", align_bytes=64)
+
+        nc.vector.memset(tab_sc[:].bitcast(I32), 0)
+        nc.vector.memset(w2_s[:].rearrange("p a n -> p (a n)").bitcast(I32), 0)
+
+        def load_tab(a):
+            nc.sync.dma_start(out=tab[a][:], in_=tab_words[a].rearrange("p t i -> p (t i)").bitcast(I32))
+
+        def load_w1(n0, width):
+            for a in range(KP):
+                rows = w1[a * P * PACK : (a + 1) * P * PACK, n0 : n0 + width]
+                nc.sync.dma_start(out=w1_raw[n0, a][:], in_=rows.rearrange("(p j) n -> p j n", j=PACK))
+
+        nc.sync.dma_start(offs_sb[:], offs)
+        load_tab(0)
+        load_w1(*W1_LOADS[0])
+        for q in range(4):
+            nc.scalar.dma_start(
+                out=tab_sc[32 * q : 32 * q + 4 * KP, :].bitcast(I32),
+                in_=tab_scales[:, 4 * q : 4 * q + 4, :].bitcast(I32),
+            )
+        with nc.allow_non_contiguous_dma(reason="one gain a partition and tile"):
+            nc.scalar.dma_start(out=gain_sb[:], in_=gain.rearrange("(j p) -> p j", p=P))
+        load_tab(1)
+        nc.sync.dma_start(pos1_sb[:], pos1)
+        load_tab(2)
+        load_w1(*W1_LOADS[1])
+        nc.sync.dma_start(pos2_sb[:], pos2)
+        load_w1(*W1_LOADS[2])
+        nc.sync.dma_start(out=w2_w[:].bitcast(I32), in_=w2_words.rearrange("a p n -> p a n").bitcast(I32))
+        for q in range(4):
+            nc.sync.dma_start(
+                out=w2_s[32 * q : 32 * q + 4, :, :].bitcast(I32),
+                in_=w2_scales[:, 4 * q : 4 * q + 4, :].rearrange("a r n -> r a n").bitcast(I32),
+            )
+
+        v_w = [keep.tile([P, S], U32, name=f"v_w{a}", align_bytes=64) for a in range(KP)]
+        v_s = keep.tile([P, S], U8, name="v_s", align_bytes=64)
+
+        def gather_tab(a, pieces):
+            step = S // pieces
+            for s0 in range(0, S, step):
+                nc.vector.tensor_copy(v_w[a][:, s0 : s0 + step], tab[a][:].bitcast(U32).indirect(offs_sb[:, s0 // 16 : (s0 + step) // 16]))
+
+        w1_c = {}
+        w1_s = {}
+
+        def quantise_w1(c, a, grouped):
+            n0, width = [ld for ld in W1_LOADS if ld[0] <= c * CW][-1]
+            src = w1_raw[n0, a][:, :, c * CW - n0 : (c + 1) * CW - n0].rearrange("p t (g i) -> p g t i", i=4)
+            nc.scalar.copy(out=grouped.rearrange("p (g i t) -> p g t i", i=4, t=PACK), in_=src)
+            w1_c[c, a] = keep.tile([P, CW], U32, name=f"w1_c{c}_{a}", align_bytes=64)
+            w1_s[c, a] = keep.tile([P, CW], U8, name=f"w1_s{c}_{a}", align_bytes=64)
+            nc.vector.quantize_mx(out=w1_c[c, a][:].bitcast(FP8X4), scales=w1_s[c, a][:], in_=grouped)
+
+        h = [keep.tile([P, S], F32, name=f"h{j}") for j in range(TILES)]
+
+        def first_product(j):
+            c, cols = divmod(j * P, CW)
+            for s0 in range(0, S, BANK):
+                acc = psum.tile([P, BANK], F32, name="acc")
+                for a in range(KP):
+                    nc.tensor.matmul_mx(
+                        out=acc[:],
+                        lhsT=w1_c[c, a][:, cols : cols + P].bitcast(FP8X4),
+                        lhsT_scale=w1_s[c, a][:, cols : cols + P],
+                        rhs=v_w[a][:, s0 : s0 + BANK].bitcast(FP8X4),
+                        rhs_scale=v_s[4 * a :, s0 : s0 + BANK],
+                        start=(a == 0),
+                        stop=(a == KP - 1),
+                    )
+                nc.scalar.copy(out=h[j][:, s0 : s0 + BANK], in_=acc[:])
+
+        z_slots = [keep.tile([P, PACK, M], BF16, name=f"z_slots{b}") for b in range(HP)]
+
+        xs = {}
+
+        def gather_x(j):
+            xs[j] = keep.tile([P, M], F32, name=f"x{j}", tag=f"x{j}")
+            nc.vector.tensor_copy(xs[j][:], h[j][:].indirect(pos1_sb[:]))
+
+        def probe(ap, dtype, name):
+            t = keep.tile([P, 1], dtype, name=name)
+            nc.gpsimd.tensor_copy(out=t[:], in_=ap)
+
+        def make_z(j):
+            x = xs[j]
+            ge = keep.tile([P, M], F32, name=f"ge{j}", tag=f"ge{j % 2}")
+            nc.scalar.activation(out=ge[:], in_=x[:], func=ACT.Gelu_apprx_tanh)
+            zb = ring.tile([P, M], BF16, name="zb", bufs=4)
+            nc.vector.tensor_scalar(out=zb[:], in0=ge[:], scalar1=gain_sb[:, j : j + 1], scalar2=None, op0=MULT)
+            b, q = divmod(j, 4)
+            for i in range(PACK):
+                nc.sync.dma_start(out=z_slots[b][32 * q : 32 * q + 32, i, :], in_=zb[i:P:PACK, :])
+
+        z_c = [keep.tile([P, M], U32, name=f"z_c{b}", align_bytes=64) for b in range(HP)]
+        z_s = [keep.tile([P, M], U8, name=f"z_s{b}", align_bytes=64) for b in range(HP)]
+
+        def quantise_z(b):
+            z_grouped = keep.tile([P, M, PACK], BF16, name=f"z_grouped{b}", tag="z_grouped", align_bytes=64)
+            nc.vector.tensor_copy(
+                out=z_grouped[:].rearrange("p (g i) t -> p g t i", i=4),
+                in_=z_slots[b][:].rearrange("p t (g i) -> p g t i", i=4),
+            )
+            nc.vector.quantize_mx(out=z_c[b][:].bitcast(FP8X4), scales=z_s[b][:], in_=z_grouped[:].rearrange("p m t -> p (m t)"))
+
+        cited = {}
+
+        def gather_h2(j, dst):
+            cited[j] = dst
+            nc.vector.tensor_copy(dst, h[j][:].indirect(pos2_sb[:]))
+
+        gather_tab(0, 1)
+        for a in range(KP):
+            grouped0 = ring.tile([P, CW * PACK], BF16, name="grouped0", align_bytes=64)
+            quantise_w1(0, a, grouped0[:])
+        nc.vector.tensor_copy(v_s[:], tab_sc[:].indirect(offs_sb[:]))
+        gather_tab(1, 1)
+        gather_tab(2, 2)
+        late = keep.tile([P, (CHUNKS - 1) * KP * CW * PACK], BF16, name="late", tag="tab2", align_bytes=64)
+
+        def quantise_late(c, a):
+            if c < CHUNKS:
+                at = ((c - 1) * KP + a) * CW * PACK
+                quantise_w1(c, a, late[:, at : at + CW * PACK])
+
+        for c in range(CHUNKS):
+            first_product(2 * c)
+            gather_x(2 * c)
+            quantise_late(c + 1, 0)
+            first_product(2 * c + 1)
+            gather_x(2 * c + 1)
+            quantise_late(c + 1, 1)
+            quantise_late(c + 1, 2)
+            for j in (2 * c, 2 * c + 1):
+                make_z(j)
+                if j < 5:
+                    h2 = keep.tile([P, M], F32, name=f"h2_{j}", tag=f"x{j}")
+                    gather_h2(j, h2[:])
+            if c == 1:
+                quantise_z(0)
+        h2_pair = keep.tile([P, 2, M], F32, name="h2_pair", tag="ge1")
+        gather_h2(5, h2_pair[:, 0, :])
+        gather_h2(6, h2_pair[:, 1, :])
+        quantise_z(1)
+        h2_last = keep.tile([P, M], F32, name="h2_last", tag="z_grouped", align_bytes=64)
+        gather_h2(7, h2_last[:])
+
+        y = [psum.tile([P, BANK], F32, name=f"y{j}", tag="acc") for j in range(TILES)]
+        for b in range(HP):
+            for j in range(TILES):
+                nc.tensor.matmul_mx(
+                    out=y[j][:],
+                    lhsT=w2_w[:, b, 2 * j * P : 2 * (j + 1) * P].bitcast(FP4X4),
+                    lhsT_scale=w2_s[:, b, j * P : (j + 1) * P],
+                    rhs=z_c[b][:].bitcast(FP8X4),
+                    rhs_scale=z_s[b][:],
+                    start=(b == 0),
+                    stop=(b == HP - 1),
+                )
+        for j in range(TILES):
+            gate = ring.tile([P, M], F32, name="gate")
+            nc.scalar.activation(out=gate[:], in_=y[j][:], func=ACT.Sigmoid)
+            nc.vector.tensor_tensor(out=cited[j], in0=gate[:], in1=cited[j], op=MULT)
+            nc.sync.dma_start(out=out[j * P : (j + 1) * P, :], in_=cited[j])

@@ -1,6 +1,7 @@
 from contextlib import ExitStack
 
 import concourse.mybir as mybir
+from concourse.masks import make_identity
 
 K, H, T, S, M = 1536, 1024, 4096, 1024, 512
 FLOPS = 2 * K * H * S + 2 * H * H * M
@@ -47,7 +48,19 @@ def tile_list_citation_chain_gate_kernel(tc, tab_words, tab_scales, offs, pos1, 
         w2_w = keep.tile([P, HP, 2 * H], U8, name="w2_w", align_bytes=64)
         w2_s = keep.tile([P, HP, H], U8, name="w2_s", align_bytes=64)
 
+        gain_rows = keep.tile([P, P], F32, name="gain_rows")
+        ident = keep.tile([P, P], F32, name="ident")
+        v_s = keep.tile([P, S], U8, name="v_s", align_bytes=64)
+        warm = keep.tile([P, 1], F32, name="warm")
+
         nc.vector.memset(tab_sc[:].bitcast(I32), 0)
+        nc.gpsimd.memset(gain_rows[:], 0.0)
+        nc.scalar.dma_start(out=gain_rows[0:TILES, :], in_=gain.rearrange("(j p) -> j p", p=P))
+        make_identity(nc, ident[:])
+        nc.scalar.activation(out=warm[:], in_=ident[:, 0:1], func=ACT.Gelu_apprx_tanh)
+        gain_ps = psum.tile([P, BANK], F32, name="gain_ps", tag="acc")
+        nc.tensor.transpose(gain_ps[:, 0:P], gain_rows[:], ident[:])
+        nc.scalar.copy(out=gain_sb[:], in_=gain_ps[:, 0:TILES])
         nc.vector.memset(w2_s[:].rearrange("p a n -> p (a n)").bitcast(I32), 0)
 
         def load_tab(a):
@@ -66,8 +79,6 @@ def tile_list_citation_chain_gate_kernel(tc, tab_words, tab_scales, offs, pos1, 
                 out=tab_sc[32 * q : 32 * q + 4 * KP, :].bitcast(I32),
                 in_=tab_scales[:, 4 * q : 4 * q + 4, :].bitcast(I32),
             )
-        with nc.allow_non_contiguous_dma(reason="one gain a partition and tile"):
-            nc.scalar.dma_start(out=gain_sb[:], in_=gain.rearrange("(j p) -> p j", p=P))
         load_tab(1)
         nc.sync.dma_start(pos1_sb[:], pos1)
         load_tab(2)
@@ -82,7 +93,6 @@ def tile_list_citation_chain_gate_kernel(tc, tab_words, tab_scales, offs, pos1, 
             )
 
         v_w = [keep.tile([P, S], U32, name=f"v_w{a}", align_bytes=64) for a in range(KP)]
-        v_s = keep.tile([P, S], U8, name="v_s", align_bytes=64)
 
         def gather_tab(a, pieces):
             step = S // pieces
@@ -95,7 +105,11 @@ def tile_list_citation_chain_gate_kernel(tc, tab_words, tab_scales, offs, pos1, 
         def quantise_w1(c, a, grouped):
             n0, width = [ld for ld in W1_LOADS if ld[0] <= c * CW][-1]
             src = w1_raw[n0, a][:, :, c * CW - n0 : (c + 1) * CW - n0].rearrange("p t (g i) -> p g t i", i=4)
-            nc.scalar.copy(out=grouped.rearrange("p (g i t) -> p g t i", i=4, t=PACK), in_=src)
+            dst = grouped.rearrange("p (g i t) -> p g t i", i=4, t=PACK)
+            if (c, a) == (1, 0):
+                nc.vector.tensor_copy(out=dst, in_=src)
+            else:
+                nc.scalar.copy(out=dst, in_=src)
             w1_c[c, a] = keep.tile([P, CW], U32, name=f"w1_c{c}_{a}", align_bytes=64)
             w1_s[c, a] = keep.tile([P, CW], U8, name=f"w1_s{c}_{a}", align_bytes=64)
             nc.vector.quantize_mx(out=w1_c[c, a][:].bitcast(FP8X4), scales=w1_s[c, a][:], in_=grouped)
@@ -123,16 +137,12 @@ def tile_list_citation_chain_gate_kernel(tc, tab_words, tab_scales, offs, pos1, 
         xs = {}
 
         def gather_x(j):
-            xs[j] = keep.tile([P, M], F32, name=f"x{j}", tag=f"x{j}")
+            xs[j] = keep.tile([P, M], F32, name=f"x{j}", tag=f"x{j}", align_bytes=64)
             nc.vector.tensor_copy(xs[j][:], h[j][:].indirect(pos1_sb[:]))
-
-        def probe(ap, dtype, name):
-            t = keep.tile([P, 1], dtype, name=name)
-            nc.gpsimd.tensor_copy(out=t[:], in_=ap)
 
         def make_z(j):
             x = xs[j]
-            ge = keep.tile([P, M], F32, name=f"ge{j}", tag=f"ge{j % 2}")
+            ge = keep.tile([P, M], F32, name=f"ge{j}", tag=f"ge{j}")
             nc.scalar.activation(out=ge[:], in_=x[:], func=ACT.Gelu_apprx_tanh)
             zb = ring.tile([P, M], BF16, name="zb", bufs=4)
             nc.vector.tensor_scalar(out=zb[:], in0=ge[:], scalar1=gain_sb[:, j : j + 1], scalar2=None, op0=MULT)
@@ -164,29 +174,49 @@ def tile_list_citation_chain_gate_kernel(tc, tab_words, tab_scales, offs, pos1, 
         nc.vector.tensor_copy(v_s[:], tab_sc[:].indirect(offs_sb[:]))
         gather_tab(1, 1)
         gather_tab(2, 2)
-        late = keep.tile([P, (CHUNKS - 1) * KP * CW * PACK], BF16, name="late", tag="tab2", align_bytes=64)
+        late = keep.tile([P, KP, CW * PACK], BF16, name="late", tag="tab2", align_bytes=64)
 
-        def quantise_late(c, a):
-            if c < CHUNKS:
-                at = ((c - 1) * KP + a) * CW * PACK
-                quantise_w1(c, a, late[:, at : at + CW * PACK])
+        def quantise_in(c, a, tag):
+            grouped = keep.tile([P, CW * PACK], BF16, name=f"grouped{c}_{a}", tag=tag, align_bytes=64)
+            quantise_w1(c, a, grouped[:])
 
-        for c in range(CHUNKS):
-            first_product(2 * c)
-            gather_x(2 * c)
-            quantise_late(c + 1, 0)
-            first_product(2 * c + 1)
-            gather_x(2 * c + 1)
-            quantise_late(c + 1, 1)
-            quantise_late(c + 1, 2)
-            for j in (2 * c, 2 * c + 1):
-                make_z(j)
-                if j < 5:
-                    h2 = keep.tile([P, M], F32, name=f"h2_{j}", tag=f"x{j}")
-                    gather_h2(j, h2[:])
-            if c == 1:
-                quantise_z(0)
-        h2_pair = keep.tile([P, 2, M], F32, name="h2_pair", tag="ge1")
+        def finish(j):
+            make_z(j)
+            if j < 5:
+                h2 = keep.tile([P, M], F32, name=f"h2_{j}", tag=f"ge{j}")
+                gather_h2(j, h2[:])
+
+        def start(j):
+            first_product(j)
+            gather_x(j)
+
+        quantise_w1(1, 0, late[:, 0, :])
+        start(0)
+        start(1)
+        quantise_w1(1, 1, late[:, 1, :])
+        quantise_w1(1, 2, late[:, 2, :])
+        finish(0)
+        finish(1)
+        start(2)
+        quantise_in(2, 0, "x0")
+        start(3)
+        quantise_in(2, 1, "x1")
+        quantise_in(2, 2, "x0")
+        finish(2)
+        finish(3)
+        start(4)
+        quantise_in(3, 0, "x2")
+        start(5)
+        quantise_in(3, 1, "x3")
+        quantise_in(3, 2, "x2")
+        quantise_z(0)
+        finish(4)
+        finish(5)
+        start(6)
+        start(7)
+        finish(6)
+        finish(7)
+        h2_pair = keep.tile([P, 2, M], F32, name="h2_pair", tag="ge7")
         gather_h2(5, h2_pair[:, 0, :])
         gather_h2(6, h2_pair[:, 1, :])
         quantise_z(1)

@@ -19,13 +19,12 @@ MULT = mybir.AluOpType.mult
 
 P = 128
 PACK = 4
-KP = K // (P * PACK)
-HP = H // (P * PACK)
+HALF = P * PACK
+KP = K // HALF
+HP = H // HALF
 TILES = H // P
 BANK = 512
 CW = 256
-CHUNKS = H // CW
-W1_LOADS = [(0, 256), (256, 256), (512, 512)]
 
 
 def tile_list_citation_chain_gate_kernel(tc, tab_words, tab_scales, offs, pos1, pos2, w1, gain, w2_words, w2_scales, out):
@@ -40,14 +39,15 @@ def tile_list_citation_chain_gate_kernel(tc, tab_words, tab_scales, offs, pos1, 
         pos2_sb = keep.tile([P, M // 16], U16, name="pos2_sb")
         tab = [keep.tile([P, T], I32, name=f"tab{a}", align_bytes=64) for a in range(KP)]
         tab_sc = keep.tile([P, T], U8, name="tab_sc")
-        w1_raw = {}
-        for n0, width in W1_LOADS:
-            for a in range(KP):
-                w1_raw[n0, a] = keep.tile([P, PACK, width], F32, name=f"w1_raw{n0}_{a}")
-        gain_sb = keep.tile([P, TILES], F32, name="gain_sb")
-        w2_w = keep.tile([P, HP, 2 * H], U8, name="w2_w", align_bytes=64)
+        w1_lo = {(c, a): keep.tile([P, PACK, CW], F32, name=f"w1_lo{c}_{a}") for c in range(2) for a in range(KP)}
+        w1_hi = [keep.tile([P, PACK, HALF], F32, name=f"w1_hi{a}") for a in range(KP)]
+        gain_lo = keep.tile([P, PACK], F32, name="gain_lo")
+        gain_hi = keep.tile([P, PACK], F32, name="gain_hi")
+        w2_lo = keep.tile([P, HP, 2 * HALF], U8, name="w2_lo", align_bytes=64)
+        w2_hi_raw = keep.tile([P, HP, 2 * HALF], U8, name="w2_hi_raw")
+        w2_hi = keep.tile([P, HP, 2 * HALF], U8, name="w2_hi", align_bytes=64)
         w2_s = keep.tile([P, HP, H], U8, name="w2_s", align_bytes=64)
-
+        w2_s_hi = keep.tile([P, HP, HALF], U8, name="w2_s_hi", align_bytes=64)
         gain_rows = keep.tile([P, P], F32, name="gain_rows")
         ident = keep.tile([P, P], F32, name="ident")
         v_s = keep.tile([P, S], U8, name="v_s", align_bytes=64)
@@ -55,42 +55,50 @@ def tile_list_citation_chain_gate_kernel(tc, tab_words, tab_scales, offs, pos1, 
 
         nc.vector.memset(tab_sc[:].bitcast(I32), 0)
         nc.gpsimd.memset(gain_rows[:], 0.0)
-        nc.scalar.dma_start(out=gain_rows[0:TILES, :], in_=gain.rearrange("(j p) -> j p", p=P))
+        nc.scalar.dma_start(out=gain_rows[0:PACK, :], in_=gain[0:HALF].rearrange("(j p) -> j p", p=P))
         make_identity(nc, ident[:])
         nc.scalar.activation(out=warm[:], in_=ident[:, 0:1], func=ACT.Gelu_apprx_tanh)
         gain_ps = psum.tile([P, BANK], F32, name="gain_ps", tag="acc")
         nc.tensor.transpose(gain_ps[:, 0:P], gain_rows[:], ident[:])
-        nc.scalar.copy(out=gain_sb[:], in_=gain_ps[:, 0:TILES])
+        nc.scalar.copy(out=gain_lo[:], in_=gain_ps[:, 0:PACK])
         nc.vector.memset(w2_s[:].rearrange("p a n -> p (a n)").bitcast(I32), 0)
 
         def load_tab(a):
             nc.sync.dma_start(out=tab[a][:], in_=tab_words[a].rearrange("p t i -> p (t i)").bitcast(I32))
 
-        def load_w1(n0, width):
-            for a in range(KP):
-                rows = w1[a * P * PACK : (a + 1) * P * PACK, n0 : n0 + width]
-                nc.sync.dma_start(out=w1_raw[n0, a][:], in_=rows.rearrange("(p j) n -> p j n", j=PACK))
+        def load_w1(dst, a, n0, width):
+            rows = w1[a * HALF : (a + 1) * HALF, n0 : n0 + width]
+            nc.sync.dma_start(out=dst[:], in_=rows.rearrange("(p j) n -> p j n", j=PACK))
+
+        def load_w2(dst, half):
+            cols = w2_words[:, :, half * 2 * HALF : (half + 1) * 2 * HALF]
+            nc.sync.dma_start(out=dst[:].bitcast(I32), in_=cols.rearrange("a p n -> p a n").bitcast(I32))
 
         nc.sync.dma_start(offs_sb[:], offs)
         load_tab(0)
-        load_w1(*W1_LOADS[0])
+        for a in range(KP):
+            load_w1(w1_lo[0, a], a, 0, CW)
         for q in range(4):
             nc.scalar.dma_start(
                 out=tab_sc[32 * q : 32 * q + 4 * KP, :].bitcast(I32),
                 in_=tab_scales[:, 4 * q : 4 * q + 4, :].bitcast(I32),
             )
         load_tab(1)
-        nc.sync.dma_start(pos1_sb[:], pos1)
-        load_tab(2)
-        load_w1(*W1_LOADS[1])
-        nc.sync.dma_start(pos2_sb[:], pos2)
-        load_w1(*W1_LOADS[2])
-        nc.sync.dma_start(out=w2_w[:].bitcast(I32), in_=w2_words.rearrange("a p n -> p a n").bitcast(I32))
+        load_w2(w2_hi_raw, 1)
         for q in range(4):
             nc.sync.dma_start(
                 out=w2_s[32 * q : 32 * q + 4, :, :].bitcast(I32),
                 in_=w2_scales[:, 4 * q : 4 * q + 4, :].rearrange("a r n -> r a n").bitcast(I32),
             )
+        nc.sync.dma_start(out=gain_hi[:], in_=gain[HALF:].rearrange("(p t) -> p t", t=PACK))
+        nc.sync.dma_start(pos1_sb[:], pos1)
+        load_tab(2)
+        for a in range(KP):
+            load_w1(w1_lo[1, a], a, CW, CW)
+        nc.sync.dma_start(pos2_sb[:], pos2)
+        for a in range(KP):
+            load_w1(w1_hi[a], a, HALF, HALF)
+        load_w2(w2_lo, 0)
 
         v_w = [keep.tile([P, S], U32, name=f"v_w{a}", align_bytes=64) for a in range(KP)]
 
@@ -99,56 +107,64 @@ def tile_list_citation_chain_gate_kernel(tc, tab_words, tab_scales, offs, pos1, 
             for s0 in range(0, S, step):
                 nc.vector.tensor_copy(v_w[a][:, s0 : s0 + step], tab[a][:].bitcast(U32).indirect(offs_sb[:, s0 // 16 : (s0 + step) // 16]))
 
-        w1_c = {}
-        w1_s = {}
+        w1_c = [keep.tile([P, H], U32, name=f"w1_c{a}", align_bytes=64) for a in range(KP)]
+        w1_s = [keep.tile([P, H], U8, name=f"w1_s{a}", align_bytes=64) for a in range(KP)]
 
-        def quantise_w1(c, a, grouped):
-            n0, width = [ld for ld in W1_LOADS if ld[0] <= c * CW][-1]
-            src = w1_raw[n0, a][:, :, c * CW - n0 : (c + 1) * CW - n0].rearrange("p t (g i) -> p g t i", i=4)
-            dst = grouped.rearrange("p (g i t) -> p g t i", i=4, t=PACK)
-            if (c, a) == (1, 0):
-                nc.vector.tensor_copy(out=dst, in_=src)
-            else:
-                nc.scalar.copy(out=dst, in_=src)
-            w1_c[c, a] = keep.tile([P, CW], U32, name=f"w1_c{c}_{a}", align_bytes=64)
-            w1_s[c, a] = keep.tile([P, CW], U8, name=f"w1_s{c}_{a}", align_bytes=64)
-            nc.vector.quantize_mx(out=w1_c[c, a][:].bitcast(FP8X4), scales=w1_s[c, a][:], in_=grouped)
+        def quantise_w1(a, n0, width, grouped):
+            nc.vector.quantize_mx(out=w1_c[a][:, n0 : n0 + width].bitcast(FP8X4), scales=w1_s[a][:, n0 : n0 + width], in_=grouped)
+
+        def w1_low(c, a, grouped, copy):
+            copy(
+                out=grouped.rearrange("p (g i j) -> p g j i", i=4, j=PACK),
+                in_=w1_lo[c, a][:].rearrange("p j (g i) -> p g j i", i=4),
+            )
+            quantise_w1(a, c * CW, CW, grouped)
+
+        def round_high(a, half, grouped, copy):
+            ms = slice(half * P // 2, (half + 1) * P // 2)
+            copy(
+                out=grouped[:].rearrange("p (t m j) -> p m j t", t=PACK, j=PACK)[:, ms],
+                in_=w1_hi[a][:].rearrange("p j (m t) -> p m j t", t=PACK)[:, ms],
+            )
 
         h = [keep.tile([P, S], F32, name=f"h{j}") for j in range(TILES)]
+        xs = {}
+        x_low = [keep.tile([P, M], F32, name=f"x{j}", align_bytes=64) for j in range(PACK)]
 
-        def first_product(j):
-            c, cols = divmod(j * P, CW)
+        def start(j, x):
+            cols = slice(j * P, (j + 1) * P)
             for s0 in range(0, S, BANK):
                 acc = psum.tile([P, BANK], F32, name="acc")
                 for a in range(KP):
                     nc.tensor.matmul_mx(
                         out=acc[:],
-                        lhsT=w1_c[c, a][:, cols : cols + P].bitcast(FP8X4),
-                        lhsT_scale=w1_s[c, a][:, cols : cols + P],
+                        lhsT=w1_c[a][:, cols].bitcast(FP8X4),
+                        lhsT_scale=w1_s[a][:, cols],
                         rhs=v_w[a][:, s0 : s0 + BANK].bitcast(FP8X4),
                         rhs_scale=v_s[4 * a :, s0 : s0 + BANK],
                         start=(a == 0),
                         stop=(a == KP - 1),
                     )
                 nc.scalar.copy(out=h[j][:, s0 : s0 + BANK], in_=acc[:])
+            xs[j] = x
+            nc.vector.tensor_copy(x, h[j][:].indirect(pos1_sb[:]))
 
         z_slots = [keep.tile([P, PACK, M], BF16, name=f"z_slots{b}") for b in range(HP)]
 
-        xs = {}
+        def gelu(j):
+            ge = keep.tile([P, M], F32, name=f"ge{j}", tag=f"ge{j % PACK}", align_bytes=64)
+            nc.scalar.activation(out=ge[:], in_=xs[j], func=ACT.Gelu_apprx_tanh)
+            return ge
 
-        def gather_x(j):
-            xs[j] = keep.tile([P, M], F32, name=f"x{j}", tag=f"x{j}", align_bytes=64)
-            nc.vector.tensor_copy(xs[j][:], h[j][:].indirect(pos1_sb[:]))
-
-        def make_z(j):
-            x = xs[j]
-            ge = keep.tile([P, M], F32, name=f"ge{j}", tag=f"ge{j}")
-            nc.scalar.activation(out=ge[:], in_=x[:], func=ACT.Gelu_apprx_tanh)
+        def z_low(j):
+            ge = gelu(j)
             zb = ring.tile([P, M], BF16, name="zb", bufs=4)
-            nc.vector.tensor_scalar(out=zb[:], in0=ge[:], scalar1=gain_sb[:, j : j + 1], scalar2=None, op0=MULT)
-            b, q = divmod(j, 4)
+            nc.vector.tensor_scalar(out=zb[:], in0=ge[:], scalar1=gain_lo[:, j : j + 1], scalar2=None, op0=MULT)
             for i in range(PACK):
-                nc.sync.dma_start(out=z_slots[b][32 * q : 32 * q + 32, i, :], in_=zb[i:P:PACK, :])
+                nc.sync.dma_start(out=z_slots[0][32 * j : 32 * j + 32, i, :], in_=zb[i:P:PACK, :])
+
+        def z_high(t, ge):
+            nc.scalar.activation(out=z_slots[1][:, t, :], in_=ge[:], func=ACT.Copy, scale=gain_hi[:, t : t + 1])
 
         z_c = [keep.tile([P, M], U32, name=f"z_c{b}", align_bytes=64) for b in range(HP)]
         z_s = [keep.tile([P, M], U8, name=f"z_s{b}", align_bytes=64) for b in range(HP)]
@@ -161,82 +177,95 @@ def tile_list_citation_chain_gate_kernel(tc, tab_words, tab_scales, offs, pos1, 
             )
             nc.vector.quantize_mx(out=z_c[b][:].bitcast(FP8X4), scales=z_s[b][:], in_=z_grouped[:].rearrange("p m t -> p (m t)"))
 
-        cited = {}
+        citing = {}
 
-        def gather_h2(j, dst):
-            cited[j] = dst
-            nc.vector.tensor_copy(dst, h[j][:].indirect(pos2_sb[:]))
+        def gather_citing(tiles, tag):
+            picked = keep.tile([P, len(tiles), M], F32, name=f"citing{tiles[0]}", tag=tag, align_bytes=64)
+            for n, j in enumerate(tiles):
+                citing[j] = picked[:, n, :]
+                nc.vector.tensor_copy(citing[j], h[j][:].indirect(pos2_sb[:]))
 
         gather_tab(0, 1)
         for a in range(KP):
             grouped0 = ring.tile([P, CW * PACK], BF16, name="grouped0", align_bytes=64)
-            quantise_w1(0, a, grouped0[:])
+            w1_low(0, a, grouped0[:], nc.scalar.copy)
         nc.vector.tensor_copy(v_s[:], tab_sc[:].indirect(offs_sb[:]))
         gather_tab(1, 1)
+        nc.vector.tensor_copy(
+            out=w2_hi[:].bitcast(U16).rearrange("p a (t m) -> p a t m", t=PACK),
+            in_=w2_hi_raw[:].bitcast(U16).rearrange("p a (m t) -> p a t m", t=PACK),
+        )
+        nc.vector.tensor_copy(
+            out=w2_s_hi[:].rearrange("p a (t m) -> p a t m", t=PACK),
+            in_=w2_s[:, :, HALF:].rearrange("p a (m t) -> p a t m", t=PACK),
+        )
         gather_tab(2, 2)
-        late = keep.tile([P, KP, CW * PACK], BF16, name="late", tag="tab2", align_bytes=64)
 
-        def quantise_in(c, a, tag):
-            grouped = keep.tile([P, CW * PACK], BF16, name=f"grouped{c}_{a}", tag=tag, align_bytes=64)
-            quantise_w1(c, a, grouped[:])
-
-        def finish(j):
-            make_z(j)
-            if j < 5:
-                h2 = keep.tile([P, M], F32, name=f"h2_{j}", tag=f"ge{j}")
-                gather_h2(j, h2[:])
-
-        def start(j):
-            first_product(j)
-            gather_x(j)
-
-        quantise_w1(1, 0, late[:, 0, :])
-        start(0)
-        start(1)
-        quantise_w1(1, 1, late[:, 1, :])
-        quantise_w1(1, 2, late[:, 2, :])
-        finish(0)
-        finish(1)
-        start(2)
-        quantise_in(2, 0, "x0")
-        start(3)
-        quantise_in(2, 1, "x1")
-        quantise_in(2, 2, "x0")
-        finish(2)
-        finish(3)
-        start(4)
-        quantise_in(3, 0, "x2")
-        start(5)
-        quantise_in(3, 1, "x3")
-        quantise_in(3, 2, "x2")
+        grouped1 = keep.tile([P, KP, CW * PACK], BF16, name="grouped1", tag="tab2", align_bytes=64)
+        w1_low(1, 0, grouped1[:, 0, :], nc.vector.tensor_copy)
+        start(0, x_low[0][:])
+        start(1, x_low[1][:])
+        w1_low(1, 1, grouped1[:, 1, :], nc.scalar.copy)
+        w1_low(1, 2, grouped1[:, 2, :], nc.scalar.copy)
+        gather_citing([0, 1], "tab2")
+        z_low(0)
+        z_low(1)
+        high0 = keep.tile([P, HALF * PACK], BF16, name="high0", tag="x0", align_bytes=64)
+        round_high(0, 0, high0, nc.scalar.copy)
+        start(2, x_low[2][:])
+        gather_citing([2], "citing2")
+        start(3, x_low[3][:])
+        round_high(0, 1, high0, nc.scalar.copy)
+        quantise_w1(0, HALF, HALF, high0[:])
+        high1 = keep.tile([P, HALF * PACK], BF16, name="high1", tag="x1", align_bytes=64)
+        round_high(1, 0, high1, nc.scalar.copy)
+        z_low(2)
+        z_low(3)
+        round_high(1, 1, high1, nc.vector.tensor_copy)
+        quantise_w1(1, HALF, HALF, high1[:])
+        high2 = keep.tile([P, HALF * PACK], BF16, name="high2", tag="x3", align_bytes=64)
+        round_high(2, 0, high2, nc.scalar.copy)
+        round_high(2, 1, high2, nc.vector.tensor_copy)
+        for c in range(2):
+            quantise_w1(2, HALF + c * CW, CW, high2[:, c * CW * PACK : (c + 1) * CW * PACK])
+        gather_citing([3], "x3")
         quantise_z(0)
-        finish(4)
-        finish(5)
-        start(6)
-        start(7)
-        finish(6)
-        finish(7)
-        h2_pair = keep.tile([P, 2, M], F32, name="h2_pair", tag="ge7")
-        gather_h2(5, h2_pair[:, 0, :])
-        gather_h2(6, h2_pair[:, 1, :])
+        x_high = keep.tile([P, PACK, M], F32, name="x_high", tag="z_grouped", align_bytes=64)
+        for t in range(PACK):
+            start(PACK + t, x_high[:, t, :])
+        ge_high = [gelu(PACK)]
+        for t in range(PACK):
+            if t + 1 < PACK:
+                ge_high.append(gelu(PACK + t + 1))
+            z_high(t, ge_high[t])
+        gather_citing([4, 5], "ge0")
         quantise_z(1)
-        h2_last = keep.tile([P, M], F32, name="h2_last", tag="z_grouped", align_bytes=64)
-        gather_h2(7, h2_last[:])
+        gather_citing([6], "z_grouped")
 
         y = [psum.tile([P, BANK], F32, name=f"y{j}", tag="acc") for j in range(TILES)]
+        order = [TILES - 1] + list(range(TILES - 1))
         for b in range(HP):
-            for j in range(TILES):
+            for j in order if b else range(TILES):
+                n = j % PACK
+                words, scales = (w2_lo, w2_s) if j < PACK else (w2_hi, w2_s_hi)
                 nc.tensor.matmul_mx(
                     out=y[j][:],
-                    lhsT=w2_w[:, b, 2 * j * P : 2 * (j + 1) * P].bitcast(FP4X4),
-                    lhsT_scale=w2_s[:, b, j * P : (j + 1) * P],
+                    lhsT=words[:, b, 2 * n * P : 2 * (n + 1) * P].bitcast(FP4X4),
+                    lhsT_scale=scales[:, b, n * P : (n + 1) * P],
                     rhs=z_c[b][:].bitcast(FP8X4),
                     rhs_scale=z_s[b][:],
                     start=(b == 0),
                     stop=(b == HP - 1),
                 )
-        for j in range(TILES):
-            gate = ring.tile([P, M], F32, name="gate")
+        out_hi = out[HALF:, :].rearrange("(p t) m -> p t m", t=PACK)
+        for j in order:
+            gate = ring.tile([P, M], F32, name="gate", bufs=4)
             nc.scalar.activation(out=gate[:], in_=y[j][:], func=ACT.Sigmoid)
-            nc.vector.tensor_tensor(out=cited[j], in0=gate[:], in1=cited[j], op=MULT)
-            nc.sync.dma_start(out=out[j * P : (j + 1) * P, :], in_=cited[j])
+            if j in citing:
+                gated = citing[j]
+                nc.vector.tensor_tensor(out=gated, in0=gate[:], in1=gated, op=MULT)
+            else:
+                last = keep.tile([P, M], F32, name="last", tag="ge3", align_bytes=64)
+                gated = last[:]
+                nc.vector.tensor_tensor(gated, h[j][:].indirect(pos2_sb[:]), gate[:], MULT)
+            nc.sync.dma_start(out=out[j * P : (j + 1) * P, :] if j < PACK else out_hi[:, j - PACK, :], in_=gated)

@@ -46,7 +46,8 @@ def tile_list_citation_chain_gate_kernel(tc, tab_words, tab_scales, offs, pos1, 
         w2_lo = keep.tile([P, HP, 2 * HALF], U8, name="w2_lo", align_bytes=64)
         w2_hi_raw = keep.tile([P, HP, 2 * HALF], U8, name="w2_hi_raw")
         w2_hi = keep.tile([P, HP, 2 * HALF], U8, name="w2_hi", align_bytes=64)
-        w2_s = keep.tile([P, HP, H], U8, name="w2_s", align_bytes=64)
+        w2_s_lo = keep.tile([P, HP, HALF], U8, name="w2_s_lo", align_bytes=64)
+        w2_s_hi_raw = keep.tile([P, HP, HALF], U8, name="w2_s_hi_raw")
         w2_s_hi = keep.tile([P, HP, HALF], U8, name="w2_s_hi", align_bytes=64)
         gain_rows = keep.tile([P, P], F32, name="gain_rows")
         ident = keep.tile([P, P], F32, name="ident")
@@ -61,7 +62,8 @@ def tile_list_citation_chain_gate_kernel(tc, tab_words, tab_scales, offs, pos1, 
         gain_ps = psum.tile([P, BANK], F32, name="gain_ps", tag="acc")
         nc.tensor.transpose(gain_ps[:, 0:P], gain_rows[:], ident[:])
         nc.scalar.copy(out=gain_lo[:], in_=gain_ps[:, 0:PACK])
-        nc.vector.memset(w2_s[:].rearrange("p a n -> p (a n)").bitcast(I32), 0)
+        for plane in (w2_s_hi_raw, w2_s_lo):
+            nc.vector.memset(plane[:].rearrange("p a n -> p (a n)").bitcast(I32), 0)
 
         def load_tab(a):
             nc.sync.dma_start(out=tab[a][:], in_=tab_words[a].rearrange("p t i -> p (t i)").bitcast(I32))
@@ -70,9 +72,12 @@ def tile_list_citation_chain_gate_kernel(tc, tab_words, tab_scales, offs, pos1, 
             rows = w1[a * HALF : (a + 1) * HALF, n0 : n0 + width]
             nc.sync.dma_start(out=dst[:], in_=rows.rearrange("(p j) n -> p j n", j=PACK))
 
-        def load_w2(dst, half):
+        def load_w2(dst, plane, half):
             cols = w2_words[:, :, half * 2 * HALF : (half + 1) * 2 * HALF]
             nc.sync.dma_start(out=dst[:].bitcast(I32), in_=cols.rearrange("a p n -> p a n").bitcast(I32))
+            for q in range(4):
+                rows = w2_scales[:, 4 * q : 4 * q + 4, half * HALF : (half + 1) * HALF]
+                nc.sync.dma_start(out=plane[32 * q : 32 * q + 4, :, :].bitcast(I32), in_=rows.rearrange("a r n -> r a n").bitcast(I32))
 
         nc.sync.dma_start(offs_sb[:], offs)
         load_tab(0)
@@ -84,21 +89,16 @@ def tile_list_citation_chain_gate_kernel(tc, tab_words, tab_scales, offs, pos1, 
                 in_=tab_scales[:, 4 * q : 4 * q + 4, :].bitcast(I32),
             )
         load_tab(1)
-        load_w2(w2_hi_raw, 1)
-        for q in range(4):
-            nc.sync.dma_start(
-                out=w2_s[32 * q : 32 * q + 4, :, :].bitcast(I32),
-                in_=w2_scales[:, 4 * q : 4 * q + 4, :].rearrange("a r n -> r a n").bitcast(I32),
-            )
-        nc.sync.dma_start(out=gain_hi[:], in_=gain[HALF:].rearrange("(p t) -> p t", t=PACK))
-        nc.sync.dma_start(pos1_sb[:], pos1)
+        load_w2(w2_hi_raw, w2_s_hi_raw, 1)
         load_tab(2)
+        nc.sync.dma_start(pos1_sb[:], pos1)
         for a in range(KP):
             load_w1(w1_lo[1, a], a, CW, CW)
         nc.sync.dma_start(pos2_sb[:], pos2)
+        nc.sync.dma_start(out=gain_hi[:], in_=gain[HALF:].rearrange("(p t) -> p t", t=PACK))
         for a in range(KP):
             load_w1(w1_hi[a], a, HALF, HALF)
-        load_w2(w2_lo, 0)
+        load_w2(w2_lo, w2_s_lo, 0)
 
         v_w = [keep.tile([P, S], U32, name=f"v_w{a}", align_bytes=64) for a in range(KP)]
 
@@ -152,7 +152,7 @@ def tile_list_citation_chain_gate_kernel(tc, tab_words, tab_scales, offs, pos1, 
         z_slots = [keep.tile([P, PACK, M], BF16, name=f"z_slots{b}") for b in range(HP)]
 
         def gelu(j):
-            ge = keep.tile([P, M], F32, name=f"ge{j}", tag=f"ge{j % PACK}", align_bytes=64)
+            ge = keep.tile([P, M], F32, name=f"ge{j}", tag="ge7" if j == TILES - 1 else f"ge{j % PACK}", align_bytes=64)
             nc.scalar.activation(out=ge[:], in_=xs[j], func=ACT.Gelu_apprx_tanh)
             return ge
 
@@ -197,7 +197,7 @@ def tile_list_citation_chain_gate_kernel(tc, tab_words, tab_scales, offs, pos1, 
         )
         nc.vector.tensor_copy(
             out=w2_s_hi[:].rearrange("p a (t m) -> p a t m", t=PACK),
-            in_=w2_s[:, :, HALF:].rearrange("p a (m t) -> p a t m", t=PACK),
+            in_=w2_s_hi_raw[:].rearrange("p a (m t) -> p a t m", t=PACK),
         )
         gather_tab(2, 2)
 
@@ -213,14 +213,14 @@ def tile_list_citation_chain_gate_kernel(tc, tab_words, tab_scales, offs, pos1, 
         high0 = keep.tile([P, HALF * PACK], BF16, name="high0", tag="x0", align_bytes=64)
         round_high(0, 0, high0, nc.scalar.copy)
         start(2, x_low[2][:])
-        gather_citing([2], "citing2")
         start(3, x_low[3][:])
         round_high(0, 1, high0, nc.scalar.copy)
         quantise_w1(0, HALF, HALF, high0[:])
         high1 = keep.tile([P, HALF * PACK], BF16, name="high1", tag="x1", align_bytes=64)
-        round_high(1, 0, high1, nc.scalar.copy)
         z_low(2)
         z_low(3)
+        gather_citing([2], "ge3")
+        round_high(1, 0, high1, nc.scalar.copy)
         round_high(1, 1, high1, nc.vector.tensor_copy)
         quantise_w1(1, HALF, HALF, high1[:])
         high2 = keep.tile([P, HALF * PACK], BF16, name="high2", tag="x3", align_bytes=64)
@@ -247,7 +247,7 @@ def tile_list_citation_chain_gate_kernel(tc, tab_words, tab_scales, offs, pos1, 
         for b in range(HP):
             for j in order if b else range(TILES):
                 n = j % PACK
-                words, scales = (w2_lo, w2_s) if j < PACK else (w2_hi, w2_s_hi)
+                words, scales = (w2_lo, w2_s_lo) if j < PACK else (w2_hi, w2_s_hi)
                 nc.tensor.matmul_mx(
                     out=y[j][:],
                     lhsT=words[:, b, 2 * n * P : 2 * (n + 1) * P].bitcast(FP4X4),
@@ -265,7 +265,7 @@ def tile_list_citation_chain_gate_kernel(tc, tab_words, tab_scales, offs, pos1, 
                 gated = citing[j]
                 nc.vector.tensor_tensor(out=gated, in0=gate[:], in1=gated, op=MULT)
             else:
-                last = keep.tile([P, M], F32, name="last", tag="ge3", align_bytes=64)
+                last = keep.tile([P, M], F32, name="last", tag="ge7", align_bytes=64)
                 gated = last[:]
                 nc.vector.tensor_tensor(gated, h[j][:].indirect(pos2_sb[:]), gate[:], MULT)
             nc.sync.dma_start(out=out[j * P : (j + 1) * P, :] if j < PACK else out_hi[:, j - PACK, :], in_=gated)

@@ -1,7 +1,6 @@
 from contextlib import ExitStack
 
 import concourse.mybir as mybir
-from concourse.masks import make_identity
 
 K, H, T, S, M = 1536, 1024, 4096, 1024, 512
 FLOPS = 2 * K * H * S + 2 * H * H * M
@@ -16,6 +15,7 @@ FP8X4 = mybir.dt.float8_e4m3fn_x4
 FP4X4 = mybir.dt.float4_e2m1fn_x4
 ACT = mybir.ActivationFunctionType
 MULT = mybir.AluOpType.mult
+ADD = mybir.AluOpType.add
 
 P = 128
 PACK = 4
@@ -31,241 +31,298 @@ def tile_list_citation_chain_gate_kernel(tc, tab_words, tab_scales, offs, pos1, 
     nc = tc.nc
     with ExitStack() as ctx:
         keep = ctx.enter_context(tc.tile_pool(name="keep", bufs=1))
-        ring = ctx.enter_context(tc.tile_pool(name="ring", bufs=3))
         psum = ctx.enter_context(tc.psum_pool(name="psum", bufs=8))
 
-        offs_sb = keep.tile([P, S // 16], U16, name="offs_sb")
-        pos1_sb = keep.tile([P, M // 16], U16, name="pos1_sb")
-        pos2_sb = keep.tile([P, M // 16], U16, name="pos2_sb")
-        tab = [keep.tile([P, T], I32, name=f"tab{a}", align_bytes=64) for a in range(KP)]
-        tab_sc = keep.tile([P, T], U8, name="tab_sc")
-        w1_lo = {(c, a): keep.tile([P, PACK, CW], F32, name=f"w1_lo{c}_{a}") for c in range(2) for a in range(KP)}
-        w1_hi = [keep.tile([P, PACK, HALF], F32, name=f"w1_hi{a}") for a in range(KP)]
-        gain_lo = keep.tile([P, PACK], F32, name="gain_lo")
-        gain_hi = keep.tile([P, PACK], F32, name="gain_hi")
-        w2_lo = keep.tile([P, HP, 2 * HALF], U8, name="w2_lo", align_bytes=64)
-        w2_hi_raw = keep.tile([P, HP, 2 * HALF], U8, name="w2_hi_raw")
-        w2_hi = keep.tile([P, HP, 2 * HALF], U8, name="w2_hi", align_bytes=64)
-        w2_s_lo = keep.tile([P, HP, HALF], U8, name="w2_s_lo", align_bytes=64)
-        w2_s_hi_raw = keep.tile([P, HP, HALF], U8, name="w2_s_hi_raw")
-        w2_s_hi = keep.tile([P, HP, HALF], U8, name="w2_s_hi", align_bytes=64)
-        gain_rows = keep.tile([P, P], F32, name="gain_rows")
-        ident = keep.tile([P, P], F32, name="ident")
-        v_s = keep.tile([P, S], U8, name="v_s", align_bytes=64)
-        warm = keep.tile([P, 1], F32, name="warm")
+        def sbuf(name, shape, dtype, tag=None, bufs=1):
+            return keep.tile([P] + shape, dtype, name=name, tag=tag or name, bufs=bufs, align_bytes=64)
 
-        nc.vector.memset(tab_sc[:].bitcast(I32), 0)
-        nc.gpsimd.memset(gain_rows[:], 0.0)
-        nc.scalar.dma_start(out=gain_rows[0:PACK, :], in_=gain[0:HALF].rearrange("(j p) -> j p", p=P))
-        make_identity(nc, ident[:])
-        nc.scalar.activation(out=warm[:], in_=ident[:, 0:1], func=ACT.Gelu_apprx_tanh)
-        gain_ps = psum.tile([P, BANK], F32, name="gain_ps", tag="acc")
-        nc.tensor.transpose(gain_ps[:, 0:P], gain_rows[:], ident[:])
-        nc.scalar.copy(out=gain_lo[:], in_=gain_ps[:, 0:PACK])
-        for plane in (w2_s_hi_raw, w2_s_lo):
-            nc.vector.memset(plane[:].rearrange("p a n -> p (a n)").bitcast(I32), 0)
+        offs_sb = sbuf("offs_sb", [S // 16], U16)
+        pos1_sb = sbuf("pos1_sb", [M // 16], U16)
+        pos2_sb = sbuf("pos2_sb", [M // 16], U16)
+        tab_sc = sbuf("tab_sc", [T], U8)
+        gain_lo = sbuf("gain_lo", [PACK], F32)
+        gain_hi = sbuf("gain_hi", [PACK], F32)
+        w2_hi_raw = sbuf("w2_hi_raw", [HP, 2 * HALF], U8)
+        w2_hi = sbuf("w2_hi", [HP, 2 * HALF], U8)
+        w2_s = sbuf("w2_s", [HP, H], U8)
+        w2_s_hi = sbuf("w2_s_hi", [HP, HALF], U8)
+        v_s = sbuf("v_s", [S], U8)
+        tab, w1_lo, w1_hi, w2_lo = {}, {}, {}, {}
 
-        def load_tab(a):
+        def load_tab(a, tag=None):
+            tab[a] = sbuf(f"tab{a}", [T], I32, tag=tag)
             nc.sync.dma_start(out=tab[a][:], in_=tab_words[a].rearrange("p t i -> p (t i)").bitcast(I32))
 
         def load_w1(dst, a, n0, width):
             rows = w1[a * HALF : (a + 1) * HALF, n0 : n0 + width]
-            nc.sync.dma_start(out=dst[:], in_=rows.rearrange("(p j) n -> p j n", j=PACK))
+            nc.sync.dma_start(out=dst, in_=rows.rearrange("(p j) n -> p j n", j=PACK))
 
-        def load_w2(dst, plane, half):
+        def load_w1_low(c, a, tag=None):
+            w1_lo[c, a] = sbuf(f"w1_lo{c}{a}", [PACK, CW], F32, tag=tag)
+            load_w1(w1_lo[c, a][:], a, c * CW, CW)
+
+        def load_w1_high(tag=None):
+            rows = sbuf("w1_hi", [KP, PACK, HALF], F32, tag=tag)
+            for a in range(KP):
+                w1_hi[a] = rows[:, a]
+                load_w1(w1_hi[a], a, HALF, HALF)
+
+        def load_w2(dst, half):
             cols = w2_words[:, :, half * 2 * HALF : (half + 1) * 2 * HALF]
             nc.sync.dma_start(out=dst[:].bitcast(I32), in_=cols.rearrange("a p n -> p a n").bitcast(I32))
+
+        def load_w2_low(tag=None):
+            w2_lo[0] = sbuf("w2_lo", [HP, 2 * HALF], U8, tag=tag)
+            load_w2(w2_lo[0], 0)
+
+        def load_tab_scales(queue):
             for q in range(4):
-                rows = w2_scales[:, 4 * q : 4 * q + 4, half * HALF : (half + 1) * HALF]
-                nc.sync.dma_start(out=plane[32 * q : 32 * q + 4, :, :].bitcast(I32), in_=rows.rearrange("a r n -> r a n").bitcast(I32))
+                queue.dma_start(
+                    out=tab_sc[32 * q : 32 * q + 4 * KP, :].bitcast(I32),
+                    in_=tab_scales[:, 4 * q : 4 * q + 4, :].bitcast(I32),
+                )
 
-        nc.sync.dma_start(offs_sb[:], offs)
-        load_tab(0)
-        for a in range(KP):
-            load_w1(w1_lo[0, a], a, 0, CW)
-        for q in range(4):
-            nc.scalar.dma_start(
-                out=tab_sc[32 * q : 32 * q + 4 * KP, :].bitcast(I32),
-                in_=tab_scales[:, 4 * q : 4 * q + 4, :].bitcast(I32),
-            )
-        load_tab(1)
-        load_w2(w2_hi_raw, w2_s_hi_raw, 1)
-        load_tab(2)
-        nc.sync.dma_start(pos1_sb[:], pos1)
-        for a in range(KP):
-            load_w1(w1_lo[1, a], a, CW, CW)
-        nc.sync.dma_start(pos2_sb[:], pos2)
-        nc.sync.dma_start(out=gain_hi[:], in_=gain[HALF:].rearrange("(p t) -> p t", t=PACK))
-        for a in range(KP):
-            load_w1(w1_hi[a], a, HALF, HALF)
-        load_w2(w2_lo, w2_s_lo, 0)
+        def load_w2_scales(queue):
+            for q in range(4):
+                rows = w2_scales[:, 4 * q : 4 * q + 4, :]
+                queue.dma_start(out=w2_s[32 * q : 32 * q + 4, :, :].bitcast(I32), in_=rows.rearrange("a r n -> r a n").bitcast(I32))
 
-        v_w = [keep.tile([P, S], U32, name=f"v_w{a}", align_bytes=64) for a in range(KP)]
+        def load_low_gains(queue):
+            with nc.allow_non_contiguous_dma(reason="one gain a partition"):
+                queue.dma_start(out=gain_lo[:], in_=gain[0:HALF].rearrange("(j p) -> p j", p=P))
 
-        def gather_tab(a, pieces):
+        def load_high_gains(queue):
+            queue.dma_start(out=gain_hi[:], in_=gain[HALF:].rearrange("(p t) -> p t", t=PACK))
+
+        def warm_up():
+            warm = sbuf("warm", [1], F32)
+            nc.gpsimd.memset(warm[:], 0.0)
+            nc.scalar.activation(out=warm[:], in_=warm[:], func=ACT.Gelu_apprx_tanh)
+
+        v_w = {}
+
+        def gather_tab(a, pieces, tag=None):
+            v_w[a] = sbuf(f"v_w{a}", [S], U32, tag=tag)
             step = S // pieces
             for s0 in range(0, S, step):
                 nc.vector.tensor_copy(v_w[a][:, s0 : s0 + step], tab[a][:].bitcast(U32).indirect(offs_sb[:, s0 // 16 : (s0 + step) // 16]))
 
-        w1_c = [keep.tile([P, H], U32, name=f"w1_c{a}", align_bytes=64) for a in range(KP)]
-        w1_s = [keep.tile([P, H], U8, name=f"w1_s{a}", align_bytes=64) for a in range(KP)]
+        def gather_tab_scales():
+            nc.vector.tensor_copy(v_s[:], tab_sc[:].indirect(offs_sb[:]))
 
-        def quantise_w1(a, n0, width, grouped):
-            nc.vector.quantize_mx(out=w1_c[a][:, n0 : n0 + width].bitcast(FP8X4), scales=w1_s[a][:, n0 : n0 + width], in_=grouped)
+        def deal_w2_words():
+            nc.vector.tensor_copy(
+                out=w2_hi[:].bitcast(U16).rearrange("p a (t m) -> p a t m", t=PACK),
+                in_=w2_hi_raw[:].bitcast(U16).rearrange("p a (m t) -> p a t m", t=PACK),
+            )
 
-        def w1_low(c, a, grouped, copy):
+        def deal_w2_scales():
+            nc.gpsimd.tensor_copy(
+                out=w2_s_hi[:].rearrange("p a (t m) -> p a t m", t=PACK),
+                in_=w2_s[:, :, HALF:].rearrange("p a (m t) -> p a t m", t=PACK),
+            )
+
+        w1_c = [sbuf(f"w1_c{a}", [H], U32) for a in range(KP)]
+        w1_s = [sbuf(f"w1_s{a}", [H], U8) for a in range(KP)]
+
+        def pool_copy(out, in_):
+            nc.gpsimd.tensor_scalar(out=out, in0=in_, scalar1=1.0, scalar2=0.0, op0=MULT, op1=ADD)
+
+        def round_low(c, a, grouped, copy):
             copy(
                 out=grouped.rearrange("p (g i j) -> p g j i", i=4, j=PACK),
                 in_=w1_lo[c, a][:].rearrange("p j (g i) -> p g j i", i=4),
             )
-            quantise_w1(a, c * CW, CW, grouped)
 
-        def round_high(a, half, grouped, copy):
-            ms = slice(half * P // 2, (half + 1) * P // 2)
+        def round_high(a, grouped, copy, m0=0, m1=P):
             copy(
-                out=grouped[:].rearrange("p (t m j) -> p m j t", t=PACK, j=PACK)[:, ms],
-                in_=w1_hi[a][:].rearrange("p j (m t) -> p m j t", t=PACK)[:, ms],
+                out=grouped.rearrange("p (t m j) -> p m j t", t=PACK, j=PACK)[:, m0:m1],
+                in_=w1_hi[a].rearrange("p j (m t) -> p m j t", t=PACK)[:, m0:m1],
             )
 
-        h = [keep.tile([P, S], F32, name=f"h{j}") for j in range(TILES)]
-        xs = {}
-        x_low = [keep.tile([P, M], F32, name=f"x{j}", align_bytes=64) for j in range(PACK)]
+        def quantise_w1(a, n0, width, grouped):
+            nc.vector.quantize_mx(out=w1_c[a][:, n0 : n0 + width].bitcast(FP8X4), scales=w1_s[a][:, n0 : n0 + width], in_=grouped)
 
-        def start(j, x):
-            cols = slice(j * P, (j + 1) * P)
-            for s0 in range(0, S, BANK):
-                acc = psum.tile([P, BANK], F32, name="acc")
-                for a in range(KP):
+        h = [sbuf(f"h{j}", [S], F32) for j in range(TILES)]
+        acc = {}
+
+        def first_product(banks, passes):
+            for a in passes:
+                for j, s in banks:
+                    if a == 0:
+                        acc[j, s] = psum.tile([P, BANK], F32, name=f"acc{j}", tag="acc")
+                    cols = slice(j * P, (j + 1) * P)
                     nc.tensor.matmul_mx(
-                        out=acc[:],
+                        out=acc[j, s][:],
                         lhsT=w1_c[a][:, cols].bitcast(FP8X4),
                         lhsT_scale=w1_s[a][:, cols],
-                        rhs=v_w[a][:, s0 : s0 + BANK].bitcast(FP8X4),
-                        rhs_scale=v_s[4 * a :, s0 : s0 + BANK],
+                        rhs=v_w[a][:, s * BANK : (s + 1) * BANK].bitcast(FP8X4),
+                        rhs_scale=v_s[4 * a :, s * BANK : (s + 1) * BANK],
                         start=(a == 0),
                         stop=(a == KP - 1),
                     )
-                nc.scalar.copy(out=h[j][:, s0 : s0 + BANK], in_=acc[:])
-            xs[j] = x
-            nc.vector.tensor_copy(x, h[j][:].indirect(pos1_sb[:]))
 
-        z_slots = [keep.tile([P, PACK, M], BF16, name=f"z_slots{b}") for b in range(HP)]
+        def empty(j, s, copy=nc.scalar.copy):
+            copy(out=h[j][:, s * BANK : (s + 1) * BANK], in_=acc[j, s][:])
 
-        def gelu(j):
-            ge = keep.tile([P, M], F32, name=f"ge{j}", tag="ge7" if j == TILES - 1 else f"ge{j % PACK}", align_bytes=64)
-            nc.scalar.activation(out=ge[:], in_=xs[j], func=ACT.Gelu_apprx_tanh)
-            return ge
+        xs = {}
 
-        def z_low(j):
-            ge = gelu(j)
-            zb = ring.tile([P, M], BF16, name="zb", bufs=4)
-            nc.vector.tensor_scalar(out=zb[:], in0=ge[:], scalar1=gain_lo[:, j : j + 1], scalar2=None, op0=MULT)
-            for i in range(PACK):
-                nc.sync.dma_start(out=z_slots[0][32 * j : 32 * j + 32, i, :], in_=zb[i:P:PACK, :])
-
-        def z_high(t, ge):
-            nc.scalar.activation(out=z_slots[1][:, t, :], in_=ge[:], func=ACT.Copy, scale=gain_hi[:, t : t + 1])
-
-        z_c = [keep.tile([P, M], U32, name=f"z_c{b}", align_bytes=64) for b in range(HP)]
-        z_s = [keep.tile([P, M], U8, name=f"z_s{b}", align_bytes=64) for b in range(HP)]
-
-        def quantise_z(b):
-            z_grouped = keep.tile([P, M, PACK], BF16, name=f"z_grouped{b}", tag="z_grouped", align_bytes=64)
-            nc.vector.tensor_copy(
-                out=z_grouped[:].rearrange("p (g i) t -> p g t i", i=4),
-                in_=z_slots[b][:].rearrange("p t (g i) -> p g t i", i=4),
-            )
-            nc.vector.quantize_mx(out=z_c[b][:].bitcast(FP8X4), scales=z_s[b][:], in_=z_grouped[:].rearrange("p m t -> p (m t)"))
+        def gather_cited(j, tag=None):
+            xs[j] = sbuf(f"x{j}", [M], F32, tag=tag)
+            nc.vector.tensor_copy(xs[j][:], h[j][:].indirect(pos1_sb[:]))
 
         citing = {}
 
-        def gather_citing(tiles, tag):
-            picked = keep.tile([P, len(tiles), M], F32, name=f"citing{tiles[0]}", tag=tag, align_bytes=64)
-            for n, j in enumerate(tiles):
-                citing[j] = picked[:, n, :]
-                nc.vector.tensor_copy(citing[j], h[j][:].indirect(pos2_sb[:]))
+        def gather_citing(j, tag=None):
+            citing[j] = sbuf(f"citing{j}", [M], F32, tag=tag)
+            nc.vector.tensor_copy(citing[j][:], h[j][:].indirect(pos2_sb[:]))
 
-        gather_tab(0, 1)
-        for a in range(KP):
-            grouped0 = ring.tile([P, CW * PACK], BF16, name="grouped0", align_bytes=64)
-            w1_low(0, a, grouped0[:], nc.scalar.copy)
-        nc.vector.tensor_copy(v_s[:], tab_sc[:].indirect(offs_sb[:]))
-        gather_tab(1, 1)
-        nc.vector.tensor_copy(
-            out=w2_hi[:].bitcast(U16).rearrange("p a (t m) -> p a t m", t=PACK),
-            in_=w2_hi_raw[:].bitcast(U16).rearrange("p a (m t) -> p a t m", t=PACK),
-        )
-        nc.vector.tensor_copy(
-            out=w2_s_hi[:].rearrange("p a (t m) -> p a t m", t=PACK),
-            in_=w2_s_hi_raw[:].rearrange("p a (m t) -> p a t m", t=PACK),
-        )
-        gather_tab(2, 2)
+        z_slots = [sbuf(f"z_slots{b}", [PACK, M], BF16) for b in range(HP)]
+        ge = {}
 
-        grouped1 = keep.tile([P, KP, CW * PACK], BF16, name="grouped1", tag="tab2", align_bytes=64)
-        w1_low(1, 0, grouped1[:, 0, :], nc.vector.tensor_copy)
-        start(0, x_low[0][:])
-        start(1, x_low[1][:])
-        w1_low(1, 1, grouped1[:, 1, :], nc.scalar.copy)
-        w1_low(1, 2, grouped1[:, 2, :], nc.scalar.copy)
-        gather_citing([0, 1], "tab2")
-        z_low(0)
-        z_low(1)
-        high0 = keep.tile([P, HALF * PACK], BF16, name="high0", tag="x0", align_bytes=64)
-        round_high(0, 0, high0, nc.scalar.copy)
-        start(2, x_low[2][:])
-        start(3, x_low[3][:])
-        round_high(0, 1, high0, nc.scalar.copy)
-        quantise_w1(0, HALF, HALF, high0[:])
-        high1 = keep.tile([P, HALF * PACK], BF16, name="high1", tag="x1", align_bytes=64)
-        z_low(2)
-        z_low(3)
-        gather_citing([2], "ge3")
-        round_high(1, 0, high1, nc.scalar.copy)
-        round_high(1, 1, high1, nc.vector.tensor_copy)
-        quantise_w1(1, HALF, HALF, high1[:])
-        high2 = keep.tile([P, HALF * PACK], BF16, name="high2", tag="x3", align_bytes=64)
-        round_high(2, 0, high2, nc.scalar.copy)
-        round_high(2, 1, high2, nc.vector.tensor_copy)
-        for c in range(2):
-            quantise_w1(2, HALF + c * CW, CW, high2[:, c * CW * PACK : (c + 1) * CW * PACK])
-        gather_citing([3], "x3")
-        quantise_z(0)
-        x_high = keep.tile([P, PACK, M], F32, name="x_high", tag="z_grouped", align_bytes=64)
-        for t in range(PACK):
-            start(PACK + t, x_high[:, t, :])
-        ge_high = [gelu(PACK)]
-        for t in range(PACK):
-            if t + 1 < PACK:
-                ge_high.append(gelu(PACK + t + 1))
-            z_high(t, ge_high[t])
-        gather_citing([4, 5], "ge0")
-        quantise_z(1)
-        gather_citing([6], "z_grouped")
+        def gelu(j, tag="ge", bufs=4):
+            ge[j] = sbuf(f"ge{j}", [M], F32, tag=tag, bufs=bufs)
+            nc.scalar.activation(out=ge[j][:], in_=xs[j][:], func=ACT.Gelu_apprx_tanh)
 
-        y = [psum.tile([P, BANK], F32, name=f"y{j}", tag="acc") for j in range(TILES)]
-        order = [TILES - 1] + list(range(TILES - 1))
-        for b in range(HP):
-            for j in order if b else range(TILES):
+        def on_scalar(dst, src, factor):
+            nc.scalar.activation(out=dst, in_=src, func=ACT.Copy, scale=factor)
+
+        def on_vector(dst, src, factor):
+            nc.vector.tensor_scalar(out=dst, in0=src, scalar1=factor, scalar2=None, op0=MULT)
+
+        def on_pool(dst, src, factor):
+            nc.gpsimd.tensor_scalar(out=dst, in0=src, scalar1=factor, scalar2=0.0, op0=MULT, op1=ADD)
+
+        def apply_gain(j, scale):
+            if j >= PACK:
+                scale(z_slots[1][:, j - PACK, :], ge[j][:], gain_hi[:, j - PACK : j - PACK + 1])
+                return
+            zb = sbuf(f"zb{j}", [M], BF16)
+            scale(zb[:], ge[j][:], gain_lo[:, j : j + 1])
+            for i in range(PACK):
+                nc.sync.dma_start(out=z_slots[0][32 * j : 32 * j + 32, i, :], in_=zb[i:P:PACK, :])
+
+        z_c = [sbuf(f"z_c{b}", [M], U32) for b in range(HP)]
+        z_s = [sbuf(f"z_s{b}", [M], U8) for b in range(HP)]
+        z_grouped = {}
+
+        def weave_z(b, tag=None):
+            z_grouped[b] = sbuf(f"z_grouped{b}", [M, PACK], BF16, tag=tag)
+            nc.vector.tensor_copy(
+                out=z_grouped[b][:].rearrange("p (g i) t -> p g t i", i=4),
+                in_=z_slots[b][:].rearrange("p t (g i) -> p g t i", i=4),
+            )
+
+        def quantise_z(b):
+            nc.vector.quantize_mx(out=z_c[b][:].bitcast(FP8X4), scales=z_s[b][:], in_=z_grouped[b][:].rearrange("p m t -> p (m t)"))
+
+        y = {}
+
+        def second_product(b, tiles):
+            for j in tiles:
+                if b == 0:
+                    y[j] = psum.tile([P, BANK], F32, name=f"y{j}", tag="acc")
                 n = j % PACK
-                words, scales = (w2_lo, w2_s_lo) if j < PACK else (w2_hi, w2_s_hi)
                 nc.tensor.matmul_mx(
                     out=y[j][:],
-                    lhsT=words[:, b, 2 * n * P : 2 * (n + 1) * P].bitcast(FP4X4),
-                    lhsT_scale=scales[:, b, n * P : (n + 1) * P],
+                    lhsT=(w2_lo[0] if j < PACK else w2_hi)[:, b, 2 * n * P : 2 * (n + 1) * P].bitcast(FP4X4),
+                    lhsT_scale=(w2_s if j < PACK else w2_s_hi)[:, b, n * P : (n + 1) * P],
                     rhs=z_c[b][:].bitcast(FP8X4),
                     rhs_scale=z_s[b][:],
                     start=(b == 0),
                     stop=(b == HP - 1),
                 )
+
         out_hi = out[HALF:, :].rearrange("(p t) m -> p t m", t=PACK)
-        for j in order:
-            gate = ring.tile([P, M], F32, name="gate", bufs=4)
+
+        def finish(j):
+            gate = sbuf(f"gate{j}", [M], F32, tag="gate", bufs=4)
             nc.scalar.activation(out=gate[:], in_=y[j][:], func=ACT.Sigmoid)
             if j in citing:
                 gated = citing[j]
-                nc.vector.tensor_tensor(out=gated, in0=gate[:], in1=gated, op=MULT)
+                nc.vector.tensor_tensor(out=gated[:], in0=gate[:], in1=gated[:], op=MULT)
             else:
-                last = keep.tile([P, M], F32, name="last", tag="ge7", align_bytes=64)
-                gated = last[:]
-                nc.vector.tensor_tensor(gated, h[j][:].indirect(pos2_sb[:]), gate[:], MULT)
-            nc.sync.dma_start(out=out[j * P : (j + 1) * P, :] if j < PACK else out_hi[:, j - PACK, :], in_=gated)
+                gated = sbuf(f"gated{j}", [M], F32, tag="gated", bufs=4)
+                nc.vector.tensor_tensor(gated[:], h[j][:].indirect(pos2_sb[:]), gate[:], MULT)
+            nc.sync.dma_start(out=out[j * P : (j + 1) * P, :] if j < PACK else out_hi[:, j - PACK, :], in_=gated[:])
+
+        nc.vector.memset(tab_sc[:].bitcast(I32), 0)
+        nc.vector.memset(w2_s[:].rearrange("p a n -> p (a n)").bitcast(I32), 0)
+        nc.sync.dma_start(offs_sb[:], offs)
+        load_tab(0)
+        load_w2(w2_hi_raw, 1)
+        for a in range(KP):
+            load_w1_low(0, a, "tab2" if a == 0 else None)
+        nc.sync.dma_start(pos1_sb[:], pos1)
+        nc.sync.dma_start(pos2_sb[:], pos2)
+        load_tab_scales(nc.gpsimd)
+        load_w2_scales(nc.gpsimd)
+        warm_up()
+        load_low_gains(nc.gpsimd)
+        load_high_gains(nc.gpsimd)
+        gather_tab(0, 1)
+        load_tab(1, "tab0")
+        for a in range(KP):
+            grouped0 = sbuf(f"grouped0{a}", [CW * PACK], BF16)
+            round_low(0, a, grouped0[:], nc.scalar.copy)
+            quantise_w1(a, 0, CW, grouped0[:])
+        load_tab(2)
+        gather_tab_scales()
+        for a, tag in enumerate(["w1_lo01", "w1_lo02", "tab_sc"]):
+            load_w1_low(1, a, tag)
+        deal_w2_words()
+        gather_tab(1, 1)
+        load_w1_high("tab0")
+        deal_w2_scales()
+        gather_tab(2, 2)
+
+        first_product([(0, 0), (1, 0), (0, 1), (1, 1)], range(KP))
+        for j, s in [(0, 0), (1, 0), (0, 1), (1, 1)]:
+            empty(j, s)
+        grouped1 = sbuf("grouped1", [KP, CW * PACK], BF16, tag="tab2")
+        for a in range(KP):
+            round_low(1, a, grouped1[:, a, :], nc.scalar.copy if a >= 2 else nc.vector.tensor_copy)
+            quantise_w1(a, CW, CW, grouped1[:, a, :])
+        first_product([(2, 0), (2, 1), (3, 0), (3, 1)], range(KP))
+        for j, s in [(2, 0), (2, 1), (3, 0), (3, 1)]:
+            empty(j, s)
+        gather_cited(0)
+        gather_cited(1)
+        high = [sbuf(f"high{a}", [HALF * PACK], BF16, tag=[None, None, None][a]) for a in range(KP)]
+        for a, split in enumerate([128, 128, 64]):
+            if split:
+                round_high(a, high[a][:], nc.vector.tensor_copy, 0, split)
+            if split < P:
+                round_high(a, high[a][:], nc.scalar.copy, split, P)
+            if a < KP - 1:
+                quantise_w1(a, HALF, HALF, high[a][:])
+        for c in range(2):
+            quantise_w1(2, HALF + c * CW, CW, high[2][:, c * CW * PACK : (c + 1) * CW * PACK])
+        upper = [(j, s) for j in range(PACK, TILES) for s in range(2)]
+        first_product(upper, range(KP))
+        gather_cited(2, None)
+        gather_cited(3, None)
+        for j in range(PACK):
+            gelu(j)
+            apply_gain(j, on_scalar)
+            if j == 0:
+                load_w2_low("x0")
+        for j, s in upper:
+            empty(j, s)
+        for j in range(PACK, TILES):
+            gather_cited(j)
+        for j in range(PACK, TILES):
+            gelu(j)
+        weave_z(0, "x4")
+        quantise_z(0)
+        for j in range(PACK, TILES):
+            apply_gain(j, on_vector if j < 6 else on_scalar)
+        weave_z(1)
+        quantise_z(1)
+        for j in range(TILES):
+            second_product(0, [j])
+            second_product(1, [j])
+        for j, tag in [(7, "z_grouped1")]:
+            gather_citing(j, tag)
+        for j in range(TILES):
+            finish(j)

@@ -25,15 +25,21 @@ HP = H // HALF
 TILES = H // P
 BANK = 512
 CW = 256
+GATE_BYTES = M * 4
+HIGH_BYTES = PACK * HALF * 4
 
 
 def tile_list_citation_chain_gate_kernel(tc, tab_words, tab_scales, offs, pos1, pos2, w1, gain, w2_words, w2_scales, out):
     nc = tc.nc
     with ExitStack() as ctx:
         keep = ctx.enter_context(tc.tile_pool(name="keep", bufs=1))
+        placed = ctx.enter_context(tc.tile_pool(name="placed", bufs=1))
+        chain = ctx.enter_context(tc.tile_pool(name="chain", bufs=1))
         psum = ctx.enter_context(tc.psum_pool(name="psum", bufs=8))
 
         def sbuf(name, shape, dtype, tag=None, bufs=1):
+            if isinstance(tag, int):
+                return chain.tile([P] + shape, dtype, name=name, offset=tag, align_bytes=64)
             return keep.tile([P] + shape, dtype, name=name, tag=tag or name, bufs=bufs, align_bytes=64)
 
         offs_sb = sbuf("offs_sb", [S // 16], U16)
@@ -49,8 +55,8 @@ def tile_list_citation_chain_gate_kernel(tc, tab_words, tab_scales, offs, pos1, 
         v_s = sbuf("v_s", [S], U8)
         tab, w1_lo, w1_hi, w2_lo = {}, {}, {}, {}
 
-        def load_tab(a, tag=None):
-            tab[a] = sbuf(f"tab{a}", [T], I32, tag=tag)
+        def load_tab(a):
+            tab[a] = sbuf(f"tab{a}", [T], I32) if a == KP - 1 else placed.tile([P, T], I32, name=f"tab{a}", offset=HIGH_BYTES // 2, align_bytes=64)
             nc.sync.dma_start(out=tab[a][:], in_=tab_words[a].rearrange("p t i -> p (t i)").bitcast(I32))
 
         def load_w1(dst, a, n0, width):
@@ -61,11 +67,9 @@ def tile_list_citation_chain_gate_kernel(tc, tab_words, tab_scales, offs, pos1, 
             w1_lo[c, a] = sbuf(f"w1_lo{c}{a}", [PACK, CW], F32, tag=tag)
             load_w1(w1_lo[c, a][:], a, c * CW, CW)
 
-        def load_w1_high(tag=None):
-            rows = sbuf("w1_hi", [KP, PACK, HALF], F32, tag=tag)
-            for a in range(KP):
-                w1_hi[a] = rows[:, a]
-                load_w1(w1_hi[a], a, HALF, HALF)
+        def load_w1_high(a):
+            w1_hi[a] = placed.tile([P, PACK, HALF], F32, name=f"w1_hi{a}", offset=a * HIGH_BYTES, align_bytes=64)
+            load_w1(w1_hi[a][:], a, HALF, HALF)
 
         def load_w2(dst, half):
             cols = w2_words[:, :, half * 2 * HALF : (half + 1) * 2 * HALF]
@@ -137,7 +141,7 @@ def tile_list_citation_chain_gate_kernel(tc, tab_words, tab_scales, offs, pos1, 
         def round_high(a, grouped, copy, m0=0, m1=P):
             copy(
                 out=grouped.rearrange("p (t m j) -> p m j t", t=PACK, j=PACK)[:, m0:m1],
-                in_=w1_hi[a].rearrange("p j (m t) -> p m j t", t=PACK)[:, m0:m1],
+                in_=w1_hi[a][:].rearrange("p j (m t) -> p m j t", t=PACK)[:, m0:m1],
             )
 
         def quantise_w1(a, n0, width, grouped):
@@ -173,9 +177,11 @@ def tile_list_citation_chain_gate_kernel(tc, tab_words, tab_scales, offs, pos1, 
 
         citing = {}
 
-        def gather_citing(j, tag=None):
-            citing[j] = sbuf(f"citing{j}", [M], F32, tag=tag)
-            nc.vector.tensor_copy(citing[j][:], h[j][:].indirect(pos2_sb[:]))
+        def gather_citing(tiles, tag=None):
+            picked = sbuf(f"citing{tiles[0]}", [len(tiles), M], F32, tag=tag)
+            for n, j in enumerate(tiles):
+                citing[j] = picked[:, n, :]
+                nc.vector.tensor_copy(citing[j], h[j][:].indirect(pos2_sb[:]))
 
         z_slots = [sbuf(f"z_slots{b}", [PACK, M], BF16) for b in range(HP)]
         ge = {}
@@ -235,16 +241,24 @@ def tile_list_citation_chain_gate_kernel(tc, tab_words, tab_scales, offs, pos1, 
 
         out_hi = out[HALF:, :].rearrange("(p t) m -> p t m", t=PACK)
 
-        def finish(j):
-            gate = sbuf(f"gate{j}", [M], F32, tag="gate", bufs=4)
-            nc.scalar.activation(out=gate[:], in_=y[j][:], func=ACT.Sigmoid)
-            if j in citing:
-                gated = citing[j]
-                nc.vector.tensor_tensor(out=gated[:], in0=gate[:], in1=gated[:], op=MULT)
-            else:
-                gated = sbuf(f"gated{j}", [M], F32, tag="gated", bufs=4)
-                nc.vector.tensor_tensor(gated[:], h[j][:].indirect(pos2_sb[:]), gate[:], MULT)
-            nc.sync.dma_start(out=out[j * P : (j + 1) * P, :] if j < PACK else out_hi[:, j - PACK, :], in_=gated[:])
+        def store(j, gated):
+            nc.sync.dma_start(out=out[j * P : (j + 1) * P, :] if j < PACK else out_hi[:, j - PACK, :], in_=gated)
+
+        def finish(on_pool):
+            gates = {}
+            for j in range(TILES):
+                if j < on_pool:
+                    gates[j] = placed.tile([P, M], F32, name=f"gate{j}", offset=j * GATE_BYTES, align_bytes=64)
+                else:
+                    gates[j] = sbuf(f"gate{j}", [M], F32)
+                nc.scalar.activation(out=gates[j][:], in_=y[j][:], func=ACT.Sigmoid)
+            for j in range(on_pool):
+                nc.gpsimd.tensor_tensor(out=citing[j], in0=gates[j][:], in1=citing[j], op=MULT)
+                store(j, citing[j])
+            gated = placed.tile([P, TILES - on_pool, M], F32, name="gated", offset=max(on_pool - 1, 0) * GATE_BYTES, align_bytes=64)
+            for j in range(on_pool, TILES):
+                nc.vector.tensor_tensor(out=gated[:, j - on_pool, :], in0=gates[j][:], in1=citing[j], op=MULT)
+                store(j, gated[:, j - on_pool, :])
 
         nc.vector.memset(tab_sc[:].bitcast(I32), 0)
         nc.vector.memset(w2_s[:].rearrange("p a n -> p (a n)").bitcast(I32), 0)
@@ -261,18 +275,19 @@ def tile_list_citation_chain_gate_kernel(tc, tab_words, tab_scales, offs, pos1, 
         load_low_gains(nc.gpsimd)
         load_high_gains(nc.gpsimd)
         gather_tab(0, 1)
-        load_tab(1, "tab0")
+        load_tab(1)
         for a in range(KP):
             grouped0 = sbuf(f"grouped0{a}", [CW * PACK], BF16)
             round_low(0, a, grouped0[:], nc.scalar.copy)
             quantise_w1(a, 0, CW, grouped0[:])
         load_tab(2)
         gather_tab_scales()
-        for a, tag in enumerate(["w1_lo01", "w1_lo02", "tab_sc"]):
+        for a, tag in enumerate(["grouped00", "w1_lo01", "w1_lo02"]):
             load_w1_low(1, a, tag)
         deal_w2_words()
         gather_tab(1, 1)
-        load_w1_high("tab0")
+        for a in range(KP):
+            load_w1_high(a)
         deal_w2_scales()
         gather_tab(2, 2)
 
@@ -281,7 +296,7 @@ def tile_list_citation_chain_gate_kernel(tc, tab_words, tab_scales, offs, pos1, 
             empty(j, s)
         grouped1 = sbuf("grouped1", [KP, CW * PACK], BF16, tag="tab2")
         for a in range(KP):
-            round_low(1, a, grouped1[:, a, :], nc.scalar.copy if a >= 2 else nc.vector.tensor_copy)
+            round_low(1, a, grouped1[:, a, :], nc.scalar.copy if a >= 1 else nc.vector.tensor_copy)
             quantise_w1(a, CW, CW, grouped1[:, a, :])
         first_product([(2, 0), (2, 1), (3, 0), (3, 1)], range(KP))
         for j, s in [(2, 0), (2, 1), (3, 0), (3, 1)]:
@@ -289,7 +304,7 @@ def tile_list_citation_chain_gate_kernel(tc, tab_words, tab_scales, offs, pos1, 
         gather_cited(0)
         gather_cited(1)
         high = [sbuf(f"high{a}", [HALF * PACK], BF16, tag=[None, None, None][a]) for a in range(KP)]
-        for a, split in enumerate([128, 128, 64]):
+        for a, split in enumerate([128, 64, 64]):
             if split:
                 round_high(a, high[a][:], nc.vector.tensor_copy, 0, split)
             if split < P:
@@ -300,6 +315,8 @@ def tile_list_citation_chain_gate_kernel(tc, tab_words, tab_scales, offs, pos1, 
             quantise_w1(2, HALF + c * CW, CW, high[2][:, c * CW * PACK : (c + 1) * CW * PACK])
         upper = [(j, s) for j in range(PACK, TILES) for s in range(2)]
         first_product(upper, range(KP))
+        for j, tag in []:
+            gather_citing(j, tag)
         gather_cited(2, None)
         gather_cited(3, None)
         for j in range(PACK):
@@ -310,19 +327,20 @@ def tile_list_citation_chain_gate_kernel(tc, tab_words, tab_scales, offs, pos1, 
         for j, s in upper:
             empty(j, s)
         for j in range(PACK, TILES):
-            gather_cited(j)
+            gather_cited(j, 0 if j == PACK else None)
         for j in range(PACK, TILES):
             gelu(j)
-        weave_z(0, "x4")
+        weave_z(0, 0)
         quantise_z(0)
         for j in range(PACK, TILES):
-            apply_gain(j, on_vector if j < 6 else on_scalar)
-        weave_z(1)
+            apply_gain(j, on_scalar)
+        for j, tag in [([3], 0)]:
+            gather_citing(j, tag)
+        weave_z(1, 2048)
         quantise_z(1)
         for j in range(TILES):
             second_product(0, [j])
             second_product(1, [j])
-        for j, tag in [(7, "z_grouped1")]:
+        for j, tag in [([0], "high0"), ([1, 2], "high2"), ([4, 5, 6, 7], 2048)]:
             gather_citing(j, tag)
-        for j in range(TILES):
-            finish(j)
+        finish(3)

@@ -51,7 +51,7 @@ def tile_list_citation_chain_gate_kernel(tc, tab_words, tab_scales, offs, pos1, 
         w2_hi_raw = sbuf("w2_hi_raw", [HP, 2 * HALF], U8)
         w2_hi = sbuf("w2_hi", [HP, 2 * HALF], U8)
         w2_s = sbuf("w2_s", [HP, H], U8)
-        w2_s_hi = sbuf("w2_s_hi", [HP, HALF], U8)
+        w2_s_hi = {}
         v_s = sbuf("v_s", [S], U8)
         tab, w1_lo, w1_hi, w2_lo = {}, {}, {}, {}
 
@@ -82,7 +82,7 @@ def tile_list_citation_chain_gate_kernel(tc, tab_words, tab_scales, offs, pos1, 
         def load_tab_scales(queue):
             for q in range(4):
                 queue.dma_start(
-                    out=tab_sc[32 * q : 32 * q + 4 * KP, :].bitcast(I32),
+                    out=tab_sc[32 * q + 4 : 32 * q + 4 + 4 * KP, :].bitcast(I32),
                     in_=tab_scales[:, 4 * q : 4 * q + 4, :].bitcast(I32),
                 )
 
@@ -120,9 +120,10 @@ def tile_list_citation_chain_gate_kernel(tc, tab_words, tab_scales, offs, pos1, 
                 in_=w2_hi_raw[:].bitcast(U16).rearrange("p a (m t) -> p a t m", t=PACK),
             )
 
-        def deal_w2_scales():
+        def deal_w2_scales(tag=None):
+            w2_s_hi[0] = sbuf("w2_s_hi", [HP, HALF], U8, tag=tag)
             nc.gpsimd.tensor_copy(
-                out=w2_s_hi[:].rearrange("p a (t m) -> p a t m", t=PACK),
+                out=w2_s_hi[0][:].rearrange("p a (t m) -> p a t m", t=PACK),
                 in_=w2_s[:, :, HALF:].rearrange("p a (m t) -> p a t m", t=PACK),
             )
 
@@ -138,6 +139,9 @@ def tile_list_citation_chain_gate_kernel(tc, tab_words, tab_scales, offs, pos1, 
                 in_=w1_lo[c, a][:].rearrange("p j (g i) -> p g j i", i=4),
             )
 
+        def round_low_on_pool(c, a, grouped):
+            nc.gpsimd.tensor_copy(out=grouped.rearrange("p (n j) -> p n j", j=PACK), in_=w1_lo[c, a][:].rearrange("p j n -> p n j"))
+
         def round_high(a, grouped, copy, m0=0, m1=P):
             copy(
                 out=grouped.rearrange("p (t m j) -> p m j t", t=PACK, j=PACK)[:, m0:m1],
@@ -149,19 +153,22 @@ def tile_list_citation_chain_gate_kernel(tc, tab_words, tab_scales, offs, pos1, 
 
         h = [sbuf(f"h{j}", [S], F32) for j in range(TILES)]
         acc = {}
+        paired = {}
 
         def first_product(banks, passes):
             for a in passes:
                 for j, s in banks:
                     if a == 0:
                         acc[j, s] = psum.tile([P, BANK], F32, name=f"acc{j}", tag="acc")
-                    cols = slice(j * P, (j + 1) * P)
+                    codes, scales, cols = w1_c[a], w1_s[a], slice(j * P, (j + 1) * P)
+                    if (j, a) in paired:
+                        codes, scales, cols = paired[j, a]
                     nc.tensor.matmul_mx(
                         out=acc[j, s][:],
-                        lhsT=w1_c[a][:, cols].bitcast(FP8X4),
-                        lhsT_scale=w1_s[a][:, cols],
+                        lhsT=codes[:, cols].bitcast(FP8X4),
+                        lhsT_scale=scales[:, cols],
                         rhs=v_w[a][:, s * BANK : (s + 1) * BANK].bitcast(FP8X4),
-                        rhs_scale=v_s[4 * a :, s * BANK : (s + 1) * BANK],
+                        rhs_scale=v_s[4 + 4 * a :, s * BANK : (s + 1) * BANK],
                         start=(a == 0),
                         stop=(a == KP - 1),
                     )
@@ -183,7 +190,7 @@ def tile_list_citation_chain_gate_kernel(tc, tab_words, tab_scales, offs, pos1, 
                 citing[j] = picked[:, n, :]
                 nc.vector.tensor_copy(citing[j], h[j][:].indirect(pos2_sb[:]))
 
-        z_slots = [sbuf(f"z_slots{b}", [PACK, M], BF16) for b in range(HP)]
+        z_slots = {0: sbuf("z_slots0", [PACK, M], BF16)}
         ge = {}
 
         def gelu(j, tag="ge", bufs=4):
@@ -199,11 +206,11 @@ def tile_list_citation_chain_gate_kernel(tc, tab_words, tab_scales, offs, pos1, 
         def on_pool(dst, src, factor):
             nc.gpsimd.tensor_scalar(out=dst, in0=src, scalar1=factor, scalar2=0.0, op0=MULT, op1=ADD)
 
-        def apply_gain(j, scale):
+        def apply_gain(j, scale, tag=None):
             if j >= PACK:
                 scale(z_slots[1][:, j - PACK, :], ge[j][:], gain_hi[:, j - PACK : j - PACK + 1])
                 return
-            zb = sbuf(f"zb{j}", [M], BF16)
+            zb = sbuf(f"zb{j}", [M], BF16, tag=tag)
             scale(zb[:], ge[j][:], gain_lo[:, j : j + 1])
             for i in range(PACK):
                 nc.sync.dma_start(out=z_slots[0][32 * j : 32 * j + 32, i, :], in_=zb[i:P:PACK, :])
@@ -219,6 +226,10 @@ def tile_list_citation_chain_gate_kernel(tc, tab_words, tab_scales, offs, pos1, 
                 in_=z_slots[b][:].rearrange("p t (g i) -> p g t i", i=4),
             )
 
+        def weave_z_on_pool(b, tag=None):
+            z_grouped[b] = sbuf(f"z_grouped{b}", [M, PACK], BF16, tag=tag)
+            nc.gpsimd.tensor_copy(out=z_grouped[b][:], in_=z_slots[b][:].rearrange("p t m -> p m t"))
+
         def quantise_z(b):
             nc.vector.quantize_mx(out=z_c[b][:].bitcast(FP8X4), scales=z_s[b][:], in_=z_grouped[b][:].rearrange("p m t -> p (m t)"))
 
@@ -232,7 +243,7 @@ def tile_list_citation_chain_gate_kernel(tc, tab_words, tab_scales, offs, pos1, 
                 nc.tensor.matmul_mx(
                     out=y[j][:],
                     lhsT=(w2_lo[0] if j < PACK else w2_hi)[:, b, 2 * n * P : 2 * (n + 1) * P].bitcast(FP4X4),
-                    lhsT_scale=(w2_s if j < PACK else w2_s_hi)[:, b, n * P : (n + 1) * P],
+                    lhsT_scale=(w2_s if j < PACK else w2_s_hi[0])[:, b, n * P : (n + 1) * P],
                     rhs=z_c[b][:].bitcast(FP8X4),
                     rhs_scale=z_s[b][:],
                     start=(b == 0),
@@ -288,22 +299,36 @@ def tile_list_citation_chain_gate_kernel(tc, tab_words, tab_scales, offs, pos1, 
         gather_tab(1, 1)
         for a in range(KP):
             load_w1_high(a)
-        deal_w2_scales()
         gather_tab(2, 2)
 
         first_product([(0, 0), (1, 0), (0, 1), (1, 1)], range(KP))
         for j, s in [(0, 0), (1, 0), (0, 1), (1, 1)]:
             empty(j, s)
-        grouped1 = sbuf("grouped1", [KP, CW * PACK], BF16, tag="tab2")
-        for a in range(KP):
-            round_low(1, a, grouped1[:, a, :], nc.scalar.copy if a >= 1 else nc.vector.tensor_copy)
-            quantise_w1(a, CW, CW, grouped1[:, a, :])
-        first_product([(2, 0), (2, 1), (3, 0), (3, 1)], range(KP))
-        for j, s in [(2, 0), (2, 1), (3, 0), (3, 1)]:
-            empty(j, s)
+        grouped1 = sbuf("grouped1", [CW * PACK], BF16, tag="tab2")
+        round_low(1, 0, grouped1[:], nc.vector.tensor_copy)
+        quantise_w1(0, CW, CW, grouped1[:])
+        pair = sbuf("pair", [2, CW * PACK], BF16, tag="tab2")
+        pair_c = sbuf("pair_c", [2 * CW], U32, tag=20480)
+        pair_s = sbuf("pair_s", [2 * CW], U8)
+        round_low_on_pool(1, 1, pair[:, 0, :])
+        round_low_on_pool(1, 2, pair[:, 1, :])
         gather_cited(0)
         gather_cited(1)
-        high = [sbuf(f"high{a}", [HALF * PACK], BF16, tag=[None, None, None][a]) for a in range(KP)]
+        nc.vector.quantize_mx(out=pair_c[:].bitcast(FP8X4), scales=pair_s[:], in_=pair[:].rearrange("p a n -> p (a n)"))
+        for j in (2, 3):
+            for a in (1, 2):
+                n0 = (a - 1) * CW + (j - 2) * P
+                paired[j, a] = (pair_c, pair_s, slice(n0, n0 + P))
+        first_product([(2, 0), (2, 1), (3, 0), (3, 1)], [0])
+        for bank in [(2, 0), (2, 1), (3, 0), (3, 1)]:
+            first_product([bank], [1, 2])
+        for j, s in [(2, 0), (2, 1), (3, 0), (3, 1)]:
+            empty(j, s)
+        for j in range(2):
+            gelu(j)
+            apply_gain(j, on_scalar)
+        load_w2_low("x0")
+        high = [sbuf(f"high{a}", [HALF * PACK], BF16, tag=["tab2", None, 20480][a]) for a in range(KP)]
         for a, split in enumerate([128, 64, 64]):
             if split:
                 round_high(a, high[a][:], nc.vector.tensor_copy, 0, split)
@@ -314,33 +339,35 @@ def tile_list_citation_chain_gate_kernel(tc, tab_words, tab_scales, offs, pos1, 
         for c in range(2):
             quantise_w1(2, HALF + c * CW, CW, high[2][:, c * CW * PACK : (c + 1) * CW * PACK])
         upper = [(j, s) for j in range(PACK, TILES) for s in range(2)]
-        first_product(upper, range(KP))
-        for j, tag in []:
-            gather_citing(j, tag)
-        gather_cited(2, None)
-        gather_cited(3, None)
-        for j in range(PACK):
+        first_product(upper, [0])
+        for bank in upper:
+            first_product([bank], [1, 2])
+        gather_cited(2)
+        gather_cited(3)
+        for j in range(2, PACK):
             gelu(j)
-            apply_gain(j, on_scalar)
-            if j == 0:
-                load_w2_low("x0")
+            if j < 2:
+                apply_gain(j, on_scalar)
+            else:
+                apply_gain(j, on_pool, 20480 + 1024 * j)
+        deal_w2_scales(21504)
         for j, s in upper:
             empty(j, s)
         for j in range(PACK, TILES):
-            gather_cited(j, 0 if j == PACK else None)
+            gather_cited(j)
         for j in range(PACK, TILES):
             gelu(j)
-        weave_z(0, 0)
+        gather_citing([0, 1], 17408)
+        weave_z_on_pool(0, 0)
         quantise_z(0)
+        gather_citing([2], 0)
+        z_slots[1] = sbuf("z_slots1", [PACK, M], BF16, tag=2048)
         for j in range(PACK, TILES):
-            apply_gain(j, on_scalar)
-        for j, tag in [([3], 0)]:
-            gather_citing(j, tag)
-        weave_z(1, 2048)
+            apply_gain(j, on_pool if j < 6 else on_scalar)
+        weave_z(1, 6144)
         quantise_z(1)
         for j in range(TILES):
             second_product(0, [j])
             second_product(1, [j])
-        for j, tag in [([0], "high0"), ([1, 2], "high2"), ([4, 5, 6, 7], 2048)]:
-            gather_citing(j, tag)
+        gather_citing([3, 4, 5, 6, 7], 6144)
         finish(3)

@@ -304,31 +304,26 @@ def tile_list_citation_chain_gate_kernel(tc, tab_words, tab_scales, offs, pos1, 
         first_product([(0, 0), (1, 0), (0, 1), (1, 1)], range(KP))
         for j, s in [(0, 0), (1, 0), (0, 1), (1, 1)]:
             empty(j, s)
-        grouped1 = sbuf("grouped1", [CW * PACK], BF16, tag="tab2")
-        round_low(1, 0, grouped1[:], nc.vector.tensor_copy)
-        quantise_w1(0, CW, CW, grouped1[:])
-        pair = sbuf("pair", [2, CW * PACK], BF16, tag="tab2")
-        pair_c = sbuf("pair_c", [2 * CW], U32, tag=20480)
-        pair_s = sbuf("pair_s", [2 * CW], U8)
-        round_low_on_pool(1, 1, pair[:, 0, :])
-        round_low_on_pool(1, 2, pair[:, 1, :])
+        grouped1 = [sbuf(f"grouped1{a}", [CW * PACK], BF16, tag=["grouped1", "grouped1", "tab2"][a]) for a in range(KP)]
+        round_low(1, 0, grouped1[0][:], nc.vector.tensor_copy)
+        quantise_w1(0, CW, CW, grouped1[0][:])
+        round_low_on_pool(1, 1, grouped1[1][:])
+        round_low(1, 2, grouped1[2][:], nc.scalar.copy)
         gather_cited(0)
         gather_cited(1)
-        nc.vector.quantize_mx(out=pair_c[:].bitcast(FP8X4), scales=pair_s[:], in_=pair[:].rearrange("p a n -> p (a n)"))
-        for j in (2, 3):
-            for a in (1, 2):
-                n0 = (a - 1) * CW + (j - 2) * P
-                paired[j, a] = (pair_c, pair_s, slice(n0, n0 + P))
-        first_product([(2, 0), (2, 1), (3, 0), (3, 1)], [0])
-        for bank in [(2, 0), (2, 1), (3, 0), (3, 1)]:
+        for a in (1, 2):
+            quantise_w1(a, CW, CW, grouped1[a][:])
+        second = [(2, 0), (2, 1), (3, 0), (3, 1)]
+        first_product(second, [0])
+        for bank in second:
             first_product([bank], [1, 2])
-        for j, s in [(2, 0), (2, 1), (3, 0), (3, 1)]:
+        for j, s in second:
             empty(j, s)
         for j in range(2):
             gelu(j)
-            apply_gain(j, on_scalar)
+        apply_gain(0, on_scalar)
         load_w2_low("x0")
-        high = [sbuf(f"high{a}", [HALF * PACK], BF16, tag=["tab2", None, 20480][a]) for a in range(KP)]
+        high = [sbuf(f"high{a}", [HALF * PACK], BF16, tag=[None, None, 20480][a]) for a in range(KP)]
         for a, split in enumerate([128, 64, 64]):
             if split:
                 round_high(a, high[a][:], nc.vector.tensor_copy, 0, split)
@@ -342,15 +337,14 @@ def tile_list_citation_chain_gate_kernel(tc, tab_words, tab_scales, offs, pos1, 
         first_product(upper, [0])
         for bank in upper:
             first_product([bank], [1, 2])
+        apply_gain(1, on_pool, "high0")
         gather_cited(2)
         gather_cited(3)
         for j in range(2, PACK):
             gelu(j)
-            if j < 2:
-                apply_gain(j, on_scalar)
-            else:
-                apply_gain(j, on_pool, 20480 + 1024 * j)
+            apply_gain(j, on_scalar)
         deal_w2_scales(21504)
+        pass
         for j, s in upper:
             empty(j, s)
         for j in range(PACK, TILES):
@@ -360,14 +354,14 @@ def tile_list_citation_chain_gate_kernel(tc, tab_words, tab_scales, offs, pos1, 
         gather_citing([0, 1], 17408)
         weave_z_on_pool(0, 0)
         quantise_z(0)
-        gather_citing([2], 0)
-        z_slots[1] = sbuf("z_slots1", [PACK, M], BF16, tag=2048)
+        gather_citing([2], "z_slots0")
+        z_slots[1] = sbuf("z_slots1", [PACK, M], BF16)
         for j in range(PACK, TILES):
-            apply_gain(j, on_pool if j < 6 else on_scalar)
-        weave_z(1, 6144)
+            apply_gain(j, on_vector if j < 6 else on_scalar)
+        weave_z(1, 2048)
         quantise_z(1)
         for j in range(TILES):
             second_product(0, [j])
             second_product(1, [j])
-        gather_citing([3, 4, 5, 6, 7], 6144)
+        gather_citing([3, 4, 5, 6, 7], "z_slots1")
         finish(3)

@@ -25,6 +25,7 @@ HP = H // HALF
 TILES = H // P
 BANK = 512
 CW = 256
+LAST_SPLIT = 256
 GATE_BYTES = M * 4
 HIGH_BYTES = PACK * HALF * 4
 
@@ -48,8 +49,7 @@ def tile_list_citation_chain_gate_kernel(tc, tab_words, tab_scales, offs, pos1, 
         tab_sc = sbuf("tab_sc", [T], U8)
         gain_lo = sbuf("gain_lo", [PACK], F32)
         gain_hi = sbuf("gain_hi", [PACK], F32)
-        w2_hi_raw = sbuf("w2_hi_raw", [HP, 2 * HALF], U8)
-        w2_hi = sbuf("w2_hi", [HP, 2 * HALF], U8)
+        w2_hi = {}
         w2_s = sbuf("w2_s", [HP, H], U8)
         w2_s_hi = {}
         v_s = sbuf("v_s", [S], U8)
@@ -71,13 +71,9 @@ def tile_list_citation_chain_gate_kernel(tc, tab_words, tab_scales, offs, pos1, 
             w1_hi[a] = placed.tile([P, PACK, HALF], F32, name=f"w1_hi{a}", offset=a * HIGH_BYTES, align_bytes=64)
             load_w1(w1_hi[a][:], a, HALF, HALF)
 
-        def load_w2(dst, half):
-            cols = w2_words[:, :, half * 2 * HALF : (half + 1) * 2 * HALF]
-            nc.sync.dma_start(out=dst[:].bitcast(I32), in_=cols.rearrange("a p n -> p a n").bitcast(I32))
-
-        def load_w2_low(tag=None):
-            w2_lo[0] = sbuf("w2_lo", [HP, 2 * HALF], U8, tag=tag)
-            load_w2(w2_lo[0], 0)
+        def load_w2(tag=None):
+            w2_lo[0] = sbuf("w2_words", [HP, 2 * H], U8, tag=tag)
+            nc.sync.dma_start(out=w2_lo[0][:].bitcast(I32), in_=w2_words.rearrange("a p n -> p a n").bitcast(I32))
 
         def load_tab_scales(queue):
             for q in range(4):
@@ -114,11 +110,13 @@ def tile_list_citation_chain_gate_kernel(tc, tab_words, tab_scales, offs, pos1, 
         def gather_tab_scales():
             nc.vector.tensor_copy(v_s[:], tab_sc[:].indirect(offs_sb[:]))
 
-        def deal_w2_words():
-            nc.vector.tensor_copy(
-                out=w2_hi[:].bitcast(U16).rearrange("p a (t m) -> p a t m", t=PACK),
-                in_=w2_hi_raw[:].bitcast(U16).rearrange("p a (m t) -> p a t m", t=PACK),
-            )
+        def deal_w2_words_on_pool(tag):
+            w2_hi[0] = sbuf("w2_hi", [HP, 2 * HALF], U8, tag=tag)
+            for b in range(HP):
+                nc.gpsimd.tensor_copy(
+                    out=w2_hi[0][:, b, :].rearrange("p (t m e) -> p t m e", t=PACK, e=2),
+                    in_=w2_lo[0][:, b, 2 * HALF :].rearrange("p (m t e) -> p t m e", t=PACK, e=2),
+                )
 
         def deal_w2_scales(tag=None):
             w2_s_hi[0] = sbuf("w2_s_hi", [HP, HALF], U8, tag=tag)
@@ -226,6 +224,14 @@ def tile_list_citation_chain_gate_kernel(tc, tab_words, tab_scales, offs, pos1, 
                 in_=z_slots[b][:].rearrange("p t (g i) -> p g t i", i=4),
             )
 
+        def weave_z_shared(b, split, tag=None):
+            z_grouped[b] = sbuf(f"z_grouped{b}", [M, PACK], BF16, tag=tag)
+            for copy, ms in ((nc.vector.tensor_copy, slice(0, split)), (nc.scalar.copy, slice(split, M))):
+                copy(
+                    out=z_grouped[b][:, ms, :].rearrange("p (g i) t -> p g t i", i=4),
+                    in_=z_slots[b][:, :, ms].rearrange("p t (g i) -> p g t i", i=4),
+                )
+
         def weave_z_on_pool(b, tag=None):
             z_grouped[b] = sbuf(f"z_grouped{b}", [M, PACK], BF16, tag=tag)
             nc.gpsimd.tensor_copy(out=z_grouped[b][:], in_=z_slots[b][:].rearrange("p t m -> p m t"))
@@ -242,7 +248,7 @@ def tile_list_citation_chain_gate_kernel(tc, tab_words, tab_scales, offs, pos1, 
                 n = j % PACK
                 nc.tensor.matmul_mx(
                     out=y[j][:],
-                    lhsT=(w2_lo[0] if j < PACK else w2_hi)[:, b, 2 * n * P : 2 * (n + 1) * P].bitcast(FP4X4),
+                    lhsT=(w2_lo[0] if j < PACK else w2_hi[0])[:, b, 2 * n * P : 2 * (n + 1) * P].bitcast(FP4X4),
                     lhsT_scale=(w2_s if j < PACK else w2_s_hi[0])[:, b, n * P : (n + 1) * P],
                     rhs=z_c[b][:].bitcast(FP8X4),
                     rhs_scale=z_s[b][:],
@@ -252,8 +258,8 @@ def tile_list_citation_chain_gate_kernel(tc, tab_words, tab_scales, offs, pos1, 
 
         out_hi = out[HALF:, :].rearrange("(p t) m -> p t m", t=PACK)
 
-        def store(j, gated):
-            nc.sync.dma_start(out=out[j * P : (j + 1) * P, :] if j < PACK else out_hi[:, j - PACK, :], in_=gated)
+        def store(j, gated, ms=slice(0, M)):
+            nc.sync.dma_start(out=out[j * P : (j + 1) * P, ms] if j < PACK else out_hi[:, j - PACK, ms], in_=gated)
 
         def finish(on_pool):
             gates = {}
@@ -268,14 +274,14 @@ def tile_list_citation_chain_gate_kernel(tc, tab_words, tab_scales, offs, pos1, 
                 store(j, citing[j])
             gated = placed.tile([P, TILES - on_pool, M], F32, name="gated", offset=max(on_pool - 1, 0) * GATE_BYTES, align_bytes=64)
             for j in range(on_pool, TILES):
-                nc.vector.tensor_tensor(out=gated[:, j - on_pool, :], in0=gates[j][:], in1=citing[j], op=MULT)
-                store(j, gated[:, j - on_pool, :])
+                for ms in [slice(0, M)] if j < TILES - 1 else [slice(0, LAST_SPLIT), slice(LAST_SPLIT, M)]:
+                    nc.vector.tensor_tensor(out=gated[:, j - on_pool, ms], in0=gates[j][:, ms], in1=citing[j][:, ms], op=MULT)
+                    store(j, gated[:, j - on_pool, ms], ms)
 
         nc.vector.memset(tab_sc[:].bitcast(I32), 0)
         nc.vector.memset(w2_s[:].rearrange("p a n -> p (a n)").bitcast(I32), 0)
-        nc.sync.dma_start(offs_sb[:], offs)
         load_tab(0)
-        load_w2(w2_hi_raw, 1)
+        nc.sync.dma_start(offs_sb[:], offs)
         for a in range(KP):
             load_w1_low(0, a, "tab2" if a == 0 else None)
         nc.sync.dma_start(pos1_sb[:], pos1)
@@ -295,7 +301,6 @@ def tile_list_citation_chain_gate_kernel(tc, tab_words, tab_scales, offs, pos1, 
         gather_tab_scales()
         for a, tag in enumerate(["grouped00", "w1_lo01", "w1_lo02"]):
             load_w1_low(1, a, tag)
-        deal_w2_words()
         gather_tab(1, 1)
         for a in range(KP):
             load_w1_high(a)
@@ -304,27 +309,25 @@ def tile_list_citation_chain_gate_kernel(tc, tab_words, tab_scales, offs, pos1, 
         first_product([(0, 0), (1, 0), (0, 1), (1, 1)], range(KP))
         for j, s in [(0, 0), (1, 0), (0, 1), (1, 1)]:
             empty(j, s)
-        grouped1 = [sbuf(f"grouped1{a}", [CW * PACK], BF16, tag=["grouped1", "grouped1", "tab2"][a]) for a in range(KP)]
-        round_low(1, 0, grouped1[0][:], nc.vector.tensor_copy)
-        quantise_w1(0, CW, CW, grouped1[0][:])
-        round_low_on_pool(1, 1, grouped1[1][:])
-        round_low(1, 2, grouped1[2][:], nc.scalar.copy)
+        grouped1 = [sbuf(f"grouped1{a}", [CW * PACK], BF16, tag=28672 if a else None) for a in range(KP)]
+        round_low_on_pool(1, 0, grouped1[0][:])
+        round_low(1, 1, grouped1[1][:], nc.vector.tensor_copy)
+        for a in range(2):
+            quantise_w1(a, CW, CW, grouped1[a][:])
+        round_low_on_pool(1, 2, grouped1[2][:])
         gather_cited(0)
         gather_cited(1)
-        for a in (1, 2):
-            quantise_w1(a, CW, CW, grouped1[a][:])
+        quantise_w1(2, CW, CW, grouped1[2][:])
         second = [(2, 0), (2, 1), (3, 0), (3, 1)]
-        first_product(second, [0])
-        for bank in second:
-            first_product([bank], [1, 2])
+        first_product(second, range(KP))
         for j, s in second:
             empty(j, s)
         for j in range(2):
             gelu(j)
         apply_gain(0, on_scalar)
-        load_w2_low("x0")
-        high = [sbuf(f"high{a}", [HALF * PACK], BF16, tag=[None, None, 20480][a]) for a in range(KP)]
-        for a, split in enumerate([128, 64, 64]):
+        load_w2("x0")
+        high = [sbuf(f"high{a}", [HALF * PACK], BF16, tag=[28672, None, 20480][a]) for a in range(KP)]
+        for a, split in enumerate([128, 0, 96]):
             if split:
                 round_high(a, high[a][:], nc.vector.tensor_copy, 0, split)
             if split < P:
@@ -337,14 +340,14 @@ def tile_list_citation_chain_gate_kernel(tc, tab_words, tab_scales, offs, pos1, 
         first_product(upper, [0])
         for bank in upper:
             first_product([bank], [1, 2])
-        apply_gain(1, on_pool, "high0")
+        apply_gain(1, on_pool, 28672)
+        deal_w2_scales(29696)
         gather_cited(2)
         gather_cited(3)
         for j in range(2, PACK):
             gelu(j)
             apply_gain(j, on_scalar)
-        deal_w2_scales(21504)
-        pass
+        deal_w2_words_on_pool(22528)
         for j, s in upper:
             empty(j, s)
         for j in range(PACK, TILES):
@@ -358,7 +361,7 @@ def tile_list_citation_chain_gate_kernel(tc, tab_words, tab_scales, offs, pos1, 
         z_slots[1] = sbuf("z_slots1", [PACK, M], BF16)
         for j in range(PACK, TILES):
             apply_gain(j, on_vector if j < 6 else on_scalar)
-        weave_z(1, 2048)
+        weave_z_shared(1, 336, 2048)
         quantise_z(1)
         for j in range(TILES):
             second_product(0, [j])

@@ -24,10 +24,9 @@ KP = K // HALF
 HP = H // HALF
 TILES = H // P
 BANK = 512
-CW = 256
-LAST_SPLIT = 256
+RAW_BYTES = PACK * HALF * 4
 GATE_BYTES = M * 4
-HIGH_BYTES = PACK * HALF * 4
+LAST_SPLIT = 256
 
 
 def tile_list_citation_chain_gate_kernel(tc, tab_words, tab_scales, offs, pos1, pos2, w1, gain, w2_words, w2_scales, out):
@@ -47,33 +46,27 @@ def tile_list_citation_chain_gate_kernel(tc, tab_words, tab_scales, offs, pos1, 
         pos1_sb = sbuf("pos1_sb", [M // 16], U16)
         pos2_sb = sbuf("pos2_sb", [M // 16], U16)
         tab_sc = sbuf("tab_sc", [T], U8)
-        gain_lo = sbuf("gain_lo", [PACK], F32)
-        gain_hi = sbuf("gain_hi", [PACK], F32)
-        w2_hi = {}
-        w2_s = sbuf("w2_s", [HP, H], U8)
-        w2_s_hi = {}
+        gains = sbuf("gains", [HP, PACK], F32)
+        w2_s_raw = sbuf("w2_s_raw", [HP, H], U8)
         v_s = sbuf("v_s", [S], U8)
-        tab, w1_lo, w1_hi, w2_lo = {}, {}, {}, {}
+        tab, w1_raw, w2_raw, w2_w, w2_s = {}, {}, {}, {}, {}
 
-        def load_tab(a):
-            tab[a] = sbuf(f"tab{a}", [T], I32) if a == KP - 1 else placed.tile([P, T], I32, name=f"tab{a}", offset=HIGH_BYTES // 2, align_bytes=64)
+        def load_tab(a, tag=None):
+            tab[a] = sbuf(f"tab{a}", [T], I32, tag=tag) if a == KP - 1 else placed.tile([P, T], I32, name=f"tab{a}", offset=RAW_BYTES // 2, align_bytes=64)
             nc.sync.dma_start(out=tab[a][:], in_=tab_words[a].rearrange("p t i -> p (t i)").bitcast(I32))
 
-        def load_w1(dst, a, n0, width):
-            rows = w1[a * HALF : (a + 1) * HALF, n0 : n0 + width]
-            nc.sync.dma_start(out=dst, in_=rows.rearrange("(p j) n -> p j n", j=PACK))
+        def load_w1(b, a, tag=None):
+            if b == 0:
+                w1_raw[b, a] = sbuf(f"w1_raw{b}{a}", [PACK, HALF], F32, tag=tag)
+            else:
+                w1_raw[b, a] = placed.tile([P, PACK, HALF], F32, name=f"w1_raw{b}{a}", offset=a * RAW_BYTES, align_bytes=64)
+            rows = w1[a * HALF : (a + 1) * HALF, b * HALF : (b + 1) * HALF]
+            nc.sync.dma_start(out=w1_raw[b, a][:], in_=rows.rearrange("(p j) n -> p j n", j=PACK))
 
-        def load_w1_low(c, a, tag=None):
-            w1_lo[c, a] = sbuf(f"w1_lo{c}{a}", [PACK, CW], F32, tag=tag)
-            load_w1(w1_lo[c, a][:], a, c * CW, CW)
-
-        def load_w1_high(a):
-            w1_hi[a] = placed.tile([P, PACK, HALF], F32, name=f"w1_hi{a}", offset=a * HIGH_BYTES, align_bytes=64)
-            load_w1(w1_hi[a][:], a, HALF, HALF)
-
-        def load_w2(tag=None):
-            w2_lo[0] = sbuf("w2_words", [HP, 2 * H], U8, tag=tag)
-            nc.sync.dma_start(out=w2_lo[0][:].bitcast(I32), in_=w2_words.rearrange("a p n -> p a n").bitcast(I32))
+        def load_w2(b, tag=None):
+            w2_raw[b] = sbuf(f"w2_raw{b}", [HP, 2 * HALF], U8, tag=tag)
+            cols = w2_words[:, :, b * 2 * HALF : (b + 1) * 2 * HALF]
+            nc.sync.dma_start(out=w2_raw[b][:].bitcast(I32), in_=cols.rearrange("a p n -> p a n").bitcast(I32))
 
         def load_tab_scales(queue):
             for q in range(4):
@@ -85,14 +78,10 @@ def tile_list_citation_chain_gate_kernel(tc, tab_words, tab_scales, offs, pos1, 
         def load_w2_scales(queue):
             for q in range(4):
                 rows = w2_scales[:, 4 * q : 4 * q + 4, :]
-                queue.dma_start(out=w2_s[32 * q : 32 * q + 4, :, :].bitcast(I32), in_=rows.rearrange("a r n -> r a n").bitcast(I32))
+                queue.dma_start(out=w2_s_raw[32 * q : 32 * q + 4, :, :].bitcast(I32), in_=rows.rearrange("a r n -> r a n").bitcast(I32))
 
-        def load_low_gains(queue):
-            with nc.allow_non_contiguous_dma(reason="one gain a partition"):
-                queue.dma_start(out=gain_lo[:], in_=gain[0:HALF].rearrange("(j p) -> p j", p=P))
-
-        def load_high_gains(queue):
-            queue.dma_start(out=gain_hi[:], in_=gain[HALF:].rearrange("(p t) -> p t", t=PACK))
+        def load_gains(queue):
+            queue.dma_start(out=gains[:], in_=gain.rearrange("(b p t) -> p b t", b=HP, t=PACK))
 
         def warm_up():
             warm = sbuf("warm", [1], F32)
@@ -101,8 +90,8 @@ def tile_list_citation_chain_gate_kernel(tc, tab_words, tab_scales, offs, pos1, 
 
         v_w = {}
 
-        def gather_tab(a, pieces, tag=None):
-            v_w[a] = sbuf(f"v_w{a}", [S], U32, tag=tag)
+        def gather_tab(a, pieces):
+            v_w[a] = sbuf(f"v_w{a}", [S], U32, tag="tab_sc" if a == 1 else None)
             step = S // pieces
             for s0 in range(0, S, step):
                 nc.vector.tensor_copy(v_w[a][:, s0 : s0 + step], tab[a][:].bitcast(U32).indirect(offs_sb[:, s0 // 16 : (s0 + step) // 16]))
@@ -110,75 +99,74 @@ def tile_list_citation_chain_gate_kernel(tc, tab_words, tab_scales, offs, pos1, 
         def gather_tab_scales():
             nc.vector.tensor_copy(v_s[:], tab_sc[:].indirect(offs_sb[:]))
 
-        def deal_w2_words_on_pool(tag):
-            w2_hi[0] = sbuf("w2_hi", [HP, 2 * HALF], U8, tag=tag)
-            for b in range(HP):
-                nc.gpsimd.tensor_copy(
-                    out=w2_hi[0][:, b, :].rearrange("p (t m e) -> p t m e", t=PACK, e=2),
-                    in_=w2_lo[0][:, b, 2 * HALF :].rearrange("p (m t e) -> p t m e", t=PACK, e=2),
+        def deal_w2_words(b, engine, tag=None):
+            w2_w[b] = sbuf(f"w2_w{b}", [HP, 2 * HALF], U8, tag=tag)
+            if engine is nc.vector:
+                engine.tensor_copy(
+                    out=w2_w[b][:].bitcast(U16).rearrange("p a (t m) -> p a t m", t=PACK),
+                    in_=w2_raw[b][:].bitcast(U16).rearrange("p a (m t) -> p a t m", t=PACK),
+                )
+                return
+            for a in range(HP):
+                engine.tensor_copy(
+                    out=w2_w[b][:, a, :].rearrange("p (t m e) -> p t m e", t=PACK, e=2),
+                    in_=w2_raw[b][:, a, :].rearrange("p (m t e) -> p t m e", t=PACK, e=2),
                 )
 
-        def deal_w2_scales(tag=None):
-            w2_s_hi[0] = sbuf("w2_s_hi", [HP, HALF], U8, tag=tag)
-            nc.gpsimd.tensor_copy(
-                out=w2_s_hi[0][:].rearrange("p a (t m) -> p a t m", t=PACK),
-                in_=w2_s[:, :, HALF:].rearrange("p a (m t) -> p a t m", t=PACK),
+        def deal_w2_scales(b, engine, tag=None):
+            w2_s[b] = sbuf(f"w2_s{b}", [HP, HALF], U8, tag=tag)
+            engine.tensor_copy(
+                out=w2_s[b][:].rearrange("p a (t m) -> p a t m", t=PACK),
+                in_=w2_s_raw[:, :, b * HALF : (b + 1) * HALF].rearrange("p a (m t) -> p a t m", t=PACK),
             )
 
         w1_c = [sbuf(f"w1_c{a}", [H], U32) for a in range(KP)]
         w1_s = [sbuf(f"w1_s{a}", [H], U8) for a in range(KP)]
+        grouped = {}
 
-        def pool_copy(out, in_):
-            nc.gpsimd.tensor_scalar(out=out, in0=in_, scalar1=1.0, scalar2=0.0, op0=MULT, op1=ADD)
+        def round_w1(b, a, split, tag=None):
+            grouped[b, a] = sbuf(f"grouped{b}{a}", [HALF * PACK], BF16, tag=tag)
+            for copy, ms in ((nc.vector.tensor_copy, slice(0, split)), (nc.scalar.copy, slice(split, P))):
+                if ms.stop > ms.start:
+                    copy(
+                        out=grouped[b, a][:].rearrange("p (t m j) -> p m j t", t=PACK, j=PACK)[:, ms],
+                        in_=w1_raw[b, a][:].rearrange("p j (m t) -> p m j t", t=PACK)[:, ms],
+                    )
 
-        def round_low(c, a, grouped, copy):
-            copy(
-                out=grouped.rearrange("p (g i j) -> p g j i", i=4, j=PACK),
-                in_=w1_lo[c, a][:].rearrange("p j (g i) -> p g j i", i=4),
-            )
-
-        def round_low_on_pool(c, a, grouped):
-            nc.gpsimd.tensor_copy(out=grouped.rearrange("p (n j) -> p n j", j=PACK), in_=w1_lo[c, a][:].rearrange("p j n -> p n j"))
-
-        def round_high(a, grouped, copy, m0=0, m1=P):
-            copy(
-                out=grouped.rearrange("p (t m j) -> p m j t", t=PACK, j=PACK)[:, m0:m1],
-                in_=w1_hi[a][:].rearrange("p j (m t) -> p m j t", t=PACK)[:, m0:m1],
-            )
-
-        def quantise_w1(a, n0, width, grouped):
-            nc.vector.quantize_mx(out=w1_c[a][:, n0 : n0 + width].bitcast(FP8X4), scales=w1_s[a][:, n0 : n0 + width], in_=grouped)
+        def quantise_w1(b, a, pieces=1):
+            width = HALF // pieces
+            for n0 in range(0, HALF, width):
+                cols = slice(b * HALF + n0, b * HALF + n0 + width)
+                nc.vector.quantize_mx(out=w1_c[a][:, cols].bitcast(FP8X4), scales=w1_s[a][:, cols], in_=grouped[b, a][:, PACK * n0 : PACK * (n0 + width)])
 
         h = [sbuf(f"h{j}", [S], F32) for j in range(TILES)]
         acc = {}
-        paired = {}
 
         def first_product(banks, passes):
             for a in passes:
                 for j, s in banks:
                     if a == 0:
                         acc[j, s] = psum.tile([P, BANK], F32, name=f"acc{j}", tag="acc")
-                    codes, scales, cols = w1_c[a], w1_s[a], slice(j * P, (j + 1) * P)
-                    if (j, a) in paired:
-                        codes, scales, cols = paired[j, a]
+                    cols = slice(j * P, (j + 1) * P)
                     nc.tensor.matmul_mx(
                         out=acc[j, s][:],
-                        lhsT=codes[:, cols].bitcast(FP8X4),
-                        lhsT_scale=scales[:, cols],
+                        lhsT=w1_c[a][:, cols].bitcast(FP8X4),
+                        lhsT_scale=w1_s[a][:, cols],
                         rhs=v_w[a][:, s * BANK : (s + 1) * BANK].bitcast(FP8X4),
                         rhs_scale=v_s[4 + 4 * a :, s * BANK : (s + 1) * BANK],
                         start=(a == 0),
                         stop=(a == KP - 1),
                     )
 
-        def empty(j, s, copy=nc.scalar.copy):
-            copy(out=h[j][:, s * BANK : (s + 1) * BANK], in_=acc[j, s][:])
+        def empty(banks):
+            for j, s in banks:
+                nc.scalar.copy(out=h[j][:, s * BANK : (s + 1) * BANK], in_=acc[j, s][:])
 
         xs = {}
 
-        def gather_cited(j, tag=None):
-            xs[j] = sbuf(f"x{j}", [M], F32, tag=tag)
-            nc.vector.tensor_copy(xs[j][:], h[j][:].indirect(pos1_sb[:]))
+        def gather_cited(j, into=None):
+            xs[j] = sbuf(f"x{j}", [M], F32)[:] if into is None else into
+            nc.vector.tensor_copy(xs[j], h[j][:].indirect(pos1_sb[:]))
 
         citing = {}
 
@@ -188,49 +176,33 @@ def tile_list_citation_chain_gate_kernel(tc, tab_words, tab_scales, offs, pos1, 
                 citing[j] = picked[:, n, :]
                 nc.vector.tensor_copy(citing[j], h[j][:].indirect(pos2_sb[:]))
 
-        z_slots = {0: sbuf("z_slots0", [PACK, M], BF16)}
+        z_slots = {}
         ge = {}
 
-        def gelu(j, tag="ge", bufs=4):
-            ge[j] = sbuf(f"ge{j}", [M], F32, tag=tag, bufs=bufs)
-            nc.scalar.activation(out=ge[j][:], in_=xs[j][:], func=ACT.Gelu_apprx_tanh)
+        def gelu(j):
+            ge[j] = sbuf(f"ge{j}", [M], F32)
+            nc.scalar.activation(out=ge[j][:], in_=xs[j], func=ACT.Gelu_apprx_tanh)
 
-        def on_scalar(dst, src, factor):
-            nc.scalar.activation(out=dst, in_=src, func=ACT.Copy, scale=factor)
-
-        def on_vector(dst, src, factor):
-            nc.vector.tensor_scalar(out=dst, in0=src, scalar1=factor, scalar2=None, op0=MULT)
-
-        def on_pool(dst, src, factor):
-            nc.gpsimd.tensor_scalar(out=dst, in0=src, scalar1=factor, scalar2=0.0, op0=MULT, op1=ADD)
-
-        def apply_gain(j, scale, tag=None):
-            if j >= PACK:
-                scale(z_slots[1][:, j - PACK, :], ge[j][:], gain_hi[:, j - PACK : j - PACK + 1])
-                return
-            zb = sbuf(f"zb{j}", [M], BF16, tag=tag)
-            scale(zb[:], ge[j][:], gain_lo[:, j : j + 1])
-            for i in range(PACK):
-                nc.sync.dma_start(out=z_slots[0][32 * j : 32 * j + 32, i, :], in_=zb[i:P:PACK, :])
+        def apply_gain(j, engine):
+            b, t = divmod(j, PACK)
+            dst, factor = z_slots[b][:, t, :], gains[:, b, t : t + 1]
+            if engine is nc.scalar:
+                nc.scalar.activation(out=dst, in_=ge[j][:], func=ACT.Copy, scale=factor)
+            else:
+                engine.tensor_scalar(out=dst, in0=ge[j][:], scalar1=factor, scalar2=0.0, op0=MULT, op1=ADD)
 
         z_c = [sbuf(f"z_c{b}", [M], U32) for b in range(HP)]
         z_s = [sbuf(f"z_s{b}", [M], U8) for b in range(HP)]
         z_grouped = {}
 
-        def weave_z(b, tag=None):
-            z_grouped[b] = sbuf(f"z_grouped{b}", [M, PACK], BF16, tag=tag)
-            nc.vector.tensor_copy(
-                out=z_grouped[b][:].rearrange("p (g i) t -> p g t i", i=4),
-                in_=z_slots[b][:].rearrange("p t (g i) -> p g t i", i=4),
-            )
-
         def weave_z_shared(b, split, tag=None):
             z_grouped[b] = sbuf(f"z_grouped{b}", [M, PACK], BF16, tag=tag)
             for copy, ms in ((nc.vector.tensor_copy, slice(0, split)), (nc.scalar.copy, slice(split, M))):
-                copy(
-                    out=z_grouped[b][:, ms, :].rearrange("p (g i) t -> p g t i", i=4),
-                    in_=z_slots[b][:, :, ms].rearrange("p t (g i) -> p g t i", i=4),
-                )
+                if ms.stop > ms.start:
+                    copy(
+                        out=z_grouped[b][:, ms, :].rearrange("p (g i) t -> p g t i", i=4),
+                        in_=z_slots[b][:, :, ms].rearrange("p t (g i) -> p g t i", i=4),
+                    )
 
         def weave_z_on_pool(b, tag=None):
             z_grouped[b] = sbuf(f"z_grouped{b}", [M, PACK], BF16, tag=tag)
@@ -241,25 +213,25 @@ def tile_list_citation_chain_gate_kernel(tc, tab_words, tab_scales, offs, pos1, 
 
         y = {}
 
-        def second_product(b, tiles):
-            for j in tiles:
-                if b == 0:
-                    y[j] = psum.tile([P, BANK], F32, name=f"y{j}", tag="acc")
-                n = j % PACK
-                nc.tensor.matmul_mx(
-                    out=y[j][:],
-                    lhsT=(w2_lo[0] if j < PACK else w2_hi[0])[:, b, 2 * n * P : 2 * (n + 1) * P].bitcast(FP4X4),
-                    lhsT_scale=(w2_s if j < PACK else w2_s_hi[0])[:, b, n * P : (n + 1) * P],
-                    rhs=z_c[b][:].bitcast(FP8X4),
-                    rhs_scale=z_s[b][:],
-                    start=(b == 0),
-                    stop=(b == HP - 1),
-                )
+        def second_product():
+            for j in range(TILES):
+                y[j] = psum.tile([P, BANK], F32, name=f"y{j}", tag="acc")
+                b, n = divmod(j, PACK)
+                for a in range(HP):
+                    nc.tensor.matmul_mx(
+                        out=y[j][:],
+                        lhsT=w2_w[b][:, a, 2 * n * P : 2 * (n + 1) * P].bitcast(FP4X4),
+                        lhsT_scale=w2_s[b][:, a, n * P : (n + 1) * P],
+                        rhs=z_c[a][:].bitcast(FP8X4),
+                        rhs_scale=z_s[a][:],
+                        start=(a == 0),
+                        stop=(a == HP - 1),
+                    )
 
-        out_hi = out[HALF:, :].rearrange("(p t) m -> p t m", t=PACK)
+        out_rows = out.rearrange("(b p t) m -> p b t m", b=HP, t=PACK)
 
         def store(j, gated, ms=slice(0, M)):
-            nc.sync.dma_start(out=out[j * P : (j + 1) * P, ms] if j < PACK else out_hi[:, j - PACK, ms], in_=gated)
+            nc.sync.dma_start(out=out_rows[:, j // PACK, j % PACK, ms], in_=gated)
 
         def finish(on_pool):
             gates = {}
@@ -267,104 +239,94 @@ def tile_list_citation_chain_gate_kernel(tc, tab_words, tab_scales, offs, pos1, 
                 if j < on_pool:
                     gates[j] = placed.tile([P, M], F32, name=f"gate{j}", offset=j * GATE_BYTES, align_bytes=64)
                 else:
-                    gates[j] = sbuf(f"gate{j}", [M], F32)
+                    gates[j] = sbuf(f"gate{j}", [M], F32, tag=f"ge{j}")
                 nc.scalar.activation(out=gates[j][:], in_=y[j][:], func=ACT.Sigmoid)
             for j in range(on_pool):
                 nc.gpsimd.tensor_tensor(out=citing[j], in0=gates[j][:], in1=citing[j], op=MULT)
                 store(j, citing[j])
-            gated = placed.tile([P, TILES - on_pool, M], F32, name="gated", offset=max(on_pool - 1, 0) * GATE_BYTES, align_bytes=64)
+            gated = placed.tile([P, TILES - on_pool, M], F32, name="gated", offset=(on_pool - 1) * GATE_BYTES, align_bytes=64)
             for j in range(on_pool, TILES):
                 for ms in [slice(0, M)] if j < TILES - 1 else [slice(0, LAST_SPLIT), slice(LAST_SPLIT, M)]:
                     nc.vector.tensor_tensor(out=gated[:, j - on_pool, ms], in0=gates[j][:, ms], in1=citing[j][:, ms], op=MULT)
                     store(j, gated[:, j - on_pool, ms], ms)
 
+        V, A, G = nc.vector, nc.scalar, nc.gpsimd
         nc.vector.memset(tab_sc[:].bitcast(I32), 0)
-        nc.vector.memset(w2_s[:].rearrange("p a n -> p (a n)").bitcast(I32), 0)
+        nc.vector.memset(w2_s_raw[:].rearrange("p a n -> p (a n)").bitcast(I32), 0)
         load_tab(0)
         nc.sync.dma_start(offs_sb[:], offs)
-        for a in range(KP):
-            load_w1_low(0, a, "tab2" if a == 0 else None)
+        load_w1(0, 0)
+        load_w2(0)
+        load_w1(0, 1, "tab2")
         nc.sync.dma_start(pos1_sb[:], pos1)
         nc.sync.dma_start(pos2_sb[:], pos2)
-        load_tab_scales(nc.gpsimd)
-        load_w2_scales(nc.gpsimd)
+        load_gains(nc.sync)
+        load_tab_scales(G)
+        load_w2_scales(G)
         warm_up()
-        load_low_gains(nc.gpsimd)
-        load_high_gains(nc.gpsimd)
         gather_tab(0, 1)
         load_tab(1)
-        for a in range(KP):
-            grouped0 = sbuf(f"grouped0{a}", [CW * PACK], BF16)
-            round_low(0, a, grouped0[:], nc.scalar.copy)
-            quantise_w1(a, 0, CW, grouped0[:])
+        round_w1(0, 0, 0)
+        quantise_w1(0, 0)
+        load_w1(0, 2, "w1_raw00")
+        round_w1(0, 1, 0)
+        quantise_w1(0, 1)
         load_tab(2)
         gather_tab_scales()
-        for a, tag in enumerate(["grouped00", "w1_lo01", "w1_lo02"]):
-            load_w1_low(1, a, tag)
+        deal_w2_words(0, V)
         gather_tab(1, 1)
+        for b in range(HP):
+            deal_w2_scales(b, V)
         for a in range(KP):
-            load_w1_high(a)
+            load_w1(1, a)
+        round_w1(0, 2, 0, "grouped01")
+        quantise_w1(0, 2)
         gather_tab(2, 2)
-
-        first_product([(0, 0), (1, 0), (0, 1), (1, 1)], range(KP))
-        for j, s in [(0, 0), (1, 0), (0, 1), (1, 1)]:
-            empty(j, s)
-        grouped1 = [sbuf(f"grouped1{a}", [CW * PACK], BF16, tag=28672 if a else None) for a in range(KP)]
-        round_low_on_pool(1, 0, grouped1[0][:])
-        round_low(1, 1, grouped1[1][:], nc.vector.tensor_copy)
-        for a in range(2):
-            quantise_w1(a, CW, CW, grouped1[a][:])
-        round_low_on_pool(1, 2, grouped1[2][:])
-        gather_cited(0)
-        gather_cited(1)
-        quantise_w1(2, CW, CW, grouped1[2][:])
-        second = [(2, 0), (2, 1), (3, 0), (3, 1)]
-        first_product(second, range(KP))
-        for j, s in second:
-            empty(j, s)
-        for j in range(2):
-            gelu(j)
-        apply_gain(0, on_scalar)
-        load_w2("x0")
-        high = [sbuf(f"high{a}", [HALF * PACK], BF16, tag=[28672, None, 20480][a]) for a in range(KP)]
-        for a, split in enumerate([128, 0, 96]):
-            if split:
-                round_high(a, high[a][:], nc.vector.tensor_copy, 0, split)
-            if split < P:
-                round_high(a, high[a][:], nc.scalar.copy, split, P)
-            if a < KP - 1:
-                quantise_w1(a, HALF, HALF, high[a][:])
-        for c in range(2):
-            quantise_w1(2, HALF + c * CW, CW, high[2][:, c * CW * PACK : (c + 1) * CW * PACK])
+        lower = [(0, 0), (1, 0), (0, 1), (1, 1), (2, 0), (2, 1), (3, 0), (3, 1)]
+        first_product(lower, range(KP))
+        empty(lower)
+        load_w2(1, "grouped01")
+        splits = [128, 0, 96]
+        round_w1(1, 0, splits[0])
+        quantise_w1(1, 0)
+        for j in range(3):
+            gather_cited(j)
+        round_w1(1, 1, splits[1], None)
+        round_w1(1, 2, splits[2], 8192)
+        quantise_w1(1, 1)
+        quantise_w1(1, 2, 2)
         upper = [(j, s) for j in range(PACK, TILES) for s in range(2)]
         first_product(upper, [0])
         for bank in upper:
             first_product([bank], [1, 2])
-        apply_gain(1, on_pool, 28672)
-        deal_w2_scales(29696)
-        gather_cited(2)
-        gather_cited(3)
+        held = sbuf("held", [3, M], F32, tag=8192 + 64 - 6144)
+        gather_cited(3, held[:, 0, :])
+        z_slots[0] = sbuf("z_slots0", [PACK, M], BF16, tag=12288 - 64)
+        lower_gain = [G, G, G, A]
+        for j in range(2):
+            gelu(j)
+            apply_gain(j, lower_gain[j])
+        deal_w2_words(1, G, 8192 + 64)
+        empty(upper[:2])
         for j in range(2, PACK):
             gelu(j)
-            apply_gain(j, on_scalar)
-        deal_w2_words_on_pool(22528)
-        for j, s in upper:
-            empty(j, s)
+            apply_gain(j, lower_gain[j])
+        empty(upper[2:])
         for j in range(PACK, TILES):
             gather_cited(j)
         for j in range(PACK, TILES):
             gelu(j)
-        gather_citing([0, 1], 17408)
-        weave_z_on_pool(0, 0)
+        for j in range(2):
+            citing[j] = held[:, 1 + j, :]
+            nc.vector.tensor_copy(citing[j], h[j][:].indirect(pos2_sb[:]))
+        weave_z_on_pool(0)
         quantise_z(0)
-        gather_citing([2], "z_slots0")
+        gather_citing([2], 12288)
         z_slots[1] = sbuf("z_slots1", [PACK, M], BF16)
         for j in range(PACK, TILES):
-            apply_gain(j, on_vector if j < 6 else on_scalar)
-        weave_z_shared(1, 336, 2048)
+            apply_gain(j, V if j < 6 else A)
+        weave_z_shared(1, 336)
         quantise_z(1)
-        for j in range(TILES):
-            second_product(0, [j])
-            second_product(1, [j])
+        second_product()
         gather_citing([3, 4, 5, 6, 7], "z_slots1")
         finish(3)

@@ -42,12 +42,17 @@ def tile_list_citation_chain_gate_kernel(tc, tab_words, tab_scales, offs, pos1, 
                 return chain.tile([P] + shape, dtype, name=name, offset=tag, align_bytes=64)
             return keep.tile([P] + shape, dtype, name=name, tag=tag or name, bufs=bufs, align_bytes=64)
 
+        def over(name, shape, dtype, at):
+            if at is None:
+                return sbuf(name, shape, dtype)
+            return placed.tile([P] + shape, dtype, name=name, offset=at, align_bytes=64)
+
         offs_sb = sbuf("offs_sb", [S // 16], U16)
         pos1_sb = sbuf("pos1_sb", [M // 16], U16)
         pos2_sb = sbuf("pos2_sb", [M // 16], U16)
         tab_sc = sbuf("tab_sc", [T], U8)
-        gains = sbuf("gains", [HP, PACK], F32)
-        w2_s_raw = sbuf("w2_s_raw", [HP, H], U8)
+        gains = {}
+        raws = {}
         v_s = sbuf("v_s", [S], U8)
         tab, w1_raw, w2_raw, w2_w, w2_s = {}, {}, {}, {}, {}
 
@@ -75,13 +80,16 @@ def tile_list_citation_chain_gate_kernel(tc, tab_words, tab_scales, offs, pos1, 
                     in_=tab_scales[:, 4 * q : 4 * q + 4, :].bitcast(I32),
                 )
 
-        def load_w2_scales(queue):
+        def load_w2_scales(queue, tag=None):
+            w2_s_raw = raws["w2_s"] = sbuf("w2_s_raw", [HP, H], U8, tag=tag)
+            nc.vector.memset(w2_s_raw[:].rearrange("p a n -> p (a n)").bitcast(I32), 0)
             for q in range(4):
                 rows = w2_scales[:, 4 * q : 4 * q + 4, :]
                 queue.dma_start(out=w2_s_raw[32 * q : 32 * q + 4, :, :].bitcast(I32), in_=rows.rearrange("a r n -> r a n").bitcast(I32))
 
-        def load_gains(queue):
-            queue.dma_start(out=gains[:], in_=gain.rearrange("(b p t) -> p b t", b=HP, t=PACK))
+        def load_gains(queue, tag=None):
+            gains[0] = sbuf("gains", [HP, PACK], F32, tag=tag)
+            queue.dma_start(out=gains[0][:], in_=gain.rearrange("(b p t) -> p b t", b=HP, t=PACK))
 
         def warm_up():
             warm = sbuf("warm", [1], F32)
@@ -117,11 +125,10 @@ def tile_list_citation_chain_gate_kernel(tc, tab_words, tab_scales, offs, pos1, 
             w2_s[b] = sbuf(f"w2_s{b}", [HP, HALF], U8, tag=tag)
             engine.tensor_copy(
                 out=w2_s[b][:].rearrange("p a (t m) -> p a t m", t=PACK),
-                in_=w2_s_raw[:, :, b * HALF : (b + 1) * HALF].rearrange("p a (m t) -> p a t m", t=PACK),
+                in_=raws["w2_s"][:, :, b * HALF : (b + 1) * HALF].rearrange("p a (m t) -> p a t m", t=PACK),
             )
 
-        w1_c = [sbuf(f"w1_c{a}", [H], U32) for a in range(KP)]
-        w1_s = [sbuf(f"w1_s{a}", [H], U8) for a in range(KP)]
+        w1_c, w1_s = {}, {}
         grouped = {}
 
         def round_w1(b, a, split, tag=None):
@@ -133,11 +140,13 @@ def tile_list_citation_chain_gate_kernel(tc, tab_words, tab_scales, offs, pos1, 
                         in_=w1_raw[b, a][:].rearrange("p j (m t) -> p m j t", t=PACK)[:, ms],
                     )
 
-        def quantise_w1(b, a, pieces=1):
+        def quantise_w1(b, a, pieces=1, at=None):
+            w1_c[b, a] = over(f"w1_c{b}{a}", [HALF], U32, at)
+            w1_s[b, a] = sbuf(f"w1_s{b}{a}", [HALF], U8)
             width = HALF // pieces
             for n0 in range(0, HALF, width):
-                cols = slice(b * HALF + n0, b * HALF + n0 + width)
-                nc.vector.quantize_mx(out=w1_c[a][:, cols].bitcast(FP8X4), scales=w1_s[a][:, cols], in_=grouped[b, a][:, PACK * n0 : PACK * (n0 + width)])
+                cols = slice(n0, n0 + width)
+                nc.vector.quantize_mx(out=w1_c[b, a][:, cols].bitcast(FP8X4), scales=w1_s[b, a][:, cols], in_=grouped[b, a][:, PACK * n0 : PACK * (n0 + width)])
 
         h = [sbuf(f"h{j}", [S], F32) for j in range(TILES)]
         acc = {}
@@ -147,11 +156,12 @@ def tile_list_citation_chain_gate_kernel(tc, tab_words, tab_scales, offs, pos1, 
                 for j, s in banks:
                     if a == 0:
                         acc[j, s] = psum.tile([P, BANK], F32, name=f"acc{j}", tag="acc")
-                    cols = slice(j * P, (j + 1) * P)
+                    b, t = divmod(j, PACK)
+                    cols = slice(t * P, (t + 1) * P)
                     nc.tensor.matmul_mx(
                         out=acc[j, s][:],
-                        lhsT=w1_c[a][:, cols].bitcast(FP8X4),
-                        lhsT_scale=w1_s[a][:, cols],
+                        lhsT=w1_c[b, a][:, cols].bitcast(FP8X4),
+                        lhsT_scale=w1_s[b, a][:, cols],
                         rhs=v_w[a][:, s * BANK : (s + 1) * BANK].bitcast(FP8X4),
                         rhs_scale=v_s[4 + 4 * a :, s * BANK : (s + 1) * BANK],
                         start=(a == 0),
@@ -164,8 +174,8 @@ def tile_list_citation_chain_gate_kernel(tc, tab_words, tab_scales, offs, pos1, 
 
         xs = {}
 
-        def gather_cited(j, into=None):
-            xs[j] = sbuf(f"x{j}", [M], F32)[:] if into is None else into
+        def gather_cited(j, into=None, at=None):
+            xs[j] = over(f"x{j}", [M], F32, at)[:] if into is None else into
             nc.vector.tensor_copy(xs[j], h[j][:].indirect(pos1_sb[:]))
 
         citing = {}
@@ -179,13 +189,13 @@ def tile_list_citation_chain_gate_kernel(tc, tab_words, tab_scales, offs, pos1, 
         z_slots = {}
         ge = {}
 
-        def gelu(j):
-            ge[j] = sbuf(f"ge{j}", [M], F32)
+        def gelu(j, at=None):
+            ge[j] = over(f"ge{j}", [M], F32, at)
             nc.scalar.activation(out=ge[j][:], in_=xs[j], func=ACT.Gelu_apprx_tanh)
 
         def apply_gain(j, engine):
             b, t = divmod(j, PACK)
-            dst, factor = z_slots[b][:, t, :], gains[:, b, t : t + 1]
+            dst, factor = z_slots[b][:, t, :], gains[0][:, b, t : t + 1]
             if engine is nc.scalar:
                 nc.scalar.activation(out=dst, in_=ge[j][:], func=ACT.Copy, scale=factor)
             else:
@@ -252,7 +262,6 @@ def tile_list_citation_chain_gate_kernel(tc, tab_words, tab_scales, offs, pos1, 
 
         V, A, G = nc.vector, nc.scalar, nc.gpsimd
         nc.vector.memset(tab_sc[:].bitcast(I32), 0)
-        nc.vector.memset(w2_s_raw[:].rearrange("p a n -> p (a n)").bitcast(I32), 0)
         load_tab(0)
         nc.sync.dma_start(offs_sb[:], offs)
         load_w1(0, 0)
@@ -260,9 +269,7 @@ def tile_list_citation_chain_gate_kernel(tc, tab_words, tab_scales, offs, pos1, 
         load_w1(0, 1, "tab2")
         nc.sync.dma_start(pos1_sb[:], pos1)
         nc.sync.dma_start(pos2_sb[:], pos2)
-        load_gains(nc.sync)
         load_tab_scales(G)
-        load_w2_scales(G)
         warm_up()
         gather_tab(0, 1)
         load_tab(1)
@@ -274,6 +281,7 @@ def tile_list_citation_chain_gate_kernel(tc, tab_words, tab_scales, offs, pos1, 
         load_tab(2)
         gather_tab_scales()
         deal_w2_words(0, V)
+        load_w2_scales(nc.sync, "w2_raw0")
         gather_tab(1, 1)
         for b in range(HP):
             deal_w2_scales(b, V)
@@ -282,18 +290,20 @@ def tile_list_citation_chain_gate_kernel(tc, tab_words, tab_scales, offs, pos1, 
         round_w1(0, 2, 0, "grouped01")
         quantise_w1(0, 2)
         gather_tab(2, 2)
+        load_gains(G, "tab2")
         lower = [(0, 0), (1, 0), (0, 1), (1, 1), (2, 0), (2, 1), (3, 0), (3, 1)]
         first_product(lower, range(KP))
         empty(lower)
         load_w2(1, "grouped01")
         splits = [128, 0, 96]
         round_w1(1, 0, splits[0])
+        gather_cited(0, at=0)
         quantise_w1(1, 0)
-        for j in range(3):
-            gather_cited(j)
+        for j in range(1, 3):
+            gather_cited(j, at=j * GATE_BYTES)
         round_w1(1, 1, splits[1], None)
         round_w1(1, 2, splits[2], 8192)
-        quantise_w1(1, 1)
+        quantise_w1(1, 1, at=2 * RAW_BYTES + 3 * GATE_BYTES)
         quantise_w1(1, 2, 2)
         upper = [(j, s) for j in range(PACK, TILES) for s in range(2)]
         first_product(upper, [0])
@@ -304,12 +314,12 @@ def tile_list_citation_chain_gate_kernel(tc, tab_words, tab_scales, offs, pos1, 
         z_slots[0] = sbuf("z_slots0", [PACK, M], BF16, tag=12288 - 64)
         lower_gain = [G, G, G, A]
         for j in range(2):
-            gelu(j)
+            gelu(j, 2 * RAW_BYTES + j * GATE_BYTES)
             apply_gain(j, lower_gain[j])
         deal_w2_words(1, G, 8192 + 64)
         empty(upper[:2])
         for j in range(2, PACK):
-            gelu(j)
+            gelu(j, 2 * RAW_BYTES + j * GATE_BYTES if j == 2 else None)
             apply_gain(j, lower_gain[j])
         empty(upper[2:])
         for j in range(PACK, TILES):
@@ -324,7 +334,7 @@ def tile_list_citation_chain_gate_kernel(tc, tab_words, tab_scales, offs, pos1, 
         gather_citing([2], 12288)
         z_slots[1] = sbuf("z_slots1", [PACK, M], BF16)
         for j in range(PACK, TILES):
-            apply_gain(j, V if j < 6 else A)
+            apply_gain(j, [G, G, A, A][j - PACK])
         weave_z_shared(1, 336)
         quantise_z(1)
         second_product()

@@ -269,6 +269,7 @@ def tile_list_citation_chain_gate_kernel(tc, tab_words, tab_scales, offs, pos1, 
         load_w1(0, 1, "tab2")
         nc.sync.dma_start(pos1_sb[:], pos1)
         nc.sync.dma_start(pos2_sb[:], pos2)
+        load_gains(nc.sync)
         load_tab_scales(G)
         warm_up()
         gather_tab(0, 1)
@@ -290,7 +291,6 @@ def tile_list_citation_chain_gate_kernel(tc, tab_words, tab_scales, offs, pos1, 
         round_w1(0, 2, 0, "grouped01")
         quantise_w1(0, 2)
         gather_tab(2, 2)
-        load_gains(G, "tab2")
         lower = [(0, 0), (1, 0), (0, 1), (1, 1), (2, 0), (2, 1), (3, 0), (3, 1)]
         first_product(lower, range(KP))
         empty(lower)
@@ -334,7 +334,7 @@ def tile_list_citation_chain_gate_kernel(tc, tab_words, tab_scales, offs, pos1, 
         gather_citing([2], 12288)
         z_slots[1] = sbuf("z_slots1", [PACK, M], BF16)
         for j in range(PACK, TILES):
-            apply_gain(j, [G, G, A, A][j - PACK])
+            apply_gain(j, [V, V, A, A][j - PACK])
         weave_z_shared(1, 336)
         quantise_z(1)
         second_product()

@@ -24,132 +24,74 @@ KP = K // HALF
 HP = H // HALF
 TILES = H // P
 BANK = 512
-RAW_BYTES = PACK * HALF * 4
-GATE_BYTES = M * 4
-LAST_SPLIT = 256
+RAW = PACK * HALF * 4
+ROW = M * 4
+ROUNDED_AT = 3 * ROW
+WEAVE_SPLIT = 336
+ON_GPSIMD = 3
 
 
 def tile_list_citation_chain_gate_kernel(tc, tab_words, tab_scales, offs, pos1, pos2, w1, gain, w2_words, w2_scales, out):
     nc = tc.nc
     with ExitStack() as ctx:
         keep = ctx.enter_context(tc.tile_pool(name="keep", bufs=1))
-        placed = ctx.enter_context(tc.tile_pool(name="placed", bufs=1))
-        chain = ctx.enter_context(tc.tile_pool(name="chain", bufs=1))
+        upper = ctx.enter_context(tc.tile_pool(name="upper", bufs=1))
+        turn = ctx.enter_context(tc.tile_pool(name="turn", bufs=1))
         psum = ctx.enter_context(tc.psum_pool(name="psum", bufs=8))
 
-        def sbuf(name, shape, dtype, tag=None, bufs=1):
-            if isinstance(tag, int):
-                return chain.tile([P] + shape, dtype, name=name, offset=tag, align_bytes=64)
-            return keep.tile([P] + shape, dtype, name=name, tag=tag or name, bufs=bufs, align_bytes=64)
+        def kept(name, shape, dtype, tag=None):
+            return keep.tile([P] + shape, dtype, name=name, tag=tag or name, align_bytes=64)
 
-        def over(name, shape, dtype, at):
-            if at is None:
-                return sbuf(name, shape, dtype)
-            return placed.tile([P] + shape, dtype, name=name, offset=at, align_bytes=64)
+        def laid(pool, at, name, shape, dtype):
+            return pool.tile([P] + shape, dtype, name=name, offset=at, align_bytes=64)
 
-        offs_sb = sbuf("offs_sb", [S // 16], U16)
-        pos1_sb = sbuf("pos1_sb", [M // 16], U16)
-        pos2_sb = sbuf("pos2_sb", [M // 16], U16)
-        tab_sc = sbuf("tab_sc", [T], U8)
-        gains = {}
-        raws = {}
-        v_s = sbuf("v_s", [S], U8)
-        tab, w1_raw, w2_raw, w2_w, w2_s = {}, {}, {}, {}, {}
+        offs_sb = kept("offs_sb", [S // 16], U16)
+        pos1_sb = kept("pos1_sb", [M // 16], U16)
+        pos2_sb = kept("pos2_sb", [M // 16], U16)
+        tab_sc = kept("tab_sc", [T], U8)
+        v_s = kept("v_s", [S], U8)
+        tab, v_w, w1_raw, rounded, w1_c, w1_s, w2_raw, w2_w, w2_s = {}, {}, {}, {}, {}, {}, {}, {}, {}
+        acc, cited, citing, gelus, z_slots, z_woven = {}, {}, {}, {}, {}, {}
 
-        def load_tab(a, tag=None):
-            tab[a] = sbuf(f"tab{a}", [T], I32, tag=tag) if a == KP - 1 else placed.tile([P, T], I32, name=f"tab{a}", offset=RAW_BYTES // 2, align_bytes=64)
-            nc.sync.dma_start(out=tab[a][:], in_=tab_words[a].rearrange("p t i -> p (t i)").bitcast(I32))
+        def load_tab(a, tile):
+            tab[a] = tile
+            nc.sync.dma_start(out=tile[:], in_=tab_words[a].rearrange("p t i -> p (t i)").bitcast(I32))
 
-        def load_w1(b, a, tag=None):
-            if b == 0:
-                w1_raw[b, a] = sbuf(f"w1_raw{b}{a}", [PACK, HALF], F32, tag=tag)
-            else:
-                w1_raw[b, a] = placed.tile([P, PACK, HALF], F32, name=f"w1_raw{b}{a}", offset=a * RAW_BYTES, align_bytes=64)
+        def load_w1(b, a, tile):
+            w1_raw[b, a] = tile
             rows = w1[a * HALF : (a + 1) * HALF, b * HALF : (b + 1) * HALF]
-            nc.sync.dma_start(out=w1_raw[b, a][:], in_=rows.rearrange("(p j) n -> p j n", j=PACK))
+            nc.sync.dma_start(out=tile[:], in_=rows.rearrange("(p j) n -> p j n", j=PACK))
 
         def load_w2(b, tag=None):
-            w2_raw[b] = sbuf(f"w2_raw{b}", [HP, 2 * HALF], U8, tag=tag)
+            w2_raw[b] = kept(f"w2_raw{b}", [HP, 2 * HALF], U8, tag)
             cols = w2_words[:, :, b * 2 * HALF : (b + 1) * 2 * HALF]
             nc.sync.dma_start(out=w2_raw[b][:].bitcast(I32), in_=cols.rearrange("a p n -> p a n").bitcast(I32))
 
-        def load_tab_scales(queue):
-            for q in range(4):
-                queue.dma_start(
-                    out=tab_sc[32 * q + 4 : 32 * q + 4 + 4 * KP, :].bitcast(I32),
-                    in_=tab_scales[:, 4 * q : 4 * q + 4, :].bitcast(I32),
-                )
-
-        def load_w2_scales(queue, tag=None):
-            w2_s_raw = raws["w2_s"] = sbuf("w2_s_raw", [HP, H], U8, tag=tag)
-            nc.vector.memset(w2_s_raw[:].rearrange("p a n -> p (a n)").bitcast(I32), 0)
-            for q in range(4):
-                rows = w2_scales[:, 4 * q : 4 * q + 4, :]
-                queue.dma_start(out=w2_s_raw[32 * q : 32 * q + 4, :, :].bitcast(I32), in_=rows.rearrange("a r n -> r a n").bitcast(I32))
-
-        def load_gains(queue, tag=None):
-            gains[0] = sbuf("gains", [HP, PACK], F32, tag=tag)
-            queue.dma_start(out=gains[0][:], in_=gain.rearrange("(b p t) -> p b t", b=HP, t=PACK))
-
-        def warm_up():
-            warm = sbuf("warm", [1], F32)
-            nc.gpsimd.memset(warm[:], 0.0)
-            nc.scalar.activation(out=warm[:], in_=warm[:], func=ACT.Gelu_apprx_tanh)
-
-        v_w = {}
-
-        def gather_tab(a, pieces):
-            v_w[a] = sbuf(f"v_w{a}", [S], U32, tag="tab_sc" if a == 1 else None)
+        def gather_tab(a, pieces, tag=None):
+            v_w[a] = kept(f"v_w{a}", [S], U32, tag)
             step = S // pieces
             for s0 in range(0, S, step):
                 nc.vector.tensor_copy(v_w[a][:, s0 : s0 + step], tab[a][:].bitcast(U32).indirect(offs_sb[:, s0 // 16 : (s0 + step) // 16]))
 
-        def gather_tab_scales():
-            nc.vector.tensor_copy(v_s[:], tab_sc[:].indirect(offs_sb[:]))
-
-        def deal_w2_words(b, engine, tag=None):
-            w2_w[b] = sbuf(f"w2_w{b}", [HP, 2 * HALF], U8, tag=tag)
-            if engine is nc.vector:
-                engine.tensor_copy(
-                    out=w2_w[b][:].bitcast(U16).rearrange("p a (t m) -> p a t m", t=PACK),
-                    in_=w2_raw[b][:].bitcast(U16).rearrange("p a (m t) -> p a t m", t=PACK),
-                )
-                return
-            for a in range(HP):
-                engine.tensor_copy(
-                    out=w2_w[b][:, a, :].rearrange("p (t m e) -> p t m e", t=PACK, e=2),
-                    in_=w2_raw[b][:, a, :].rearrange("p (m t e) -> p t m e", t=PACK, e=2),
-                )
-
-        def deal_w2_scales(b, engine, tag=None):
-            w2_s[b] = sbuf(f"w2_s{b}", [HP, HALF], U8, tag=tag)
-            engine.tensor_copy(
-                out=w2_s[b][:].rearrange("p a (t m) -> p a t m", t=PACK),
-                in_=raws["w2_s"][:, :, b * HALF : (b + 1) * HALF].rearrange("p a (m t) -> p a t m", t=PACK),
+        def round_w1(b, a, copy, tile):
+            rounded[b, a] = tile
+            copy(
+                out=tile[:].rearrange("p (t m j) -> p m j t", t=PACK, j=PACK),
+                in_=w1_raw[b, a][:].rearrange("p j (m t) -> p m j t", t=PACK),
             )
 
-        w1_c, w1_s = {}, {}
-        grouped = {}
-
-        def round_w1(b, a, split, tag=None):
-            grouped[b, a] = sbuf(f"grouped{b}{a}", [HALF * PACK], BF16, tag=tag)
-            for copy, ms in ((nc.vector.tensor_copy, slice(0, split)), (nc.scalar.copy, slice(split, P))):
-                if ms.stop > ms.start:
-                    copy(
-                        out=grouped[b, a][:].rearrange("p (t m j) -> p m j t", t=PACK, j=PACK)[:, ms],
-                        in_=w1_raw[b, a][:].rearrange("p j (m t) -> p m j t", t=PACK)[:, ms],
-                    )
-
-        def quantise_w1(b, a, pieces=1, at=None):
-            w1_c[b, a] = over(f"w1_c{b}{a}", [HALF], U32, at)
-            w1_s[b, a] = sbuf(f"w1_s{b}{a}", [HALF], U8)
+        def quantise_w1(b, a, pieces=1, codes=None):
+            w1_c[b, a] = codes or kept(f"w1_c{b}{a}", [HALF], U32)
+            w1_s[b, a] = kept(f"w1_s{b}{a}", [HALF], U8)
             width = HALF // pieces
             for n0 in range(0, HALF, width):
-                cols = slice(n0, n0 + width)
-                nc.vector.quantize_mx(out=w1_c[b, a][:, cols].bitcast(FP8X4), scales=w1_s[b, a][:, cols], in_=grouped[b, a][:, PACK * n0 : PACK * (n0 + width)])
+                nc.vector.quantize_mx(
+                    out=w1_c[b, a][:, n0 : n0 + width].bitcast(FP8X4),
+                    scales=w1_s[b, a][:, n0 : n0 + width],
+                    in_=rounded[b, a][:, PACK * n0 : PACK * (n0 + width)],
+                )
 
-        h = [sbuf(f"h{j}", [S], F32) for j in range(TILES)]
-        acc = {}
+        h = [kept(f"h{j}", [S], F32) for j in range(TILES)]
 
         def first_product(banks, passes):
             for a in passes:
@@ -157,11 +99,10 @@ def tile_list_citation_chain_gate_kernel(tc, tab_words, tab_scales, offs, pos1, 
                     if a == 0:
                         acc[j, s] = psum.tile([P, BANK], F32, name=f"acc{j}", tag="acc")
                     b, t = divmod(j, PACK)
-                    cols = slice(t * P, (t + 1) * P)
                     nc.tensor.matmul_mx(
                         out=acc[j, s][:],
-                        lhsT=w1_c[b, a][:, cols].bitcast(FP8X4),
-                        lhsT_scale=w1_s[b, a][:, cols],
+                        lhsT=w1_c[b, a][:, t * P : (t + 1) * P].bitcast(FP8X4),
+                        lhsT_scale=w1_s[b, a][:, t * P : (t + 1) * P],
                         rhs=v_w[a][:, s * BANK : (s + 1) * BANK].bitcast(FP8X4),
                         rhs_scale=v_s[4 + 4 * a :, s * BANK : (s + 1) * BANK],
                         start=(a == 0),
@@ -172,171 +113,170 @@ def tile_list_citation_chain_gate_kernel(tc, tab_words, tab_scales, offs, pos1, 
             for j, s in banks:
                 nc.scalar.copy(out=h[j][:, s * BANK : (s + 1) * BANK], in_=acc[j, s][:])
 
-        xs = {}
+        def gather_cited(j, into):
+            cited[j] = into
+            nc.vector.tensor_copy(into, h[j][:].indirect(pos1_sb[:]))
 
-        def gather_cited(j, into=None, at=None):
-            xs[j] = over(f"x{j}", [M], F32, at)[:] if into is None else into
-            nc.vector.tensor_copy(xs[j], h[j][:].indirect(pos1_sb[:]))
+        def gather_citing(j, into):
+            citing[j] = into
+            nc.vector.tensor_copy(into, h[j][:].indirect(pos2_sb[:]))
 
-        citing = {}
-
-        def gather_citing(tiles, tag=None):
-            picked = sbuf(f"citing{tiles[0]}", [len(tiles), M], F32, tag=tag)
-            for n, j in enumerate(tiles):
-                citing[j] = picked[:, n, :]
-                nc.vector.tensor_copy(citing[j], h[j][:].indirect(pos2_sb[:]))
-
-        z_slots = {}
-        ge = {}
-
-        def gelu(j, at=None):
-            ge[j] = over(f"ge{j}", [M], F32, at)
-            nc.scalar.activation(out=ge[j][:], in_=xs[j], func=ACT.Gelu_apprx_tanh)
+        def gelu(j, tile):
+            gelus[j] = tile
+            nc.scalar.activation(out=tile[:], in_=cited[j], func=ACT.Gelu_apprx_tanh)
 
         def apply_gain(j, engine):
             b, t = divmod(j, PACK)
-            dst, factor = z_slots[b][:, t, :], gains[0][:, b, t : t + 1]
+            dst, factor = z_slots[b][:, t, :], gains[:, b, t : t + 1]
             if engine is nc.scalar:
-                nc.scalar.activation(out=dst, in_=ge[j][:], func=ACT.Copy, scale=factor)
+                nc.scalar.activation(out=dst, in_=gelus[j][:], func=ACT.Copy, scale=factor)
             else:
-                engine.tensor_scalar(out=dst, in0=ge[j][:], scalar1=factor, scalar2=0.0, op0=MULT, op1=ADD)
+                engine.tensor_scalar(out=dst, in0=gelus[j][:], scalar1=factor, scalar2=0.0, op0=MULT, op1=ADD)
 
-        z_c = [sbuf(f"z_c{b}", [M], U32) for b in range(HP)]
-        z_s = [sbuf(f"z_s{b}", [M], U8) for b in range(HP)]
-        z_grouped = {}
-
-        def weave_z_shared(b, split, tag=None):
-            z_grouped[b] = sbuf(f"z_grouped{b}", [M, PACK], BF16, tag=tag)
-            for copy, ms in ((nc.vector.tensor_copy, slice(0, split)), (nc.scalar.copy, slice(split, M))):
-                if ms.stop > ms.start:
-                    copy(
-                        out=z_grouped[b][:, ms, :].rearrange("p (g i) t -> p g t i", i=4),
-                        in_=z_slots[b][:, :, ms].rearrange("p t (g i) -> p g t i", i=4),
-                    )
-
-        def weave_z_on_pool(b, tag=None):
-            z_grouped[b] = sbuf(f"z_grouped{b}", [M, PACK], BF16, tag=tag)
-            nc.gpsimd.tensor_copy(out=z_grouped[b][:], in_=z_slots[b][:].rearrange("p t m -> p m t"))
+        z_c = [kept(f"z_c{b}", [M], U32) for b in range(HP)]
+        z_s = [kept(f"z_s{b}", [M], U8) for b in range(HP)]
 
         def quantise_z(b):
-            nc.vector.quantize_mx(out=z_c[b][:].bitcast(FP8X4), scales=z_s[b][:], in_=z_grouped[b][:].rearrange("p m t -> p (m t)"))
+            nc.vector.quantize_mx(out=z_c[b][:].bitcast(FP8X4), scales=z_s[b][:], in_=z_woven[b][:].rearrange("p m t -> p (m t)"))
 
-        y = {}
-
-        def second_product():
-            for j in range(TILES):
-                y[j] = psum.tile([P, BANK], F32, name=f"y{j}", tag="acc")
-                b, n = divmod(j, PACK)
-                for a in range(HP):
-                    nc.tensor.matmul_mx(
-                        out=y[j][:],
-                        lhsT=w2_w[b][:, a, 2 * n * P : 2 * (n + 1) * P].bitcast(FP4X4),
-                        lhsT_scale=w2_s[b][:, a, n * P : (n + 1) * P],
-                        rhs=z_c[a][:].bitcast(FP8X4),
-                        rhs_scale=z_s[a][:],
-                        start=(a == 0),
-                        stop=(a == HP - 1),
-                    )
-
-        out_rows = out.rearrange("(b p t) m -> p b t m", b=HP, t=PACK)
-
-        def store(j, gated, ms=slice(0, M)):
-            nc.sync.dma_start(out=out_rows[:, j // PACK, j % PACK, ms], in_=gated)
-
-        def finish(on_pool):
-            gates = {}
-            for j in range(TILES):
-                if j < on_pool:
-                    gates[j] = placed.tile([P, M], F32, name=f"gate{j}", offset=j * GATE_BYTES, align_bytes=64)
-                else:
-                    gates[j] = sbuf(f"gate{j}", [M], F32, tag=f"ge{j}")
-                nc.scalar.activation(out=gates[j][:], in_=y[j][:], func=ACT.Sigmoid)
-            for j in range(on_pool):
-                nc.gpsimd.tensor_tensor(out=citing[j], in0=gates[j][:], in1=citing[j], op=MULT)
-                store(j, citing[j])
-            gated = placed.tile([P, TILES - on_pool, M], F32, name="gated", offset=(on_pool - 1) * GATE_BYTES, align_bytes=64)
-            for j in range(on_pool, TILES):
-                for ms in [slice(0, M)] if j < TILES - 1 else [slice(0, LAST_SPLIT), slice(LAST_SPLIT, M)]:
-                    nc.vector.tensor_tensor(out=gated[:, j - on_pool, ms], in0=gates[j][:, ms], in1=citing[j][:, ms], op=MULT)
-                    store(j, gated[:, j - on_pool, ms], ms)
-
-        V, A, G = nc.vector, nc.scalar, nc.gpsimd
         nc.vector.memset(tab_sc[:].bitcast(I32), 0)
-        load_tab(0)
+        load_tab(0, laid(upper, RAW // 2, "tab0", [T], I32))
         nc.sync.dma_start(offs_sb[:], offs)
-        load_w1(0, 0)
+        load_w1(0, 0, kept("w1_raw00", [PACK, HALF], F32))
         load_w2(0)
-        load_w1(0, 1, "tab2")
+        load_w1(0, 1, kept("w1_raw01", [PACK, HALF], F32, "tab2"))
         nc.sync.dma_start(pos1_sb[:], pos1)
         nc.sync.dma_start(pos2_sb[:], pos2)
-        load_gains(nc.sync)
-        load_tab_scales(G)
-        warm_up()
+        gains = kept("gains", [HP, PACK], F32)
+        nc.sync.dma_start(out=gains[:], in_=gain.rearrange("(b p t) -> p b t", b=HP, t=PACK))
+        for q in range(4):
+            nc.gpsimd.dma_start(
+                out=tab_sc[32 * q + 4 : 32 * q + 4 + 4 * KP, :].bitcast(I32),
+                in_=tab_scales[:, 4 * q : 4 * q + 4, :].bitcast(I32),
+            )
+        w2_s_raw = kept("w2_s_raw", [HP, H], U8)
+        nc.vector.memset(w2_s_raw[:].rearrange("p a n -> p (a n)").bitcast(I32), 0)
+        for q in range(4):
+            rows = w2_scales[:, 4 * q : 4 * q + 4, :]
+            nc.gpsimd.dma_start(out=w2_s_raw[32 * q : 32 * q + 4, :, :].bitcast(I32), in_=rows.rearrange("a r n -> r a n").bitcast(I32))
+
+        warm = kept("warm", [1], F32)
+        nc.gpsimd.memset(warm[:], 0.0)
+        nc.scalar.activation(out=warm[:], in_=warm[:], func=ACT.Gelu_apprx_tanh)
+
         gather_tab(0, 1)
-        load_tab(1)
-        round_w1(0, 0, 0)
+        load_tab(1, laid(upper, RAW // 2, "tab1", [T], I32))
+        round_w1(0, 0, nc.scalar.copy, kept("rounded00", [HALF * PACK], BF16))
         quantise_w1(0, 0)
-        load_w1(0, 2, "w1_raw00")
-        round_w1(0, 1, 0)
+        load_w1(0, 2, kept("w1_raw02", [PACK, HALF], F32, "w1_raw00"))
+        round_w1(0, 1, nc.scalar.copy, kept("rounded01", [HALF * PACK], BF16))
         quantise_w1(0, 1)
-        load_tab(2)
-        gather_tab_scales()
-        deal_w2_words(0, V)
-        load_w2_scales(nc.sync, "w2_raw0")
-        gather_tab(1, 1)
+        load_tab(2, kept("tab2", [T], I32))
+        nc.vector.tensor_copy(v_s[:], tab_sc[:].indirect(offs_sb[:]))
+        w2_w[0] = kept("w2_w0", [HP, 2 * HALF], U8)
+        nc.vector.tensor_copy(
+            out=w2_w[0][:].bitcast(U16).rearrange("p a (t m) -> p a t m", t=PACK),
+            in_=w2_raw[0][:].bitcast(U16).rearrange("p a (m t) -> p a t m", t=PACK),
+        )
+        gather_tab(1, 1, "tab_sc")
         for b in range(HP):
-            deal_w2_scales(b, V)
+            w2_s[b] = kept(f"w2_s{b}", [HP, HALF], U8)
+            nc.vector.tensor_copy(
+                out=w2_s[b][:].rearrange("p a (t m) -> p a t m", t=PACK),
+                in_=w2_s_raw[:, :, b * HALF : (b + 1) * HALF].rearrange("p a (m t) -> p a t m", t=PACK),
+            )
         for a in range(KP):
-            load_w1(1, a)
-        round_w1(0, 2, 0, "grouped01")
+            load_w1(1, a, laid(upper, a * RAW, f"w1_raw1{a}", [PACK, HALF], F32))
+        round_w1(0, 2, nc.scalar.copy, kept("rounded02", [HALF * PACK], BF16, "rounded01"))
         quantise_w1(0, 2)
         gather_tab(2, 2)
-        lower = [(0, 0), (1, 0), (0, 1), (1, 1), (2, 0), (2, 1), (3, 0), (3, 1)]
-        first_product(lower, range(KP))
-        empty(lower)
-        load_w2(1, "grouped01")
-        splits = [128, 0, 96]
-        round_w1(1, 0, splits[0])
-        gather_cited(0, at=0)
+        lower_banks = [(0, 0), (1, 0), (0, 1), (1, 1), (2, 0), (2, 1), (3, 0), (3, 1)]
+        upper_banks = [(j, s) for j in range(PACK, TILES) for s in range(S // BANK)]
+        first_product(lower_banks, range(KP))
+        empty(lower_banks)
+        load_w2(1, "rounded01")
+
+        round_w1(1, 0, nc.vector.tensor_copy, kept("rounded10", [HALF * PACK], BF16))
+        gather_cited(0, laid(upper, 0, "cited0", [M], F32)[:])
         quantise_w1(1, 0)
-        for j in range(1, 3):
-            gather_cited(j, at=j * GATE_BYTES)
-        round_w1(1, 1, splits[1], None)
-        round_w1(1, 2, splits[2], 8192)
-        quantise_w1(1, 1, at=2 * RAW_BYTES + 3 * GATE_BYTES)
-        quantise_w1(1, 2, 2)
-        upper = [(j, s) for j in range(PACK, TILES) for s in range(2)]
-        first_product(upper, [0])
-        for bank in upper:
+        for j in (1, 2):
+            gather_cited(j, laid(upper, j * ROW, f"cited{j}", [M], F32)[:])
+        round_w1(1, 1, nc.scalar.copy, kept("rounded11", [HALF * PACK], BF16))
+        round_w1(1, 2, nc.vector.tensor_copy, laid(turn, ROUNDED_AT, "rounded12", [HALF * PACK], BF16))
+        quantise_w1(1, 1, codes=laid(upper, 2 * RAW + 3 * ROW, "w1_c11", [HALF], U32))
+        quantise_w1(1, 2, pieces=2)
+        first_product(upper_banks, [0])
+        for bank in upper_banks:
             first_product([bank], [1, 2])
-        held = sbuf("held", [3, M], F32, tag=8192 + 64 - 6144)
-        gather_cited(3, held[:, 0, :])
-        z_slots[0] = sbuf("z_slots0", [PACK, M], BF16, tag=12288 - 64)
-        lower_gain = [G, G, G, A]
-        for j in range(2):
-            gelu(j, 2 * RAW_BYTES + j * GATE_BYTES)
-            apply_gain(j, lower_gain[j])
-        deal_w2_words(1, G, 8192 + 64)
-        empty(upper[:2])
-        for j in range(2, PACK):
-            gelu(j, 2 * RAW_BYTES + j * GATE_BYTES if j == 2 else None)
-            apply_gain(j, lower_gain[j])
-        empty(upper[2:])
+
+        fillers = laid(turn, ROUNDED_AT + ROW // 2 - 3 * ROW, "fillers", [3, M], F32)
+        gather_cited(3, fillers[:, 0, :])
+        z_slots[0] = laid(turn, ROUNDED_AT + 3 * ROW // 2, "z_slots0", [PACK, M], BF16)
+        for j in range(3):
+            gelu(j, laid(upper, RAW + j * ROW, f"gelu{j}", [M], F32))
+        apply_gain(0, nc.scalar)
+        apply_gain(1, nc.gpsimd)
+        w2_w[1] = laid(turn, ROUNDED_AT + ROW // 2, "w2_w1", [HP, 2 * HALF], U8)
+        for a in range(HP):
+            nc.gpsimd.tensor_copy(
+                out=w2_w[1][:, a, :].rearrange("p (t m e) -> p t m e", t=PACK, e=2),
+                in_=w2_raw[1][:, a, :].rearrange("p (m t e) -> p t m e", t=PACK, e=2),
+            )
+        apply_gain(2, nc.gpsimd)
+        empty(upper_banks[:4])
+        gelu(3, kept("gelu3", [M], F32))
+        apply_gain(3, nc.gpsimd)
+        empty(upper_banks[4:])
         for j in range(PACK, TILES):
-            gather_cited(j)
+            gather_cited(j, kept(f"cited{j}", [M], F32)[:])
         for j in range(PACK, TILES):
-            gelu(j)
+            gelu(j, kept(f"gelu{j}", [M], F32))
         for j in range(2):
-            citing[j] = held[:, 1 + j, :]
-            nc.vector.tensor_copy(citing[j], h[j][:].indirect(pos2_sb[:]))
-        weave_z_on_pool(0)
+            gather_citing(j, fillers[:, 1 + j, :])
+        z_woven[0] = kept("z_woven0", [M, PACK], BF16)
+        nc.gpsimd.tensor_copy(out=z_woven[0][:], in_=z_slots[0][:].rearrange("p t m -> p m t"))
         quantise_z(0)
-        gather_citing([2], 12288)
-        z_slots[1] = sbuf("z_slots1", [PACK, M], BF16)
-        for j in range(PACK, TILES):
-            apply_gain(j, [V, V, A, A][j - PACK])
-        weave_z_shared(1, 336)
+        gather_citing(2, laid(turn, ROUNDED_AT + 2 * ROW, "citing2", [M], F32)[:])
+
+        z_slots[1] = kept("z_slots1", [PACK, M], BF16)
+        for j, engine in zip(range(PACK, TILES), (nc.vector, nc.vector, nc.scalar, nc.scalar)):
+            apply_gain(j, engine)
+        z_woven[1] = kept("z_woven1", [M, PACK], BF16)
+        for copy, ms in ((nc.vector.tensor_copy, slice(0, WEAVE_SPLIT)), (nc.scalar.copy, slice(WEAVE_SPLIT, M))):
+            copy(
+                out=z_woven[1][:, ms, :].rearrange("p (g i) t -> p g t i", i=4),
+                in_=z_slots[1][:, :, ms].rearrange("p t (g i) -> p g t i", i=4),
+            )
         quantise_z(1)
-        second_product()
-        gather_citing([3, 4, 5, 6, 7], "z_slots1")
-        finish(3)
+
+        y = []
+        for j in range(TILES):
+            y.append(psum.tile([P, BANK], F32, name=f"y{j}", tag="acc"))
+            b, t = divmod(j, PACK)
+            for a in range(HP):
+                nc.tensor.matmul_mx(
+                    out=y[j][:],
+                    lhsT=w2_w[b][:, a, 2 * t * P : 2 * (t + 1) * P].bitcast(FP4X4),
+                    lhsT_scale=w2_s[b][:, a, t * P : (t + 1) * P],
+                    rhs=z_c[a][:].bitcast(FP8X4),
+                    rhs_scale=z_s[a][:],
+                    start=(a == 0),
+                    stop=(a == HP - 1),
+                )
+
+        late = kept("late", [TILES - ON_GPSIMD, M], F32, "z_slots1")
+        for j in range(ON_GPSIMD, TILES):
+            gather_citing(j, late[:, j - ON_GPSIMD, :])
+        out_rows = out.rearrange("(b p t) m -> p b t m", b=HP, t=PACK)
+        gates = []
+        for j in range(TILES):
+            gates.append(laid(upper, j * ROW, f"gate{j}", [M], F32) if j < ON_GPSIMD else kept(f"gate{j}", [M], F32, f"gelu{j}"))
+            nc.scalar.activation(out=gates[j][:], in_=y[j][:], func=ACT.Sigmoid)
+        for j in range(ON_GPSIMD):
+            nc.gpsimd.tensor_tensor(out=citing[j], in0=gates[j][:], in1=citing[j], op=MULT)
+            nc.sync.dma_start(out=out_rows[:, 0, j, :], in_=citing[j])
+        gated = laid(upper, (ON_GPSIMD - 1) * ROW, "gated", [TILES - ON_GPSIMD, M], F32)
+        for j in range(ON_GPSIMD, TILES):
+            for ms in [slice(0, M)] if j < TILES - 1 else [slice(0, M // 2), slice(M // 2, M)]:
+                nc.vector.tensor_tensor(out=gated[:, j - ON_GPSIMD, ms], in0=gates[j][:, ms], in1=citing[j][:, ms], op=MULT)
+                nc.sync.dma_start(out=out_rows[:, j // PACK, j % PACK, ms], in_=gated[:, j - ON_GPSIMD, ms])

@@ -15,7 +15,6 @@ FP8X4 = mybir.dt.float8_e4m3fn_x4
 FP4X4 = mybir.dt.float4_e2m1fn_x4
 ACT = mybir.ActivationFunctionType
 MULT = mybir.AluOpType.mult
-ADD = mybir.AluOpType.add
 
 P = 128
 PACK = 4
@@ -26,7 +25,7 @@ TILES = H // P
 BANK = 512
 RAW = PACK * HALF * 4
 ROW = M * 4
-ROUNDED_AT = 3 * ROW
+ROUNDED_AT = ROW
 WEAVE_SPLIT = 336
 ON_GPSIMD = 3
 
@@ -80,8 +79,8 @@ def tile_list_citation_chain_gate_kernel(tc, tab_words, tab_scales, offs, pos1, 
                 in_=w1_raw[b, a][:].rearrange("p j (m t) -> p m j t", t=PACK),
             )
 
-        def quantise_w1(b, a, pieces=1, codes=None):
-            w1_c[b, a] = codes or kept(f"w1_c{b}{a}", [HALF], U32)
+        def quantise_w1(b, a, pieces=1):
+            w1_c[b, a] = kept(f"w1_c{b}{a}", [HALF], U32)
             w1_s[b, a] = kept(f"w1_s{b}{a}", [HALF], U8)
             width = HALF // pieces
             for n0 in range(0, HALF, width):
@@ -131,7 +130,7 @@ def tile_list_citation_chain_gate_kernel(tc, tab_words, tab_scales, offs, pos1, 
             if engine is nc.scalar:
                 nc.scalar.activation(out=dst, in_=gelus[j][:], func=ACT.Copy, scale=factor)
             else:
-                engine.tensor_scalar(out=dst, in0=gelus[j][:], scalar1=factor, scalar2=0.0, op0=MULT, op1=ADD)
+                engine.tensor_scalar(out=dst, in0=gelus[j][:], scalar1=factor, scalar2=None, op0=MULT)
 
         z_c = [kept(f"z_c{b}", [M], U32) for b in range(HP)]
         z_s = [kept(f"z_s{b}", [M], U8) for b in range(HP)]
@@ -199,44 +198,40 @@ def tile_list_citation_chain_gate_kernel(tc, tab_words, tab_scales, offs, pos1, 
         round_w1(1, 0, nc.vector.tensor_copy, kept("rounded10", [HALF * PACK], BF16))
         gather_cited(0, laid(upper, 0, "cited0", [M], F32)[:])
         quantise_w1(1, 0)
-        for j in (1, 2):
+        for j in range(1, PACK):
             gather_cited(j, laid(upper, j * ROW, f"cited{j}", [M], F32)[:])
-        round_w1(1, 1, nc.scalar.copy, kept("rounded11", [HALF * PACK], BF16))
+        round_w1(1, 1, nc.scalar.copy, laid(turn, ROUNDED_AT, "rounded11", [HALF * PACK], BF16))
+        quantise_w1(1, 1)
         round_w1(1, 2, nc.vector.tensor_copy, laid(turn, ROUNDED_AT, "rounded12", [HALF * PACK], BF16))
-        quantise_w1(1, 1, codes=laid(upper, 2 * RAW + 3 * ROW, "w1_c11", [HALF], U32))
         quantise_w1(1, 2, pieces=2)
         first_product(upper_banks, [0])
         for bank in upper_banks:
             first_product([bank], [1, 2])
 
-        fillers = laid(turn, ROUNDED_AT + ROW // 2 - 3 * ROW, "fillers", [3, M], F32)
-        gather_cited(3, fillers[:, 0, :])
-        z_slots[0] = laid(turn, ROUNDED_AT + 3 * ROW // 2, "z_slots0", [PACK, M], BF16)
-        for j in range(3):
+        fillers = laid(turn, ROUNDED_AT - ROW, "fillers", [2, M], F32)
+        z_slots[0] = kept("z_slots0", [PACK, M], BF16)
+        for j in range(PACK):
             gelu(j, laid(upper, RAW + j * ROW, f"gelu{j}", [M], F32))
-        apply_gain(0, nc.scalar)
-        apply_gain(1, nc.gpsimd)
-        w2_w[1] = laid(turn, ROUNDED_AT + ROW // 2, "w2_w1", [HP, 2 * HALF], U8)
+        empty(upper_banks[:2])
+        for j, engine in enumerate((nc.scalar, nc.scalar, nc.vector, nc.vector)):
+            apply_gain(j, engine)
+        w2_w[1] = laid(turn, ROUNDED_AT + ROW, "w2_w1", [HP, 2 * HALF], U8)
         for a in range(HP):
             nc.gpsimd.tensor_copy(
                 out=w2_w[1][:, a, :].rearrange("p (t m e) -> p t m e", t=PACK, e=2),
                 in_=w2_raw[1][:, a, :].rearrange("p (m t e) -> p t m e", t=PACK, e=2),
             )
-        apply_gain(2, nc.gpsimd)
-        empty(upper_banks[:4])
-        gelu(3, kept("gelu3", [M], F32))
-        apply_gain(3, nc.gpsimd)
-        empty(upper_banks[4:])
+        empty(upper_banks[2:])
         for j in range(PACK, TILES):
             gather_cited(j, kept(f"cited{j}", [M], F32)[:])
         for j in range(PACK, TILES):
             gelu(j, kept(f"gelu{j}", [M], F32))
         for j in range(2):
-            gather_citing(j, fillers[:, 1 + j, :])
+            gather_citing(j, fillers[:, j, :])
         z_woven[0] = kept("z_woven0", [M, PACK], BF16)
         nc.gpsimd.tensor_copy(out=z_woven[0][:], in_=z_slots[0][:].rearrange("p t m -> p m t"))
         quantise_z(0)
-        gather_citing(2, laid(turn, ROUNDED_AT + 2 * ROW, "citing2", [M], F32)[:])
+        gather_citing(2, kept("citing2", [M], F32, "z_slots0")[:])
 
         z_slots[1] = kept("z_slots1", [PACK, M], BF16)
         for j, engine in zip(range(PACK, TILES), (nc.vector, nc.vector, nc.scalar, nc.scalar)):

@@ -15,6 +15,7 @@ FP8X4 = mybir.dt.float8_e4m3fn_x4
 FP4X4 = mybir.dt.float4_e2m1fn_x4
 ACT = mybir.ActivationFunctionType
 MULT = mybir.AluOpType.mult
+ADD = mybir.AluOpType.add
 
 P = 128
 PACK = 4
@@ -23,43 +24,40 @@ KP = K // HALF
 HP = H // HALF
 TILES = H // P
 BANK = 512
-RAW = PACK * HALF * 4
-ROW = M * 4
-ROUNDED_AT = ROW
-WEAVE_SPLIT = 336
-ON_GPSIMD = 3
+KIB = 1024
+ON_GPSIMD = 5
+LEAD = 5
 
 
 def tile_list_citation_chain_gate_kernel(tc, tab_words, tab_scales, offs, pos1, pos2, w1, gain, w2_words, w2_scales, out):
     nc = tc.nc
     with ExitStack() as ctx:
         keep = ctx.enter_context(tc.tile_pool(name="keep", bufs=1))
-        upper = ctx.enter_context(tc.tile_pool(name="upper", bufs=1))
-        turn = ctx.enter_context(tc.tile_pool(name="turn", bufs=1))
+        arena = ctx.enter_context(tc.tile_pool(name="arena", bufs=1))
         psum = ctx.enter_context(tc.psum_pool(name="psum", bufs=8))
 
         def kept(name, shape, dtype, tag=None):
             return keep.tile([P] + shape, dtype, name=name, tag=tag or name, align_bytes=64)
 
-        def laid(pool, at, name, shape, dtype):
-            return pool.tile([P] + shape, dtype, name=name, offset=at, align_bytes=64)
+        def laid(kib, name, shape, dtype):
+            return arena.tile([P] + shape, dtype, name=name, offset=kib * KIB, align_bytes=64)
 
         offs_sb = kept("offs_sb", [S // 16], U16)
         pos1_sb = kept("pos1_sb", [M // 16], U16)
         pos2_sb = kept("pos2_sb", [M // 16], U16)
         tab_sc = kept("tab_sc", [T], U8)
         v_s = kept("v_s", [S], U8)
-        tab, v_w, w1_raw, rounded, w1_c, w1_s, w2_raw, w2_w, w2_s = {}, {}, {}, {}, {}, {}, {}, {}, {}
-        acc, cited, citing, gelus, z_slots, z_woven = {}, {}, {}, {}, {}, {}
+        tab, v_w, w1_c, w1_s, w2_raw, w2_w, w2_s = {}, {}, {}, {}, {}, {}, {}
+        acc, cited, citing, z_c = {}, {}, {}, {}
 
         def load_tab(a, tile):
             tab[a] = tile
             nc.sync.dma_start(out=tile[:], in_=tab_words[a].rearrange("p t i -> p (t i)").bitcast(I32))
 
-        def load_w1(b, a, tile):
-            w1_raw[b, a] = tile
-            rows = w1[a * HALF : (a + 1) * HALF, b * HALF : (b + 1) * HALF]
+        def load_w1(a, c0, width, tile):
+            rows = w1[a * HALF : (a + 1) * HALF, c0 : c0 + width]
             nc.sync.dma_start(out=tile[:], in_=rows.rearrange("(p j) n -> p j n", j=PACK))
+            return tile
 
         def load_w2(b, tag=None):
             w2_raw[b] = kept(f"w2_raw{b}", [HP, 2 * HALF], U8, tag)
@@ -72,14 +70,16 @@ def tile_list_citation_chain_gate_kernel(tc, tab_words, tab_scales, offs, pos1, 
             for s0 in range(0, S, step):
                 nc.vector.tensor_copy(v_w[a][:, s0 : s0 + step], tab[a][:].bitcast(U32).indirect(offs_sb[:, s0 // 16 : (s0 + step) // 16]))
 
-        def round_w1(b, a, copy, tile):
-            rounded[b, a] = tile
+        def round_w1(copy, tile, raw, ms=slice(0, P)):
             copy(
-                out=tile[:].rearrange("p (t m j) -> p m j t", t=PACK, j=PACK),
-                in_=w1_raw[b, a][:].rearrange("p j (m t) -> p m j t", t=PACK),
+                out=tile[:].rearrange("p (t m j) -> p m j t", t=PACK, j=PACK)[:, ms],
+                in_=raw[:].rearrange("p j (m t) -> p m j t", t=PACK),
             )
 
-        def quantise_w1(b, a, pieces=1):
+        def gpsimd_copy(out, in_):
+            nc.gpsimd.tensor_scalar(out=out.rearrange("p m j t -> p m t j"), in0=in_.rearrange("p m j t -> p m t j"), scalar1=1.0, scalar2=0.0, op0=MULT, op1=ADD)
+
+        def quantise_w1(b, a, tile, pieces=1):
             w1_c[b, a] = kept(f"w1_c{b}{a}", [HALF], U32)
             w1_s[b, a] = kept(f"w1_s{b}{a}", [HALF], U8)
             width = HALF // pieces
@@ -87,26 +87,25 @@ def tile_list_citation_chain_gate_kernel(tc, tab_words, tab_scales, offs, pos1, 
                 nc.vector.quantize_mx(
                     out=w1_c[b, a][:, n0 : n0 + width].bitcast(FP8X4),
                     scales=w1_s[b, a][:, n0 : n0 + width],
-                    in_=rounded[b, a][:, PACK * n0 : PACK * (n0 + width)],
+                    in_=tile[:, PACK * n0 : PACK * (n0 + width)],
                 )
 
         h = [kept(f"h{j}", [S], F32) for j in range(TILES)]
 
-        def first_product(banks, passes):
-            for a in passes:
-                for j, s in banks:
-                    if a == 0:
-                        acc[j, s] = psum.tile([P, BANK], F32, name=f"acc{j}", tag="acc")
-                    b, t = divmod(j, PACK)
-                    nc.tensor.matmul_mx(
-                        out=acc[j, s][:],
-                        lhsT=w1_c[b, a][:, t * P : (t + 1) * P].bitcast(FP8X4),
-                        lhsT_scale=w1_s[b, a][:, t * P : (t + 1) * P],
-                        rhs=v_w[a][:, s * BANK : (s + 1) * BANK].bitcast(FP8X4),
-                        rhs_scale=v_s[4 + 4 * a :, s * BANK : (s + 1) * BANK],
-                        start=(a == 0),
-                        stop=(a == KP - 1),
-                    )
+        def first_product(bank, a):
+            j, s = bank
+            if a == 0:
+                acc[bank] = psum.tile([P, BANK], F32, name=f"acc{j}", tag="acc")
+            b, t = divmod(j, PACK)
+            nc.tensor.matmul_mx(
+                out=acc[bank][:],
+                lhsT=w1_c[b, a][:, t * P : (t + 1) * P].bitcast(FP8X4),
+                lhsT_scale=w1_s[b, a][:, t * P : (t + 1) * P],
+                rhs=v_w[a][:, s * BANK : (s + 1) * BANK].bitcast(FP8X4),
+                rhs_scale=v_s[4 + 4 * a :, s * BANK : (s + 1) * BANK],
+                start=(a == 0),
+                stop=(a == KP - 1),
+            )
 
         def empty(banks):
             for j, s in banks:
@@ -120,30 +119,29 @@ def tile_list_citation_chain_gate_kernel(tc, tab_words, tab_scales, offs, pos1, 
             citing[j] = into
             nc.vector.tensor_copy(into, h[j][:].indirect(pos2_sb[:]))
 
-        def gelu(j, tile):
-            gelus[j] = tile
-            nc.scalar.activation(out=tile[:], in_=cited[j], func=ACT.Gelu_apprx_tanh)
+        def gelu(dst, src):
+            nc.scalar.activation(out=dst, in_=src, func=ACT.Gelu_apprx_tanh)
 
-        def apply_gain(j, engine):
-            b, t = divmod(j, PACK)
-            dst, factor = z_slots[b][:, t, :], gains[:, b, t : t + 1]
-            if engine is nc.scalar:
-                nc.scalar.activation(out=dst, in_=gelus[j][:], func=ACT.Copy, scale=factor)
-            else:
-                engine.tensor_scalar(out=dst, in0=gelus[j][:], scalar1=factor, scalar2=None, op0=MULT)
+        def deal_w2(b, tile):
+            w2_w[b] = tile
+            nc.vector.tensor_copy(
+                out=tile[:].bitcast(U16).rearrange("p a (t m) -> p a t m", t=PACK),
+                in_=w2_raw[b][:].bitcast(U16).rearrange("p a (m t) -> p a t m", t=PACK),
+            )
 
-        z_c = [kept(f"z_c{b}", [M], U32) for b in range(HP)]
         z_s = [kept(f"z_s{b}", [M], U8) for b in range(HP)]
 
-        def quantise_z(b):
-            nc.vector.quantize_mx(out=z_c[b][:].bitcast(FP8X4), scales=z_s[b][:], in_=z_woven[b][:].rearrange("p m t -> p (m t)"))
-
         nc.vector.memset(tab_sc[:].bitcast(I32), 0)
-        load_tab(0, laid(upper, RAW // 2, "tab0", [T], I32))
+        w2_s_raw = kept("w2_s_raw", [HP, H], U8)
+        nc.vector.memset(w2_s_raw[:].rearrange("p a n -> p (a n)").bitcast(I32), 0)
+        load_tab(0, laid(0, "tab0", [T], I32))
         nc.sync.dma_start(offs_sb[:], offs)
-        load_w1(0, 0, kept("w1_raw00", [PACK, HALF], F32))
+        raw00 = load_w1(0, 0, HALF, laid(20, "raw00", [PACK, HALF], F32))
+        for q in range(4):
+            rows = w2_scales[:, 4 * q : 4 * q + 4, :]
+            nc.sync.dma_start(out=w2_s_raw[32 * q : 32 * q + 4, :, :].bitcast(I32), in_=rows.rearrange("a r n -> r a n").bitcast(I32))
+        raw01 = load_w1(1, 0, HALF, laid(40, "raw01", [PACK, HALF], F32))
         load_w2(0)
-        load_w1(0, 1, kept("w1_raw01", [PACK, HALF], F32, "tab2"))
         nc.sync.dma_start(pos1_sb[:], pos1)
         nc.sync.dma_start(pos2_sb[:], pos2)
         gains = kept("gains", [HP, PACK], F32)
@@ -153,102 +151,108 @@ def tile_list_citation_chain_gate_kernel(tc, tab_words, tab_scales, offs, pos1, 
                 out=tab_sc[32 * q + 4 : 32 * q + 4 + 4 * KP, :].bitcast(I32),
                 in_=tab_scales[:, 4 * q : 4 * q + 4, :].bitcast(I32),
             )
-        w2_s_raw = kept("w2_s_raw", [HP, H], U8)
-        nc.vector.memset(w2_s_raw[:].rearrange("p a n -> p (a n)").bitcast(I32), 0)
-        for q in range(4):
-            rows = w2_scales[:, 4 * q : 4 * q + 4, :]
-            nc.gpsimd.dma_start(out=w2_s_raw[32 * q : 32 * q + 4, :, :].bitcast(I32), in_=rows.rearrange("a r n -> r a n").bitcast(I32))
 
         warm = kept("warm", [1], F32)
         nc.gpsimd.memset(warm[:], 0.0)
         nc.scalar.activation(out=warm[:], in_=warm[:], func=ACT.Gelu_apprx_tanh)
 
         gather_tab(0, 1)
-        load_tab(1, laid(upper, RAW // 2, "tab1", [T], I32))
-        round_w1(0, 0, nc.scalar.copy, kept("rounded00", [HALF * PACK], BF16))
-        quantise_w1(0, 0)
-        load_w1(0, 2, kept("w1_raw02", [PACK, HALF], F32, "w1_raw00"))
-        round_w1(0, 1, nc.scalar.copy, kept("rounded01", [HALF * PACK], BF16))
-        quantise_w1(0, 1)
-        load_tab(2, kept("tab2", [T], I32))
+        load_tab(1, laid(0, "tab1", [T], I32))
+        rounded00 = kept("rounded00", [HALF * PACK], BF16)
+        round_w1(nc.scalar.copy, rounded00, raw00)
+        quantise_w1(0, 0, rounded00)
+        raw02 = load_w1(2, 0, HALF, laid(20, "raw02", [PACK, HALF], F32))
+        rounded01 = laid(52, "rounded01", [HALF * PACK], BF16)
+        round_w1(nc.scalar.copy, rounded01, raw01)
+        quantise_w1(0, 1, rounded01)
+        load_tab(2, laid(28, "tab2", [T], I32))
+        raw10 = load_w1(0, HALF, HALF, laid(44, "raw10", [PACK, HALF], F32))
+        raw11 = load_w1(1, HALF, HALF, laid(52, "raw11", [PACK, HALF], F32))
         nc.vector.tensor_copy(v_s[:], tab_sc[:].indirect(offs_sb[:]))
-        w2_w[0] = kept("w2_w0", [HP, 2 * HALF], U8)
-        nc.vector.tensor_copy(
-            out=w2_w[0][:].bitcast(U16).rearrange("p a (t m) -> p a t m", t=PACK),
-            in_=w2_raw[0][:].bitcast(U16).rearrange("p a (m t) -> p a t m", t=PACK),
-        )
-        gather_tab(1, 1, "tab_sc")
+        deal_w2(0, kept("w2_w0", [HP, 2 * HALF], U8))
         for b in range(HP):
             w2_s[b] = kept(f"w2_s{b}", [HP, HALF], U8)
             nc.vector.tensor_copy(
                 out=w2_s[b][:].rearrange("p a (t m) -> p a t m", t=PACK),
                 in_=w2_s_raw[:, :, b * HALF : (b + 1) * HALF].rearrange("p a (m t) -> p a t m", t=PACK),
             )
-        for a in range(KP):
-            load_w1(1, a, laid(upper, a * RAW, f"w1_raw1{a}", [PACK, HALF], F32))
-        round_w1(0, 2, nc.scalar.copy, kept("rounded02", [HALF * PACK], BF16, "rounded01"))
-        quantise_w1(0, 2)
+        gather_tab(1, 1, "tab_sc")
+        rounded02 = kept("rounded02", [HALF * PACK], BF16)
+        round_w1(nc.scalar.copy, rounded02, raw02)
+        quantise_w1(0, 2, rounded02)
+        raw12 = [load_w1(2, HALF + u * HALF // 2, HALF // 2, laid(20 + 4 * u, f"raw12{u}", [PACK, HALF // 2], F32)) for u in range(2)]
+        load_w2(1, "rounded02")
         gather_tab(2, 2)
         lower_banks = [(0, 0), (1, 0), (0, 1), (1, 1), (2, 0), (2, 1), (3, 0), (3, 1)]
         upper_banks = [(j, s) for j in range(PACK, TILES) for s in range(S // BANK)]
-        first_product(lower_banks, range(KP))
+        for a in range(KP):
+            for bank in lower_banks:
+                first_product(bank, a)
         empty(lower_banks)
-        load_w2(1, "rounded01")
 
-        round_w1(1, 0, nc.vector.tensor_copy, kept("rounded10", [HALF * PACK], BF16))
-        gather_cited(0, laid(upper, 0, "cited0", [M], F32)[:])
-        quantise_w1(1, 0)
-        for j in range(1, PACK):
-            gather_cited(j, laid(upper, j * ROW, f"cited{j}", [M], F32)[:])
-        round_w1(1, 1, nc.scalar.copy, laid(turn, ROUNDED_AT, "rounded11", [HALF * PACK], BF16))
-        quantise_w1(1, 1)
-        round_w1(1, 2, nc.vector.tensor_copy, laid(turn, ROUNDED_AT, "rounded12", [HALF * PACK], BF16))
-        quantise_w1(1, 2, pieces=2)
-        first_product(upper_banks, [0])
+        rounded10 = kept("rounded10", [HALF * PACK], BF16)
+        round_w1(nc.vector.tensor_copy, rounded10, raw10)
+        gather_cited(0, laid(44, "cited0", [M], F32)[:])
+        quantise_w1(1, 0, rounded10)
+        for j in range(1, PACK - 1):
+            gather_cited(j, laid(44 + 2 * j, f"cited{j}", [M], F32)[:])
         for bank in upper_banks:
-            first_product([bank], [1, 2])
+            first_product(bank, 0)
+        rounded11 = kept("rounded11", [HALF * PACK], BF16, "cited3")
+        round_w1(gpsimd_copy, rounded11, raw11)
+        quantise_w1(1, 1, rounded11)
+        gather_cited(3, kept("cited3", [M], F32)[:])
+        rounded12 = laid(60, "rounded12", [HALF * PACK], BF16)
+        round_w1(nc.scalar.copy, rounded12, raw12[0], slice(0, P // 2))
+        round_w1(gpsimd_copy, rounded12, raw12[1], slice(P // 2, P))
+        quantise_w1(1, 2, rounded12, pieces=2)
+        for bank in upper_banks[:LEAD]:
+            first_product(bank, 1)
+        for i, bank in enumerate(upper_banks):
+            first_product(bank, 2)
+            for ahead in upper_banks[i + LEAD : i + LEAD + 1]:
+                first_product(ahead, 1)
 
-        fillers = laid(turn, ROUNDED_AT - ROW, "fillers", [2, M], F32)
-        z_slots[0] = kept("z_slots0", [PACK, M], BF16)
-        for j in range(PACK):
-            gelu(j, laid(upper, RAW + j * ROW, f"gelu{j}", [M], F32))
-        empty(upper_banks[:2])
-        for j, engine in enumerate((nc.scalar, nc.scalar, nc.vector, nc.vector)):
-            apply_gain(j, engine)
-        w2_w[1] = laid(turn, ROUNDED_AT + ROW, "w2_w1", [HP, 2 * HALF], U8)
-        for a in range(HP):
-            nc.gpsimd.tensor_copy(
-                out=w2_w[1][:, a, :].rearrange("p (t m e) -> p t m e", t=PACK, e=2),
-                in_=w2_raw[1][:, a, :].rearrange("p (m t e) -> p t m e", t=PACK, e=2),
-            )
-        empty(upper_banks[2:])
+        gelu_lower = laid(16, "gelu_lower", [PACK, M], F32)
+        for t in range(PACK):
+            gelu(gelu_lower[:, t, :], cited[t])
+        gather_citing(0, laid(60, "citing0", [M], F32)[:])
+        z_slots = laid(62, "z_slots", [PACK, M], BF16)
+        for t in range(PACK):
+            nc.gpsimd.tensor_scalar(out=z_slots[:, t, :], in0=gelu_lower[:, t, :], scalar1=gains[:, 0, t : t + 1], scalar2=0.0, op0=MULT, op1=ADD)
+        z_lower = kept("z_lower", [M, PACK], BF16)
+        nc.gpsimd.tensor_scalar(out=z_lower[:], in0=z_slots[:].rearrange("p t m -> p m t"), scalar1=1.0, scalar2=0.0, op0=MULT, op1=ADD)
+        empty(upper_banks)
+        cited45 = laid(66, "cited45", [2, M], F32)
         for j in range(PACK, TILES):
-            gather_cited(j, kept(f"cited{j}", [M], F32)[:])
-        for j in range(PACK, TILES):
-            gelu(j, kept(f"gelu{j}", [M], F32))
-        for j in range(2):
-            gather_citing(j, fillers[:, j, :])
-        z_woven[0] = kept("z_woven0", [M, PACK], BF16)
-        nc.gpsimd.tensor_copy(out=z_woven[0][:], in_=z_slots[0][:].rearrange("p t m -> p m t"))
-        quantise_z(0)
-        gather_citing(2, kept("citing2", [M], F32, "z_slots0")[:])
+            gather_cited(j, cited45[:, j - PACK, :] if j < PACK + 2 else kept(f"cited{j}", [M], F32)[:])
+        gelu_upper = kept("gelu_upper", [PACK, M], F32)
+        gelu(gelu_upper[:, 0:2, :], cited45[:])
+        for j in range(PACK + 2, TILES):
+            gelu(gelu_upper[:, j - PACK, :], cited[j])
+        z_c[0] = laid(66, "z_c0", [M], U32)
+        nc.vector.quantize_mx(out=z_c[0][:].bitcast(FP8X4), scales=z_s[0][:], in_=z_lower[:].rearrange("p m t -> p (m t)"))
+        deal_w2(1, laid(68, "w2_w1", [HP, 2 * HALF], U8))
 
-        z_slots[1] = kept("z_slots1", [PACK, M], BF16)
-        for j, engine in zip(range(PACK, TILES), (nc.vector, nc.vector, nc.scalar, nc.scalar)):
-            apply_gain(j, engine)
-        z_woven[1] = kept("z_woven1", [M, PACK], BF16)
-        for copy, ms in ((nc.vector.tensor_copy, slice(0, WEAVE_SPLIT)), (nc.scalar.copy, slice(WEAVE_SPLIT, M))):
-            copy(
-                out=z_woven[1][:, ms, :].rearrange("p (g i) t -> p g t i", i=4),
-                in_=z_slots[1][:, :, ms].rearrange("p t (g i) -> p g t i", i=4),
+        z_upper = kept("z_upper", [M, PACK], BF16)
+        z_c[1] = kept("z_c1", [M], U32)
+        halves = (slice(0, M // 2), slice(M // 2, M))
+        for ms in halves:
+            nc.vector.tensor_tensor(
+                out=z_upper[:, ms, :].rearrange("p (g i) t -> p g t i", i=4),
+                in0=gelu_upper[:, :, ms].rearrange("p t (g i) -> p g t i", i=4),
+                in1=gains[:, 1, :].unsqueeze(1).unsqueeze(3).to_broadcast([P, M // 8, PACK, 4]),
+                op=MULT,
             )
-        quantise_z(1)
+        for ms in halves:
+            nc.vector.quantize_mx(out=z_c[1][:, ms].bitcast(FP8X4), scales=z_s[1][:, ms], in_=z_upper[:, ms, :].rearrange("p m t -> p (m t)"))
 
         y = []
-        for j in range(TILES):
-            y.append(psum.tile([P, BANK], F32, name=f"y{j}", tag="acc"))
-            b, t = divmod(j, PACK)
-            for a in range(HP):
+        for a in range(HP):
+            for j in range(TILES):
+                if a == 0:
+                    y.append(psum.tile([P, BANK], F32, name=f"y{j}", tag="acc"))
+                b, t = divmod(j, PACK)
                 nc.tensor.matmul_mx(
                     out=y[j][:],
                     lhsT=w2_w[b][:, a, 2 * t * P : 2 * (t + 1) * P].bitcast(FP4X4),
@@ -259,19 +263,19 @@ def tile_list_citation_chain_gate_kernel(tc, tab_words, tab_scales, offs, pos1, 
                     stop=(a == HP - 1),
                 )
 
-        late = kept("late", [TILES - ON_GPSIMD, M], F32, "z_slots1")
-        for j in range(ON_GPSIMD, TILES):
-            gather_citing(j, late[:, j - ON_GPSIMD, :])
+        late = kept("late", [TILES - 1, M], F32, "z_upper")
+        for j in range(1, TILES):
+            gather_citing(j, late[:, j - 1, :])
         out_rows = out.rearrange("(b p t) m -> p b t m", b=HP, t=PACK)
         gates = []
         for j in range(TILES):
-            gates.append(laid(upper, j * ROW, f"gate{j}", [M], F32) if j < ON_GPSIMD else kept(f"gate{j}", [M], F32, f"gelu{j}"))
+            gates.append(laid(28 + 2 * j, f"gate{j}", [M], F32) if j < ON_GPSIMD else kept(f"gate{j}", [M], F32))
             nc.scalar.activation(out=gates[j][:], in_=y[j][:], func=ACT.Sigmoid)
         for j in range(ON_GPSIMD):
             nc.gpsimd.tensor_tensor(out=citing[j], in0=gates[j][:], in1=citing[j], op=MULT)
-            nc.sync.dma_start(out=out_rows[:, 0, j, :], in_=citing[j])
-        gated = laid(upper, (ON_GPSIMD - 1) * ROW, "gated", [TILES - ON_GPSIMD, M], F32)
+            nc.sync.dma_start(out=out_rows[:, j // PACK, j % PACK, :], in_=citing[j])
+        gated = laid(28 + 2 * (ON_GPSIMD - 1), "gated", [TILES - ON_GPSIMD, M], F32)
         for j in range(ON_GPSIMD, TILES):
-            for ms in [slice(0, M)] if j < TILES - 1 else [slice(0, M // 2), slice(M // 2, M)]:
+            for ms in [slice(0, M)] if j < TILES - 1 else halves:
                 nc.vector.tensor_tensor(out=gated[:, j - ON_GPSIMD, ms], in0=gates[j][:, ms], in1=citing[j][:, ms], op=MULT)
                 nc.sync.dma_start(out=out_rows[:, j // PACK, j % PACK, ms], in_=gated[:, j - ON_GPSIMD, ms])

@@ -70,9 +70,9 @@ def tile_list_citation_chain_gate_kernel(tc, tab_words, tab_scales, offs, pos1, 
             for s0 in range(0, S, step):
                 nc.vector.tensor_copy(v_w[a][:, s0 : s0 + step], tab[a][:].bitcast(U32).indirect(offs_sb[:, s0 // 16 : (s0 + step) // 16]))
 
-        def round_w1(copy, tile, raw, ms=slice(0, P)):
+        def round_w1(copy, tile, raw):
             copy(
-                out=tile[:].rearrange("p (t m j) -> p m j t", t=PACK, j=PACK)[:, ms],
+                out=tile[:].rearrange("p (t m j) -> p m j t", t=PACK, j=PACK),
                 in_=raw[:].rearrange("p j (m t) -> p m j t", t=PACK),
             )
 
@@ -180,7 +180,7 @@ def tile_list_citation_chain_gate_kernel(tc, tab_words, tab_scales, offs, pos1, 
         rounded02 = kept("rounded02", [HALF * PACK], BF16)
         round_w1(nc.scalar.copy, rounded02, raw02)
         quantise_w1(0, 2, rounded02)
-        raw12 = [load_w1(2, HALF + u * HALF // 2, HALF // 2, laid(20 + 4 * u, f"raw12{u}", [PACK, HALF // 2], F32)) for u in range(2)]
+        raw12 = load_w1(2, HALF, HALF, laid(20, "raw12", [PACK, HALF], F32))
         load_w2(1, "rounded02")
         gather_tab(2, 2)
         lower_banks = [(0, 0), (1, 0), (0, 1), (1, 1), (2, 0), (2, 1), (3, 0), (3, 1)]
@@ -190,10 +190,10 @@ def tile_list_citation_chain_gate_kernel(tc, tab_words, tab_scales, offs, pos1, 
                 first_product(bank, a)
         empty(lower_banks)
 
-        rounded10 = kept("rounded10", [HALF * PACK], BF16)
+        rounded10 = kept("rounded10", [HALF * PACK], BF16, "cited3")
         round_w1(nc.vector.tensor_copy, rounded10, raw10)
-        gather_cited(0, laid(44, "cited0", [M], F32)[:])
         quantise_w1(1, 0, rounded10)
+        gather_cited(0, laid(44, "cited0", [M], F32)[:])
         for j in range(1, PACK - 1):
             gather_cited(j, laid(44 + 2 * j, f"cited{j}", [M], F32)[:])
         for bank in upper_banks:
@@ -203,8 +203,7 @@ def tile_list_citation_chain_gate_kernel(tc, tab_words, tab_scales, offs, pos1, 
         quantise_w1(1, 1, rounded11)
         gather_cited(3, kept("cited3", [M], F32)[:])
         rounded12 = laid(60, "rounded12", [HALF * PACK], BF16)
-        round_w1(nc.scalar.copy, rounded12, raw12[0], slice(0, P // 2))
-        round_w1(gpsimd_copy, rounded12, raw12[1], slice(P // 2, P))
+        round_w1(nc.scalar.copy, rounded12, raw12)
         quantise_w1(1, 2, rounded12, pieces=2)
         for bank in upper_banks[:LEAD]:
             first_product(bank, 1)

@@ -25,7 +25,7 @@ HP = H // HALF
 TILES = H // P
 BANK = 512
 KIB = 1024
-ON_GPSIMD = 5
+ON_GPSIMD = 4
 LEAD = 5
 
 
@@ -59,8 +59,8 @@ def tile_list_citation_chain_gate_kernel(tc, tab_words, tab_scales, offs, pos1, 
             nc.sync.dma_start(out=tile[:], in_=rows.rearrange("(p j) n -> p j n", j=PACK))
             return tile
 
-        def load_w2(b, tag=None):
-            w2_raw[b] = kept(f"w2_raw{b}", [HP, 2 * HALF], U8, tag)
+        def load_w2(b, tile):
+            w2_raw[b] = tile
             cols = w2_words[:, :, b * 2 * HALF : (b + 1) * 2 * HALF]
             nc.sync.dma_start(out=w2_raw[b][:].bitcast(I32), in_=cols.rearrange("a p n -> p a n").bitcast(I32))
 
@@ -70,25 +70,21 @@ def tile_list_citation_chain_gate_kernel(tc, tab_words, tab_scales, offs, pos1, 
             for s0 in range(0, S, step):
                 nc.vector.tensor_copy(v_w[a][:, s0 : s0 + step], tab[a][:].bitcast(U32).indirect(offs_sb[:, s0 // 16 : (s0 + step) // 16]))
 
-        def round_w1(copy, tile, raw):
+        def round_w1(copy, tile, raw, ts=slice(0, PACK), ms=slice(0, P)):
             copy(
-                out=tile[:].rearrange("p (t m j) -> p m j t", t=PACK, j=PACK),
-                in_=raw[:].rearrange("p j (m t) -> p m j t", t=PACK),
+                out=tile[:].rearrange("p (t m j) -> p m j t", m=P, j=PACK)[:, ms],
+                in_=raw[:].rearrange("p j (m t) -> p m j t", t=PACK)[:, ms, :, ts],
             )
 
         def gpsimd_copy(out, in_):
             nc.gpsimd.tensor_scalar(out=out.rearrange("p m j t -> p m t j"), in0=in_.rearrange("p m j t -> p m t j"), scalar1=1.0, scalar2=0.0, op0=MULT, op1=ADD)
 
-        def quantise_w1(b, a, tile, pieces=1):
-            w1_c[b, a] = kept(f"w1_c{b}{a}", [HALF], U32)
-            w1_s[b, a] = kept(f"w1_s{b}{a}", [HALF], U8)
-            width = HALF // pieces
-            for n0 in range(0, HALF, width):
-                nc.vector.quantize_mx(
-                    out=w1_c[b, a][:, n0 : n0 + width].bitcast(FP8X4),
-                    scales=w1_s[b, a][:, n0 : n0 + width],
-                    in_=tile[:, PACK * n0 : PACK * (n0 + width)],
-                )
+        def quantise_w1(b, a, tile, ts=slice(0, PACK)):
+            if ts.start == 0:
+                w1_c[b, a] = kept(f"w1_c{b}{a}", [HALF], U32)
+                w1_s[b, a] = kept(f"w1_s{b}{a}", [HALF], U8)
+            cols = slice(ts.start * P, ts.stop * P)
+            nc.vector.quantize_mx(out=w1_c[b, a][:, cols].bitcast(FP8X4), scales=w1_s[b, a][:, cols], in_=tile[:])
 
         h = [kept(f"h{j}", [S], F32) for j in range(TILES)]
 
@@ -124,7 +120,7 @@ def tile_list_citation_chain_gate_kernel(tc, tab_words, tab_scales, offs, pos1, 
 
         def deal_w2(b, tile):
             w2_w[b] = tile
-            nc.vector.tensor_copy(
+            nc.scalar.copy(
                 out=tile[:].bitcast(U16).rearrange("p a (t m) -> p a t m", t=PACK),
                 in_=w2_raw[b][:].bitcast(U16).rearrange("p a (m t) -> p a t m", t=PACK),
             )
@@ -141,11 +137,8 @@ def tile_list_citation_chain_gate_kernel(tc, tab_words, tab_scales, offs, pos1, 
             rows = w2_scales[:, 4 * q : 4 * q + 4, :]
             nc.sync.dma_start(out=w2_s_raw[32 * q : 32 * q + 4, :, :].bitcast(I32), in_=rows.rearrange("a r n -> r a n").bitcast(I32))
         raw01 = load_w1(1, 0, HALF, laid(40, "raw01", [PACK, HALF], F32))
-        load_w2(0)
         nc.sync.dma_start(pos1_sb[:], pos1)
         nc.sync.dma_start(pos2_sb[:], pos2)
-        gains = kept("gains", [HP, PACK], F32)
-        nc.sync.dma_start(out=gains[:], in_=gain.rearrange("(b p t) -> p b t", b=HP, t=PACK))
         for q in range(4):
             nc.gpsimd.dma_start(
                 out=tab_sc[32 * q + 4 : 32 * q + 4 + 4 * KP, :].bitcast(I32),
@@ -169,7 +162,6 @@ def tile_list_citation_chain_gate_kernel(tc, tab_words, tab_scales, offs, pos1, 
         raw10 = load_w1(0, HALF, HALF, laid(44, "raw10", [PACK, HALF], F32))
         raw11 = load_w1(1, HALF, HALF, laid(52, "raw11", [PACK, HALF], F32))
         nc.vector.tensor_copy(v_s[:], tab_sc[:].indirect(offs_sb[:]))
-        deal_w2(0, kept("w2_w0", [HP, 2 * HALF], U8))
         for b in range(HP):
             w2_s[b] = kept(f"w2_s{b}", [HP, HALF], U8)
             nc.vector.tensor_copy(
@@ -177,11 +169,14 @@ def tile_list_citation_chain_gate_kernel(tc, tab_words, tab_scales, offs, pos1, 
                 in_=w2_s_raw[:, :, b * HALF : (b + 1) * HALF].rearrange("p a (m t) -> p a t m", t=PACK),
             )
         gather_tab(1, 1, "tab_sc")
-        rounded02 = kept("rounded02", [HALF * PACK], BF16)
+        rounded02 = laid(90, "rounded02", [HALF * PACK], BF16)
         round_w1(nc.scalar.copy, rounded02, raw02)
         quantise_w1(0, 2, rounded02)
         raw12 = load_w1(2, HALF, HALF, laid(20, "raw12", [PACK, HALF], F32))
-        load_w2(1, "rounded02")
+        gains = laid(91, "gains", [HP, PACK], F32)
+        nc.sync.dma_start(out=gains[:], in_=gain.rearrange("(b p t) -> p b t", b=HP, t=PACK))
+        load_w2(0, laid(89, "w2_raw0", [HP, 2 * HALF], U8))
+        load_w2(1, laid(92, "w2_raw1", [HP, 2 * HALF], U8))
         gather_tab(2, 2)
         lower_banks = [(0, 0), (1, 0), (0, 1), (1, 1), (2, 0), (2, 1), (3, 0), (3, 1)]
         upper_banks = [(j, s) for j in range(PACK, TILES) for s in range(S // BANK)]
@@ -190,21 +185,26 @@ def tile_list_citation_chain_gate_kernel(tc, tab_words, tab_scales, offs, pos1, 
                 first_product(bank, a)
         empty(lower_banks)
 
-        rounded10 = kept("rounded10", [HALF * PACK], BF16, "cited3")
-        round_w1(nc.vector.tensor_copy, rounded10, raw10)
-        quantise_w1(1, 0, rounded10)
-        gather_cited(0, laid(44, "cited0", [M], F32)[:])
-        for j in range(1, PACK - 1):
+        rounded10 = [laid(72 + 2 * u, f"rounded10{u}", [HALF * 2], BF16) for u in range(2)]
+        for u in range(2):
+            round_w1(nc.vector.tensor_copy, rounded10[u], raw10, slice(2 * u, 2 * u + 2))
+        for u in range(2):
+            quantise_w1(1, 0, rounded10[u], slice(2 * u, 2 * u + 2))
+        for j in range(PACK - 1):
             gather_cited(j, laid(44 + 2 * j, f"cited{j}", [M], F32)[:])
         for bank in upper_banks:
             first_product(bank, 0)
-        rounded11 = kept("rounded11", [HALF * PACK], BF16, "cited3")
+        rounded11 = laid(72, "rounded11", [HALF * PACK], BF16)
         round_w1(gpsimd_copy, rounded11, raw11)
         quantise_w1(1, 1, rounded11)
-        gather_cited(3, kept("cited3", [M], F32)[:])
-        rounded12 = laid(60, "rounded12", [HALF * PACK], BF16)
-        round_w1(nc.scalar.copy, rounded12, raw12)
-        quantise_w1(1, 2, rounded12, pieces=2)
+        gather_cited(3, laid(52, "cited3", [M], F32)[:])
+        front = laid(60, "rounded12a", [HALF * 2], BF16)
+        round_w1(nc.scalar.copy, front, raw12, slice(0, 2))
+        back = laid(74, "rounded12b", [HALF * 2], BF16)
+        round_w1(nc.scalar.copy, back, raw12, slice(2, PACK), slice(0, P // 2))
+        round_w1(gpsimd_copy, back, raw12, slice(2, PACK), slice(P // 2, P))
+        quantise_w1(1, 2, front, slice(0, 2))
+        quantise_w1(1, 2, back, slice(2, PACK))
         for bank in upper_banks[:LEAD]:
             first_product(bank, 1)
         for i, bank in enumerate(upper_banks):
@@ -212,46 +212,49 @@ def tile_list_citation_chain_gate_kernel(tc, tab_words, tab_scales, offs, pos1, 
             for ahead in upper_banks[i + LEAD : i + LEAD + 1]:
                 first_product(ahead, 1)
 
-        gelu_lower = laid(16, "gelu_lower", [PACK, M], F32)
+        gelu_lower = laid(66, "gelu_lower", [PACK, M], F32)
         for t in range(PACK):
             gelu(gelu_lower[:, t, :], cited[t])
         gather_citing(0, laid(60, "citing0", [M], F32)[:])
-        z_slots = laid(62, "z_slots", [PACK, M], BF16)
+        z_slots = laid(75, "z_slots", [PACK, M], BF16)
         for t in range(PACK):
             nc.gpsimd.tensor_scalar(out=z_slots[:, t, :], in0=gelu_lower[:, t, :], scalar1=gains[:, 0, t : t + 1], scalar2=0.0, op0=MULT, op1=ADD)
         z_lower = kept("z_lower", [M, PACK], BF16)
         nc.gpsimd.tensor_scalar(out=z_lower[:], in0=z_slots[:].rearrange("p t m -> p m t"), scalar1=1.0, scalar2=0.0, op0=MULT, op1=ADD)
         empty(upper_banks)
-        cited45 = laid(66, "cited45", [2, M], F32)
+        cited45 = laid(80, "cited45", [2, M], F32)
         for j in range(PACK, TILES):
             gather_cited(j, cited45[:, j - PACK, :] if j < PACK + 2 else kept(f"cited{j}", [M], F32)[:])
         gelu_upper = kept("gelu_upper", [PACK, M], F32)
         gelu(gelu_upper[:, 0:2, :], cited45[:])
         for j in range(PACK + 2, TILES):
             gelu(gelu_upper[:, j - PACK, :], cited[j])
-        z_c[0] = laid(66, "z_c0", [M], U32)
+        deal_w2(0, kept("w2_w0", [HP, 2 * HALF], U8, "cited6"))
+        deal_w2(1, kept("w2_w1", [HP, 2 * HALF], U8, "cited7"))
+        z_c[0] = laid(80, "z_c0", [M], U32)
         nc.vector.quantize_mx(out=z_c[0][:].bitcast(FP8X4), scales=z_s[0][:], in_=z_lower[:].rearrange("p m t -> p (m t)"))
-        deal_w2(1, laid(68, "w2_w1", [HP, 2 * HALF], U8))
-
-        z_upper = kept("z_upper", [M, PACK], BF16)
-        z_c[1] = kept("z_c1", [M], U32)
         halves = (slice(0, M // 2), slice(M // 2, M))
-        for ms in halves:
+        early = laid(82, "early", [M // 2], F32)
+        nc.vector.tensor_copy(early[:], h[1][:].indirect(pos2_sb[:, 0 : M // 32]))
+
+        z_upper = [kept(f"z_upper{u}", [M // 2, PACK], BF16) for u in range(2)]
+        z_c[1] = kept("z_c1", [M], U32)
+        for u, ms in enumerate(halves):
             nc.vector.tensor_tensor(
-                out=z_upper[:, ms, :].rearrange("p (g i) t -> p g t i", i=4),
+                out=z_upper[u][:].rearrange("p (g i) t -> p g t i", i=4),
                 in0=gelu_upper[:, :, ms].rearrange("p t (g i) -> p g t i", i=4),
                 in1=gains[:, 1, :].unsqueeze(1).unsqueeze(3).to_broadcast([P, M // 8, PACK, 4]),
                 op=MULT,
             )
-        for ms in halves:
-            nc.vector.quantize_mx(out=z_c[1][:, ms].bitcast(FP8X4), scales=z_s[1][:, ms], in_=z_upper[:, ms, :].rearrange("p m t -> p (m t)"))
+        for u, ms in enumerate(halves):
+            nc.vector.quantize_mx(out=z_c[1][:, ms].bitcast(FP8X4), scales=z_s[1][:, ms], in_=z_upper[u][:].rearrange("p m t -> p (m t)"))
 
         y = []
-        for a in range(HP):
-            for j in range(TILES):
+        for b, a in ((b, a) for b in range(HP) for a in range(HP)):
+            for t in range(PACK):
+                j = PACK * b + t
                 if a == 0:
                     y.append(psum.tile([P, BANK], F32, name=f"y{j}", tag="acc"))
-                b, t = divmod(j, PACK)
                 nc.tensor.matmul_mx(
                     out=y[j][:],
                     lhsT=w2_w[b][:, a, 2 * t * P : 2 * (t + 1) * P].bitcast(FP4X4),
@@ -262,8 +265,9 @@ def tile_list_citation_chain_gate_kernel(tc, tab_words, tab_scales, offs, pos1, 
                     stop=(a == HP - 1),
                 )
 
-        late = kept("late", [TILES - 1, M], F32, "z_upper")
-        for j in range(1, TILES):
+        late = kept("late", [TILES - 1, M], F32, "z_upper0")
+        nc.vector.tensor_copy(late[:, 0, halves[1]], h[1][:].indirect(pos2_sb[:, M // 32 :]))
+        for j in range(2, TILES):
             gather_citing(j, late[:, j - 1, :])
         out_rows = out.rearrange("(b p t) m -> p b t m", b=HP, t=PACK)
         gates = []
@@ -271,8 +275,10 @@ def tile_list_citation_chain_gate_kernel(tc, tab_words, tab_scales, offs, pos1, 
             gates.append(laid(28 + 2 * j, f"gate{j}", [M], F32) if j < ON_GPSIMD else kept(f"gate{j}", [M], F32))
             nc.scalar.activation(out=gates[j][:], in_=y[j][:], func=ACT.Sigmoid)
         for j in range(ON_GPSIMD):
-            nc.gpsimd.tensor_tensor(out=citing[j], in0=gates[j][:], in1=citing[j], op=MULT)
-            nc.sync.dma_start(out=out_rows[:, j // PACK, j % PACK, :], in_=citing[j])
+            pieces = [(slice(0, M), citing[j])] if j != 1 else [(halves[0], early[:]), (halves[1], late[:, 0, halves[1]])]
+            for ms, values in pieces:
+                nc.gpsimd.tensor_tensor(out=values, in0=gates[j][:, ms], in1=values, op=MULT)
+                nc.sync.dma_start(out=out_rows[:, j // PACK, j % PACK, ms], in_=values)
         gated = laid(28 + 2 * (ON_GPSIMD - 1), "gated", [TILES - ON_GPSIMD, M], F32)
         for j in range(ON_GPSIMD, TILES):
             for ms in [slice(0, M)] if j < TILES - 1 else halves:

@@ -25,7 +25,7 @@ HP = H // HALF
 TILES = H // P
 BANK = 512
 KIB = 1024
-ON_GPSIMD = 4
+ON_GPSIMD = 5
 LEAD = 5
 
 
@@ -79,9 +79,9 @@ def tile_list_citation_chain_gate_kernel(tc, tab_words, tab_scales, offs, pos1, 
         def gpsimd_copy(out, in_):
             nc.gpsimd.tensor_scalar(out=out.rearrange("p m j t -> p m t j"), in0=in_.rearrange("p m j t -> p m t j"), scalar1=1.0, scalar2=0.0, op0=MULT, op1=ADD)
 
-        def quantise_w1(b, a, tile, ts=slice(0, PACK)):
+        def quantise_w1(b, a, tile, ts=slice(0, PACK), codes=None):
             if ts.start == 0:
-                w1_c[b, a] = kept(f"w1_c{b}{a}", [HALF], U32)
+                w1_c[b, a] = kept(f"w1_c{b}{a}", [HALF], U32) if codes is None else codes
                 w1_s[b, a] = kept(f"w1_s{b}{a}", [HALF], U8)
             cols = slice(ts.start * P, ts.stop * P)
             nc.vector.quantize_mx(out=w1_c[b, a][:, cols].bitcast(FP8X4), scales=w1_s[b, a][:, cols], in_=tile[:])
@@ -120,7 +120,7 @@ def tile_list_citation_chain_gate_kernel(tc, tab_words, tab_scales, offs, pos1, 
 
         def deal_w2(b, tile):
             w2_w[b] = tile
-            nc.scalar.copy(
+            nc.vector.tensor_copy(
                 out=tile[:].bitcast(U16).rearrange("p a (t m) -> p a t m", t=PACK),
                 in_=w2_raw[b][:].bitcast(U16).rearrange("p a (m t) -> p a t m", t=PACK),
             )
@@ -133,9 +133,7 @@ def tile_list_citation_chain_gate_kernel(tc, tab_words, tab_scales, offs, pos1, 
         load_tab(0, laid(0, "tab0", [T], I32))
         nc.sync.dma_start(offs_sb[:], offs)
         raw00 = load_w1(0, 0, HALF, laid(20, "raw00", [PACK, HALF], F32))
-        for q in range(4):
-            rows = w2_scales[:, 4 * q : 4 * q + 4, :]
-            nc.sync.dma_start(out=w2_s_raw[32 * q : 32 * q + 4, :, :].bitcast(I32), in_=rows.rearrange("a r n -> r a n").bitcast(I32))
+        load_w2(0, kept("w2_raw0", [HP, 2 * HALF], U8))
         raw01 = load_w1(1, 0, HALF, laid(40, "raw01", [PACK, HALF], F32))
         nc.sync.dma_start(pos1_sb[:], pos1)
         nc.sync.dma_start(pos2_sb[:], pos2)
@@ -144,6 +142,9 @@ def tile_list_citation_chain_gate_kernel(tc, tab_words, tab_scales, offs, pos1, 
                 out=tab_sc[32 * q + 4 : 32 * q + 4 + 4 * KP, :].bitcast(I32),
                 in_=tab_scales[:, 4 * q : 4 * q + 4, :].bitcast(I32),
             )
+        for q in range(4):
+            rows = w2_scales[:, 4 * q : 4 * q + 4, :]
+            nc.gpsimd.dma_start(out=w2_s_raw[32 * q : 32 * q + 4, :, :].bitcast(I32), in_=rows.rearrange("a r n -> r a n").bitcast(I32))
 
         warm = kept("warm", [1], F32)
         nc.gpsimd.memset(warm[:], 0.0)
@@ -162,6 +163,7 @@ def tile_list_citation_chain_gate_kernel(tc, tab_words, tab_scales, offs, pos1, 
         raw10 = load_w1(0, HALF, HALF, laid(44, "raw10", [PACK, HALF], F32))
         raw11 = load_w1(1, HALF, HALF, laid(52, "raw11", [PACK, HALF], F32))
         nc.vector.tensor_copy(v_s[:], tab_sc[:].indirect(offs_sb[:]))
+        deal_w2(0, kept("w2_w0", [HP, 2 * HALF], U8))
         for b in range(HP):
             w2_s[b] = kept(f"w2_s{b}", [HP, HALF], U8)
             nc.vector.tensor_copy(
@@ -171,11 +173,10 @@ def tile_list_citation_chain_gate_kernel(tc, tab_words, tab_scales, offs, pos1, 
         gather_tab(1, 1, "tab_sc")
         rounded02 = laid(90, "rounded02", [HALF * PACK], BF16)
         round_w1(nc.scalar.copy, rounded02, raw02)
-        quantise_w1(0, 2, rounded02)
+        quantise_w1(0, 2, rounded02, codes=laid(0, "w1_c02", [HALF], U32))
         raw12 = load_w1(2, HALF, HALF, laid(20, "raw12", [PACK, HALF], F32))
         gains = laid(91, "gains", [HP, PACK], F32)
         nc.sync.dma_start(out=gains[:], in_=gain.rearrange("(b p t) -> p b t", b=HP, t=PACK))
-        load_w2(0, laid(89, "w2_raw0", [HP, 2 * HALF], U8))
         load_w2(1, laid(92, "w2_raw1", [HP, 2 * HALF], U8))
         gather_tab(2, 2)
         lower_banks = [(0, 0), (1, 0), (0, 1), (1, 1), (2, 0), (2, 1), (3, 0), (3, 1)]
@@ -229,13 +230,10 @@ def tile_list_citation_chain_gate_kernel(tc, tab_words, tab_scales, offs, pos1, 
         gelu(gelu_upper[:, 0:2, :], cited45[:])
         for j in range(PACK + 2, TILES):
             gelu(gelu_upper[:, j - PACK, :], cited[j])
-        deal_w2(0, kept("w2_w0", [HP, 2 * HALF], U8, "cited6"))
-        deal_w2(1, kept("w2_w1", [HP, 2 * HALF], U8, "cited7"))
         z_c[0] = laid(80, "z_c0", [M], U32)
         nc.vector.quantize_mx(out=z_c[0][:].bitcast(FP8X4), scales=z_s[0][:], in_=z_lower[:].rearrange("p m t -> p (m t)"))
         halves = (slice(0, M // 2), slice(M // 2, M))
-        early = laid(82, "early", [M // 2], F32)
-        nc.vector.tensor_copy(early[:], h[1][:].indirect(pos2_sb[:, 0 : M // 32]))
+        deal_w2(1, laid(82, "w2_w1", [HP, 2 * HALF], U8))
 
         z_upper = [kept(f"z_upper{u}", [M // 2, PACK], BF16) for u in range(2)]
         z_c[1] = kept("z_c1", [M], U32)
@@ -250,9 +248,9 @@ def tile_list_citation_chain_gate_kernel(tc, tab_words, tab_scales, offs, pos1, 
             nc.vector.quantize_mx(out=z_c[1][:, ms].bitcast(FP8X4), scales=z_s[1][:, ms], in_=z_upper[u][:].rearrange("p m t -> p (m t)"))
 
         y = []
-        for b, a in ((b, a) for b in range(HP) for a in range(HP)):
-            for t in range(PACK):
-                j = PACK * b + t
+        for a in range(HP):
+            for j in range(TILES):
+                b, t = divmod(j, PACK)
                 if a == 0:
                     y.append(psum.tile([P, BANK], F32, name=f"y{j}", tag="acc"))
                 nc.tensor.matmul_mx(
@@ -266,8 +264,7 @@ def tile_list_citation_chain_gate_kernel(tc, tab_words, tab_scales, offs, pos1, 
                 )
 
         late = kept("late", [TILES - 1, M], F32, "z_upper0")
-        nc.vector.tensor_copy(late[:, 0, halves[1]], h[1][:].indirect(pos2_sb[:, M // 32 :]))
-        for j in range(2, TILES):
+        for j in range(1, TILES):
             gather_citing(j, late[:, j - 1, :])
         out_rows = out.rearrange("(b p t) m -> p b t m", b=HP, t=PACK)
         gates = []
@@ -275,10 +272,8 @@ def tile_list_citation_chain_gate_kernel(tc, tab_words, tab_scales, offs, pos1, 
             gates.append(laid(28 + 2 * j, f"gate{j}", [M], F32) if j < ON_GPSIMD else kept(f"gate{j}", [M], F32))
             nc.scalar.activation(out=gates[j][:], in_=y[j][:], func=ACT.Sigmoid)
         for j in range(ON_GPSIMD):
-            pieces = [(slice(0, M), citing[j])] if j != 1 else [(halves[0], early[:]), (halves[1], late[:, 0, halves[1]])]
-            for ms, values in pieces:
-                nc.gpsimd.tensor_tensor(out=values, in0=gates[j][:, ms], in1=values, op=MULT)
-                nc.sync.dma_start(out=out_rows[:, j // PACK, j % PACK, ms], in_=values)
+            nc.gpsimd.tensor_tensor(out=citing[j], in0=gates[j][:], in1=citing[j], op=MULT)
+            nc.sync.dma_start(out=out_rows[:, j // PACK, j % PACK, :], in_=citing[j])
         gated = laid(28 + 2 * (ON_GPSIMD - 1), "gated", [TILES - ON_GPSIMD, M], F32)
         for j in range(ON_GPSIMD, TILES):
             for ms in [slice(0, M)] if j < TILES - 1 else halves:

@@ -25,7 +25,8 @@ HP = H // HALF
 TILES = H // P
 BANK = 512
 KIB = 1024
-ON_GPSIMD = 5
+ON_GPSIMD = 3
+EARLY = 2
 LEAD = 5
 
 
@@ -213,13 +214,15 @@ def tile_list_citation_chain_gate_kernel(tc, tab_words, tab_scales, offs, pos1, 
             for ahead in upper_banks[i + LEAD : i + LEAD + 1]:
                 first_product(ahead, 1)
 
-        gelu_lower = laid(66, "gelu_lower", [PACK, M], F32)
+        gelu_rest = laid(68, "gelu_rest", [PACK - 1, M], F32)
+        gelu_lower = [kept("gelu0", [M], F32)[:]] + [gelu_rest[:, t, :] for t in range(PACK - 1)]
         for t in range(PACK):
-            gelu(gelu_lower[:, t, :], cited[t])
-        gather_citing(0, laid(60, "citing0", [M], F32)[:])
+            gelu(gelu_lower[t], cited[t])
+        for j in range(EARLY):
+            gather_citing(j, laid(20 + 2 * j, f"citing{j}", [M], F32)[:])
         z_slots = laid(75, "z_slots", [PACK, M], BF16)
         for t in range(PACK):
-            nc.gpsimd.tensor_scalar(out=z_slots[:, t, :], in0=gelu_lower[:, t, :], scalar1=gains[:, 0, t : t + 1], scalar2=0.0, op0=MULT, op1=ADD)
+            nc.gpsimd.tensor_scalar(out=z_slots[:, t, :], in0=gelu_lower[t], scalar1=gains[:, 0, t : t + 1], scalar2=0.0, op0=MULT, op1=ADD)
         z_lower = kept("z_lower", [M, PACK], BF16)
         nc.gpsimd.tensor_scalar(out=z_lower[:], in0=z_slots[:].rearrange("p t m -> p m t"), scalar1=1.0, scalar2=0.0, op0=MULT, op1=ADD)
         empty(upper_banks)
@@ -263,9 +266,9 @@ def tile_list_citation_chain_gate_kernel(tc, tab_words, tab_scales, offs, pos1, 
                     stop=(a == HP - 1),
                 )
 
-        late = kept("late", [TILES - 1, M], F32, "z_upper0")
-        for j in range(1, TILES):
-            gather_citing(j, late[:, j - 1, :])
+        late = kept("late", [TILES - EARLY, M], F32, "z_upper0")
+        for j in range(EARLY, TILES):
+            gather_citing(j, late[:, j - EARLY, :])
         out_rows = out.rearrange("(b p t) m -> p b t m", b=HP, t=PACK)
         gates = []
         for j in range(TILES):

@@ -25,7 +25,7 @@ HP = H // HALF
 TILES = H // P
 BANK = 512
 KIB = 1024
-ON_GPSIMD = 3
+ON_GPSIMD = 4
 EARLY = 2
 LEAD = 5
 
@@ -71,10 +71,10 @@ def tile_list_citation_chain_gate_kernel(tc, tab_words, tab_scales, offs, pos1, 
             for s0 in range(0, S, step):
                 nc.vector.tensor_copy(v_w[a][:, s0 : s0 + step], tab[a][:].bitcast(U32).indirect(offs_sb[:, s0 // 16 : (s0 + step) // 16]))
 
-        def round_w1(copy, tile, raw, ts=slice(0, PACK), ms=slice(0, P)):
+        def round_w1(copy, tile, raw):
             copy(
-                out=tile[:].rearrange("p (t m j) -> p m j t", m=P, j=PACK)[:, ms],
-                in_=raw[:].rearrange("p j (m t) -> p m j t", t=PACK)[:, ms, :, ts],
+                out=tile[:].rearrange("p (t m j) -> p m j t", m=P, j=PACK),
+                in_=raw[:].rearrange("p j (m t) -> p m j t", t=PACK),
             )
 
         def gpsimd_copy(out, in_):
@@ -85,7 +85,7 @@ def tile_list_citation_chain_gate_kernel(tc, tab_words, tab_scales, offs, pos1, 
                 w1_c[b, a] = kept(f"w1_c{b}{a}", [HALF], U32) if codes is None else codes
                 w1_s[b, a] = kept(f"w1_s{b}{a}", [HALF], U8)
             cols = slice(ts.start * P, ts.stop * P)
-            nc.vector.quantize_mx(out=w1_c[b, a][:, cols].bitcast(FP8X4), scales=w1_s[b, a][:, cols], in_=tile[:])
+            nc.vector.quantize_mx(out=w1_c[b, a][:, cols].bitcast(FP8X4), scales=w1_s[b, a][:, cols], in_=tile[:, :])
 
         h = [kept(f"h{j}", [S], F32) for j in range(TILES)]
 
@@ -122,8 +122,8 @@ def tile_list_citation_chain_gate_kernel(tc, tab_words, tab_scales, offs, pos1, 
         def deal_w2(b, tile):
             w2_w[b] = tile
             nc.vector.tensor_copy(
-                out=tile[:].bitcast(U16).rearrange("p a (t m) -> p a t m", t=PACK),
-                in_=w2_raw[b][:].bitcast(U16).rearrange("p a (m t) -> p a t m", t=PACK),
+                out=tile[:].bitcast(U16).rearrange("p a (t m) -> p a m t", t=PACK),
+                in_=w2_raw[b][:].bitcast(U16).rearrange("p a (m t) -> p a m t", t=PACK),
             )
 
         z_s = [kept(f"z_s{b}", [M], U8) for b in range(HP)]
@@ -187,11 +187,9 @@ def tile_list_citation_chain_gate_kernel(tc, tab_words, tab_scales, offs, pos1, 
                 first_product(bank, a)
         empty(lower_banks)
 
-        rounded10 = [laid(72 + 2 * u, f"rounded10{u}", [HALF * 2], BF16) for u in range(2)]
-        for u in range(2):
-            round_w1(nc.vector.tensor_copy, rounded10[u], raw10, slice(2 * u, 2 * u + 2))
-        for u in range(2):
-            quantise_w1(1, 0, rounded10[u], slice(2 * u, 2 * u + 2))
+        rounded10 = laid(72, "rounded10", [HALF * PACK], BF16)
+        round_w1(nc.vector.tensor_copy, rounded10, raw10)
+        quantise_w1(1, 0, rounded10)
         for j in range(PACK - 1):
             gather_cited(j, laid(44 + 2 * j, f"cited{j}", [M], F32)[:])
         for bank in upper_banks:
@@ -200,13 +198,10 @@ def tile_list_citation_chain_gate_kernel(tc, tab_words, tab_scales, offs, pos1, 
         round_w1(gpsimd_copy, rounded11, raw11)
         quantise_w1(1, 1, rounded11)
         gather_cited(3, laid(52, "cited3", [M], F32)[:])
-        front = laid(60, "rounded12a", [HALF * 2], BF16)
-        round_w1(nc.scalar.copy, front, raw12, slice(0, 2))
-        back = laid(74, "rounded12b", [HALF * 2], BF16)
-        round_w1(nc.scalar.copy, back, raw12, slice(2, PACK), slice(0, P // 2))
-        round_w1(gpsimd_copy, back, raw12, slice(2, PACK), slice(P // 2, P))
-        quantise_w1(1, 2, front, slice(0, 2))
-        quantise_w1(1, 2, back, slice(2, PACK))
+        rounded12 = laid(60, "rounded12", [HALF * PACK], BF16)
+        round_w1(nc.scalar.copy, rounded12, raw12)
+        quantise_w1(1, 2, rounded12[:, : 2 * HALF], slice(0, 2))
+        quantise_w1(1, 2, rounded12[:, 2 * HALF :], slice(2, PACK))
         for bank in upper_banks[:LEAD]:
             first_product(bank, 1)
         for i, bank in enumerate(upper_banks):
@@ -214,13 +209,13 @@ def tile_list_citation_chain_gate_kernel(tc, tab_words, tab_scales, offs, pos1, 
             for ahead in upper_banks[i + LEAD : i + LEAD + 1]:
                 first_product(ahead, 1)
 
-        gelu_rest = laid(68, "gelu_rest", [PACK - 1, M], F32)
+        gelu_rest = laid(16, "gelu_rest", [PACK - 1, M], F32)
         gelu_lower = [kept("gelu0", [M], F32)[:]] + [gelu_rest[:, t, :] for t in range(PACK - 1)]
         for t in range(PACK):
             gelu(gelu_lower[t], cited[t])
         for j in range(EARLY):
-            gather_citing(j, laid(20 + 2 * j, f"citing{j}", [M], F32)[:])
-        z_slots = laid(75, "z_slots", [PACK, M], BF16)
+            gather_citing(j, laid(22 + 2 * j, f"citing{j}", [M], F32)[:])
+        z_slots = laid(62, "z_slots", [PACK, M], BF16)
         for t in range(PACK):
             nc.gpsimd.tensor_scalar(out=z_slots[:, t, :], in0=gelu_lower[t], scalar1=gains[:, 0, t : t + 1], scalar2=0.0, op0=MULT, op1=ADD)
         z_lower = kept("z_lower", [M, PACK], BF16)

@@ -25,8 +25,8 @@ HP = H // HALF
 TILES = H // P
 BANK = 512
 KIB = 1024
-ON_GPSIMD = 4
-EARLY = 2
+ON_GPSIMD = 3
+EARLY = 3
 LEAD = 5
 
 
@@ -121,7 +121,7 @@ def tile_list_citation_chain_gate_kernel(tc, tab_words, tab_scales, offs, pos1, 
 
         def deal_w2(b, tile):
             w2_w[b] = tile
-            nc.vector.tensor_copy(
+            nc.scalar.copy(
                 out=tile[:].bitcast(U16).rearrange("p a (t m) -> p a m t", t=PACK),
                 in_=w2_raw[b][:].bitcast(U16).rearrange("p a (m t) -> p a m t", t=PACK),
             )
@@ -134,7 +134,6 @@ def tile_list_citation_chain_gate_kernel(tc, tab_words, tab_scales, offs, pos1, 
         load_tab(0, laid(0, "tab0", [T], I32))
         nc.sync.dma_start(offs_sb[:], offs)
         raw00 = load_w1(0, 0, HALF, laid(20, "raw00", [PACK, HALF], F32))
-        load_w2(0, kept("w2_raw0", [HP, 2 * HALF], U8))
         raw01 = load_w1(1, 0, HALF, laid(40, "raw01", [PACK, HALF], F32))
         nc.sync.dma_start(pos1_sb[:], pos1)
         nc.sync.dma_start(pos2_sb[:], pos2)
@@ -164,7 +163,6 @@ def tile_list_citation_chain_gate_kernel(tc, tab_words, tab_scales, offs, pos1, 
         raw10 = load_w1(0, HALF, HALF, laid(44, "raw10", [PACK, HALF], F32))
         raw11 = load_w1(1, HALF, HALF, laid(52, "raw11", [PACK, HALF], F32))
         nc.vector.tensor_copy(v_s[:], tab_sc[:].indirect(offs_sb[:]))
-        deal_w2(0, kept("w2_w0", [HP, 2 * HALF], U8))
         for b in range(HP):
             w2_s[b] = kept(f"w2_s{b}", [HP, HALF], U8)
             nc.vector.tensor_copy(
@@ -178,6 +176,7 @@ def tile_list_citation_chain_gate_kernel(tc, tab_words, tab_scales, offs, pos1, 
         raw12 = load_w1(2, HALF, HALF, laid(20, "raw12", [PACK, HALF], F32))
         gains = laid(91, "gains", [HP, PACK], F32)
         nc.sync.dma_start(out=gains[:], in_=gain.rearrange("(b p t) -> p b t", b=HP, t=PACK))
+        load_w2(0, laid(89, "w2_raw0", [HP, 2 * HALF], U8))
         load_w2(1, laid(92, "w2_raw1", [HP, 2 * HALF], U8))
         gather_tab(2, 2)
         lower_banks = [(0, 0), (1, 0), (0, 1), (1, 1), (2, 0), (2, 1), (3, 0), (3, 1)]
@@ -213,6 +212,7 @@ def tile_list_citation_chain_gate_kernel(tc, tab_words, tab_scales, offs, pos1, 
         gelu_lower = [kept("gelu0", [M], F32)[:]] + [gelu_rest[:, t, :] for t in range(PACK - 1)]
         for t in range(PACK):
             gelu(gelu_lower[t], cited[t])
+        deal_w2(0, kept("w2_w0", [HP, 2 * HALF], U8))
         for j in range(EARLY):
             gather_citing(j, laid(22 + 2 * j, f"citing{j}", [M], F32)[:])
         z_slots = laid(62, "z_slots", [PACK, M], BF16)
@@ -231,7 +231,7 @@ def tile_list_citation_chain_gate_kernel(tc, tab_words, tab_scales, offs, pos1, 
         z_c[0] = laid(80, "z_c0", [M], U32)
         nc.vector.quantize_mx(out=z_c[0][:].bitcast(FP8X4), scales=z_s[0][:], in_=z_lower[:].rearrange("p m t -> p (m t)"))
         halves = (slice(0, M // 2), slice(M // 2, M))
-        deal_w2(1, laid(82, "w2_w1", [HP, 2 * HALF], U8))
+        deal_w2(1, kept("w2_w1", [HP, 2 * HALF], U8, "cited6"))
 
         z_upper = [kept(f"z_upper{u}", [M // 2, PACK], BF16) for u in range(2)]
         z_c[1] = kept("z_c1", [M], U32)
@@ -246,8 +246,8 @@ def tile_list_citation_chain_gate_kernel(tc, tab_words, tab_scales, offs, pos1, 
             nc.vector.quantize_mx(out=z_c[1][:, ms].bitcast(FP8X4), scales=z_s[1][:, ms], in_=z_upper[u][:].rearrange("p m t -> p (m t)"))
 
         y = []
-        for a in range(HP):
-            for j in range(TILES):
+        for j in range(TILES):
+            for a in range(HP):
                 b, t = divmod(j, PACK)
                 if a == 0:
                     y.append(psum.tile([P, BANK], F32, name=f"y{j}", tag="acc"))
@@ -261,19 +261,27 @@ def tile_list_citation_chain_gate_kernel(tc, tab_words, tab_scales, offs, pos1, 
                     stop=(a == HP - 1),
                 )
 
-        late = kept("late", [TILES - EARLY, M], F32, "z_upper0")
-        for j in range(EARLY, TILES):
-            gather_citing(j, late[:, j - EARLY, :])
         out_rows = out.rearrange("(b p t) m -> p b t m", b=HP, t=PACK)
-        gates = []
+        gates = [laid(28 + 8 * j, f"gate{j}", [M], F32) for j in range(TILES)]
         for j in range(TILES):
-            gates.append(laid(28 + 2 * j, f"gate{j}", [M], F32) if j < ON_GPSIMD else kept(f"gate{j}", [M], F32))
             nc.scalar.activation(out=gates[j][:], in_=y[j][:], func=ACT.Sigmoid)
-        for j in range(ON_GPSIMD):
-            nc.gpsimd.tensor_tensor(out=citing[j], in0=gates[j][:], in1=citing[j], op=MULT)
-            nc.sync.dma_start(out=out_rows[:, j // PACK, j % PACK, :], in_=citing[j])
-        gated = laid(28 + 2 * (ON_GPSIMD - 1), "gated", [TILES - ON_GPSIMD, M], F32)
-        for j in range(ON_GPSIMD, TILES):
-            for ms in [slice(0, M)] if j < TILES - 1 else halves:
-                nc.vector.tensor_tensor(out=gated[:, j - ON_GPSIMD, ms], in0=gates[j][:, ms], in1=citing[j][:, ms], op=MULT)
-                nc.sync.dma_start(out=out_rows[:, j // PACK, j % PACK, ms], in_=gated[:, j - ON_GPSIMD, ms])
+
+        def gate(j, engine, dst, ms=slice(0, M)):
+            engine.tensor_tensor(out=dst[:, ms], in0=gates[j][:, ms], in1=citing[j][:, ms], op=MULT)
+            nc.sync.dma_start(out=out_rows[:, j // PACK, j % PACK, ms], in_=dst[:, ms])
+
+        first = TILES - 1 - ON_GPSIMD
+        middle = kept("middle", [first + 1 - EARLY, M], F32, "z_upper0")
+        for j in range(EARLY, first + 1):
+            gather_citing(j, middle[:, j - EARLY, :])
+        for j in range(first):
+            gate(j, nc.vector, citing[j])
+        late = laid(28 + 8 * (first - 2), "late", [ON_GPSIMD, M], F32)
+        for j in range(first + 1, TILES):
+            gather_citing(j, late[:, j - first - 1, :])
+        shared = laid(28 + 8 * (first - 1), "shared", [ON_GPSIMD, M], F32)
+        for j in range(first, TILES - 1):
+            gate(j, nc.gpsimd, shared[:, j - first, :])
+        last = laid(28 + 8 * (TILES - 2), "last", [M], F32)
+        for ms in halves:
+            gate(TILES - 1, nc.vector, last[:], ms)

@@ -25,7 +25,7 @@ HP = H // HALF
 TILES = H // P
 BANK = 512
 KIB = 1024
-ON_GPSIMD = 3
+ON_GPSIMD = 2
 EARLY = 3
 LEAD = 5
 
@@ -60,10 +60,9 @@ def tile_list_citation_chain_gate_kernel(tc, tab_words, tab_scales, offs, pos1, 
             nc.sync.dma_start(out=tile[:], in_=rows.rearrange("(p j) n -> p j n", j=PACK))
             return tile
 
-        def load_w2(b, tile):
-            w2_raw[b] = tile
-            cols = w2_words[:, :, b * 2 * HALF : (b + 1) * 2 * HALF]
-            nc.sync.dma_start(out=w2_raw[b][:].bitcast(I32), in_=cols.rearrange("a p n -> p a n").bitcast(I32))
+        def load_w2(a, tile):
+            w2_raw[a] = tile
+            nc.sync.dma_start(out=tile[:].bitcast(I32), in_=w2_words[a].bitcast(I32))
 
         def gather_tab(a, pieces, tag=None):
             v_w[a] = kept(f"v_w{a}", [S], U32, tag)
@@ -119,12 +118,11 @@ def tile_list_citation_chain_gate_kernel(tc, tab_words, tab_scales, offs, pos1, 
         def gelu(dst, src):
             nc.scalar.activation(out=dst, in_=src, func=ACT.Gelu_apprx_tanh)
 
-        def deal_w2(b, tile):
-            w2_w[b] = tile
-            nc.scalar.copy(
-                out=tile[:].bitcast(U16).rearrange("p a (t m) -> p a m t", t=PACK),
-                in_=w2_raw[b][:].bitcast(U16).rearrange("p a (m t) -> p a m t", t=PACK),
-            )
+        def deal_w2(a, halves_of_h, tile):
+            words = w2_raw[a][:].bitcast(U16).rearrange("p (b m t) -> p b m t", b=HP, t=PACK)
+            nc.scalar.copy(out=tile[:].bitcast(U16).rearrange("p (b t m) -> p b m t", t=PACK, m=P), in_=words[:, halves_of_h])
+            for b in range(halves_of_h.start, halves_of_h.stop):
+                w2_w[a, b] = tile[:, (b - halves_of_h.start) * 2 * HALF : (b - halves_of_h.start + 1) * 2 * HALF]
 
         z_s = [kept(f"z_s{b}", [M], U8) for b in range(HP)]
 
@@ -176,8 +174,8 @@ def tile_list_citation_chain_gate_kernel(tc, tab_words, tab_scales, offs, pos1, 
         raw12 = load_w1(2, HALF, HALF, laid(20, "raw12", [PACK, HALF], F32))
         gains = laid(91, "gains", [HP, PACK], F32)
         nc.sync.dma_start(out=gains[:], in_=gain.rearrange("(b p t) -> p b t", b=HP, t=PACK))
-        load_w2(0, laid(89, "w2_raw0", [HP, 2 * HALF], U8))
-        load_w2(1, laid(92, "w2_raw1", [HP, 2 * HALF], U8))
+        load_w2(0, laid(89, "w2_raw0", [2 * H], U8))
+        load_w2(1, laid(92, "w2_raw1", [2 * H], U8))
         gather_tab(2, 2)
         lower_banks = [(0, 0), (1, 0), (0, 1), (1, 1), (2, 0), (2, 1), (3, 0), (3, 1)]
         upper_banks = [(j, s) for j in range(PACK, TILES) for s in range(S // BANK)]
@@ -212,7 +210,7 @@ def tile_list_citation_chain_gate_kernel(tc, tab_words, tab_scales, offs, pos1, 
         gelu_lower = [kept("gelu0", [M], F32)[:]] + [gelu_rest[:, t, :] for t in range(PACK - 1)]
         for t in range(PACK):
             gelu(gelu_lower[t], cited[t])
-        deal_w2(0, kept("w2_w0", [HP, 2 * HALF], U8))
+        deal_w2(0, slice(0, 1), kept("w2_w00", [2 * HALF], U8))
         for j in range(EARLY):
             gather_citing(j, laid(22 + 2 * j, f"citing{j}", [M], F32)[:])
         z_slots = laid(62, "z_slots", [PACK, M], BF16)
@@ -221,6 +219,7 @@ def tile_list_citation_chain_gate_kernel(tc, tab_words, tab_scales, offs, pos1, 
         z_lower = kept("z_lower", [M, PACK], BF16)
         nc.gpsimd.tensor_scalar(out=z_lower[:], in0=z_slots[:].rearrange("p t m -> p m t"), scalar1=1.0, scalar2=0.0, op0=MULT, op1=ADD)
         empty(upper_banks)
+        deal_w2(0, slice(1, 2), kept("w2_w01", [2 * HALF], U8, "w1_c12"))
         cited45 = laid(80, "cited45", [2, M], F32)
         for j in range(PACK, TILES):
             gather_cited(j, cited45[:, j - PACK, :] if j < PACK + 2 else kept(f"cited{j}", [M], F32)[:])
@@ -231,7 +230,9 @@ def tile_list_citation_chain_gate_kernel(tc, tab_words, tab_scales, offs, pos1, 
         z_c[0] = laid(80, "z_c0", [M], U32)
         nc.vector.quantize_mx(out=z_c[0][:].bitcast(FP8X4), scales=z_s[0][:], in_=z_lower[:].rearrange("p m t -> p (m t)"))
         halves = (slice(0, M // 2), slice(M // 2, M))
-        deal_w2(1, kept("w2_w1", [HP, 2 * HALF], U8, "cited6"))
+        deal_w2(1, slice(0, HP), kept("w2_w1", [2 * H], U8, "cited6"))
+        early = laid(82, "early", [M // 2], F32)
+        nc.vector.tensor_copy(early[:], h[EARLY][:].indirect(pos2_sb[:, 0 : M // 32]))
 
         z_upper = [kept(f"z_upper{u}", [M // 2, PACK], BF16) for u in range(2)]
         z_c[1] = kept("z_c1", [M], U32)
@@ -246,14 +247,14 @@ def tile_list_citation_chain_gate_kernel(tc, tab_words, tab_scales, offs, pos1, 
             nc.vector.quantize_mx(out=z_c[1][:, ms].bitcast(FP8X4), scales=z_s[1][:, ms], in_=z_upper[u][:].rearrange("p m t -> p (m t)"))
 
         y = []
-        for j in range(TILES):
-            for a in range(HP):
+        for a in range(HP):
+            for j in range(TILES):
                 b, t = divmod(j, PACK)
                 if a == 0:
                     y.append(psum.tile([P, BANK], F32, name=f"y{j}", tag="acc"))
                 nc.tensor.matmul_mx(
                     out=y[j][:],
-                    lhsT=w2_w[b][:, a, 2 * t * P : 2 * (t + 1) * P].bitcast(FP4X4),
+                    lhsT=w2_w[a, b][:, 2 * t * P : 2 * (t + 1) * P].bitcast(FP4X4),
                     lhsT_scale=w2_s[b][:, a, t * P : (t + 1) * P],
                     rhs=z_c[a][:].bitcast(FP8X4),
                     rhs_scale=z_s[a][:],
@@ -270,12 +271,22 @@ def tile_list_citation_chain_gate_kernel(tc, tab_words, tab_scales, offs, pos1, 
             engine.tensor_tensor(out=dst[:, ms], in0=gates[j][:, ms], in1=citing[j][:, ms], op=MULT)
             nc.sync.dma_start(out=out_rows[:, j // PACK, j % PACK, ms], in_=dst[:, ms])
 
+        def gate_split(j):
+            nc.vector.tensor_tensor(out=citing[j][:, halves[0]], in0=gates[j][:, halves[0]], in1=early[:], op=MULT)
+            nc.vector.tensor_tensor(out=citing[j][:, halves[1]], in0=gates[j][:, halves[1]], in1=citing[j][:, halves[1]], op=MULT)
+            nc.sync.dma_start(out=out_rows[:, j // PACK, j % PACK, :], in_=citing[j])
+
         first = TILES - 1 - ON_GPSIMD
         middle = kept("middle", [first + 1 - EARLY, M], F32, "z_upper0")
-        for j in range(EARLY, first + 1):
+        citing[EARLY] = middle[:, 0, :]
+        nc.vector.tensor_copy(middle[:, 0, halves[1]], h[EARLY][:].indirect(pos2_sb[:, M // 32 :]))
+        for j in range(EARLY + 1, first + 1):
             gather_citing(j, middle[:, j - EARLY, :])
         for j in range(first):
-            gate(j, nc.vector, citing[j])
+            if j == EARLY:
+                gate_split(j)
+            else:
+                gate(j, nc.vector, citing[j])
         late = laid(28 + 8 * (first - 2), "late", [ON_GPSIMD, M], F32)
         for j in range(first + 1, TILES):
             gather_citing(j, late[:, j - first - 1, :])

@@ -25,7 +25,7 @@ HP = H // HALF
 TILES = H // P
 BANK = 512
 KIB = 1024
-ON_GPSIMD = 2
+FUSED = 3
 EARLY = 3
 LEAD = 5
 
@@ -276,23 +276,19 @@ def tile_list_citation_chain_gate_kernel(tc, tab_words, tab_scales, offs, pos1, 
             nc.vector.tensor_tensor(out=citing[j][:, halves[1]], in0=gates[j][:, halves[1]], in1=citing[j][:, halves[1]], op=MULT)
             nc.sync.dma_start(out=out_rows[:, j // PACK, j % PACK, :], in_=citing[j])
 
-        first = TILES - 1 - ON_GPSIMD
-        middle = kept("middle", [first + 1 - EARLY, M], F32, "z_upper0")
+        first = TILES - FUSED
+        middle = kept("middle", [first - EARLY, M], F32, "z_upper0")
         citing[EARLY] = middle[:, 0, :]
         nc.vector.tensor_copy(middle[:, 0, halves[1]], h[EARLY][:].indirect(pos2_sb[:, M // 32 :]))
-        for j in range(EARLY + 1, first + 1):
+        for j in range(EARLY + 1, first):
             gather_citing(j, middle[:, j - EARLY, :])
         for j in range(first):
             if j == EARLY:
                 gate_split(j)
             else:
                 gate(j, nc.vector, citing[j])
-        late = laid(28 + 8 * (first - 2), "late", [ON_GPSIMD, M], F32)
-        for j in range(first + 1, TILES):
-            gather_citing(j, late[:, j - first - 1, :])
-        shared = laid(28 + 8 * (first - 1), "shared", [ON_GPSIMD, M], F32)
-        for j in range(first, TILES - 1):
-            gate(j, nc.gpsimd, shared[:, j - first, :])
-        last = laid(28 + 8 * (TILES - 2), "last", [M], F32)
-        for ms in halves:
-            gate(TILES - 1, nc.vector, last[:], ms)
+        for j in range(first, TILES):
+            gated = kept(f"gated{j}", [M], F32)
+            for ms in halves if j == TILES - 1 else (slice(0, M),):
+                nc.vector.tensor_tensor(gated[:, ms], h[j][:].indirect(pos2_sb[:, ms.start // 16 : ms.stop // 16]), gates[j][:, ms], MULT)
+                nc.sync.dma_start(out=out_rows[:, j // PACK, j % PACK, ms], in_=gated[:, ms])

@@ -25,7 +25,7 @@ HP = H // HALF
 TILES = H // P
 BANK = 512
 KIB = 1024
-FUSED = 3
+STARTERS = 2
 EARLY = 3
 LEAD = 5
 
@@ -161,13 +161,13 @@ def tile_list_citation_chain_gate_kernel(tc, tab_words, tab_scales, offs, pos1, 
         raw10 = load_w1(0, HALF, HALF, laid(44, "raw10", [PACK, HALF], F32))
         raw11 = load_w1(1, HALF, HALF, laid(52, "raw11", [PACK, HALF], F32))
         nc.vector.tensor_copy(v_s[:], tab_sc[:].indirect(offs_sb[:]))
+        gather_tab(1, 1, "tab_sc")
         for b in range(HP):
-            w2_s[b] = kept(f"w2_s{b}", [HP, HALF], U8)
+            w2_s[b] = laid(2 + b, f"w2_s{b}", [HP, HALF], U8)
             nc.vector.tensor_copy(
                 out=w2_s[b][:].rearrange("p a (t m) -> p a t m", t=PACK),
                 in_=w2_s_raw[:, :, b * HALF : (b + 1) * HALF].rearrange("p a (m t) -> p a t m", t=PACK),
             )
-        gather_tab(1, 1, "tab_sc")
         rounded02 = laid(90, "rounded02", [HALF * PACK], BF16)
         round_w1(nc.scalar.copy, rounded02, raw02)
         quantise_w1(0, 2, rounded02, codes=laid(0, "w1_c02", [HALF], U32))
@@ -234,61 +234,82 @@ def tile_list_citation_chain_gate_kernel(tc, tab_words, tab_scales, offs, pos1, 
         early = laid(82, "early", [M // 2], F32)
         nc.vector.tensor_copy(early[:], h[EARLY][:].indirect(pos2_sb[:, 0 : M // 32]))
 
-        z_upper = [kept(f"z_upper{u}", [M // 2, PACK], BF16) for u in range(2)]
+        z_upper = kept("z_upper", [M, PACK], BF16)
         z_c[1] = kept("z_c1", [M], U32)
-        for u, ms in enumerate(halves):
+
+        def weave_upper(ms):
             nc.vector.tensor_tensor(
-                out=z_upper[u][:].rearrange("p (g i) t -> p g t i", i=4),
+                out=z_upper[:, ms, :].rearrange("p (g i) t -> p g t i", i=4),
                 in0=gelu_upper[:, :, ms].rearrange("p t (g i) -> p g t i", i=4),
-                in1=gains[:, 1, :].unsqueeze(1).unsqueeze(3).to_broadcast([P, M // 8, PACK, 4]),
+                in1=gains[:, 1, :].unsqueeze(1).unsqueeze(3).to_broadcast([P, (ms.stop - ms.start) // 4, PACK, 4]),
                 op=MULT,
             )
-        for u, ms in enumerate(halves):
-            nc.vector.quantize_mx(out=z_c[1][:, ms].bitcast(FP8X4), scales=z_s[1][:, ms], in_=z_upper[u][:].rearrange("p m t -> p (m t)"))
 
-        y = []
-        for a in range(HP):
-            for j in range(TILES):
-                b, t = divmod(j, PACK)
-                if a == 0:
-                    y.append(psum.tile([P, BANK], F32, name=f"y{j}", tag="acc"))
-                nc.tensor.matmul_mx(
-                    out=y[j][:],
-                    lhsT=w2_w[a, b][:, 2 * t * P : 2 * (t + 1) * P].bitcast(FP4X4),
-                    lhsT_scale=w2_s[b][:, a, t * P : (t + 1) * P],
-                    rhs=z_c[a][:].bitcast(FP8X4),
-                    rhs_scale=z_s[a][:],
-                    start=(a == 0),
-                    stop=(a == HP - 1),
-                )
+        def quantise_upper(ms):
+            nc.vector.quantize_mx(out=z_c[1][:, ms].bitcast(FP8X4), scales=z_s[1][:, ms], in_=z_upper[:, ms, :].rearrange("p m t -> p (m t)"))
+
+        weave_upper(halves[0])
+        weave_upper(slice(M // 2, 3 * M // 4))
+        quantise_upper(halves[0])
+        weave_upper(slice(3 * M // 4, M))
+        quantise_upper(halves[1])
+        late = kept("late", [M // 2], F32, "gelu_upper")
+        nc.vector.tensor_copy(late[:], h[EARLY][:].indirect(pos2_sb[:, M // 32 :]))
+
+        y = {}
+
+        def second_product(piece, a):
+            j, ms = piece
+            b, t = divmod(j, PACK)
+            if a == 0:
+                y[j, ms.start] = psum.tile([P, ms.stop - ms.start], F32, name=f"y{j}", tag="acc")
+            nc.tensor.matmul_mx(
+                out=y[j, ms.start][:],
+                lhsT=w2_w[a, b][:, 2 * t * P : 2 * (t + 1) * P].bitcast(FP4X4),
+                lhsT_scale=w2_s[b][:, a, t * P : (t + 1) * P],
+                rhs=z_c[a][:, ms].bitcast(FP8X4),
+                rhs_scale=z_s[a][:, ms],
+                start=(a == 0),
+                stop=(a == HP - 1),
+            )
+
+        whole = slice(0, M)
+        starters = range(EARLY + 1, EARLY + 1 + STARTERS)
+        front = [(j, halves[0]) for j in starters] + [(j, whole) for j in range(EARLY + 1)]
+        back = [(j, halves[1]) for j in starters]
+        last = [(j, whole) for j in range(starters.stop, TILES)]
+        for piece in front + last:
+            second_product(piece, 0)
+        for piece in front:
+            second_product(piece, 1)
+        for piece in back:
+            second_product(piece, 0)
+            second_product(piece, 1)
+        for piece in last:
+            second_product(piece, 1)
 
         out_rows = out.rearrange("(b p t) m -> p b t m", b=HP, t=PACK)
         gates = [laid(28 + 8 * j, f"gate{j}", [M], F32) for j in range(TILES)]
-        for j in range(TILES):
-            nc.scalar.activation(out=gates[j][:], in_=y[j][:], func=ACT.Sigmoid)
+        gated = [kept(f"gated{j}", [M], F32) for j in range(TILES)]
+        for j, ms in front + back + last:
+            nc.scalar.activation(out=gates[j][:, ms], in_=y[j, ms.start][:], func=ACT.Sigmoid)
 
-        def gate(j, engine, dst, ms=slice(0, M)):
-            engine.tensor_tensor(out=dst[:, ms], in0=gates[j][:, ms], in1=citing[j][:, ms], op=MULT)
-            nc.sync.dma_start(out=out_rows[:, j // PACK, j % PACK, ms], in_=dst[:, ms])
+        def fused(j, ms):
+            nc.vector.tensor_tensor(gated[j][:, ms], h[j][:].indirect(pos2_sb[:, ms.start // 16 : ms.stop // 16]), gates[j][:, ms], MULT)
 
-        def gate_split(j):
-            nc.vector.tensor_tensor(out=citing[j][:, halves[0]], in0=gates[j][:, halves[0]], in1=early[:], op=MULT)
-            nc.vector.tensor_tensor(out=citing[j][:, halves[1]], in0=gates[j][:, halves[1]], in1=citing[j][:, halves[1]], op=MULT)
-            nc.sync.dma_start(out=out_rows[:, j // PACK, j % PACK, :], in_=citing[j])
+        def store(j, ms=whole):
+            nc.sync.dma_start(out=out_rows[:, j // PACK, j % PACK, ms], in_=gated[j][:, ms])
 
-        first = TILES - FUSED
-        middle = kept("middle", [first - EARLY, M], F32, "z_upper0")
-        citing[EARLY] = middle[:, 0, :]
-        nc.vector.tensor_copy(middle[:, 0, halves[1]], h[EARLY][:].indirect(pos2_sb[:, M // 32 :]))
-        for j in range(EARLY + 1, first):
-            gather_citing(j, middle[:, j - EARLY, :])
-        for j in range(first):
-            if j == EARLY:
-                gate_split(j)
+        for j, ms in front + back + last[:-1]:
+            if j < EARLY:
+                nc.vector.tensor_tensor(out=gated[j][:], in0=gates[j][:], in1=citing[j], op=MULT)
+            elif j == EARLY:
+                for part, picked in zip(halves, (early, late)):
+                    nc.vector.tensor_tensor(out=gated[j][:, part], in0=gates[j][:, part], in1=picked[:], op=MULT)
             else:
-                gate(j, nc.vector, citing[j])
-        for j in range(first, TILES):
-            gated = kept(f"gated{j}", [M], F32)
-            for ms in halves if j == TILES - 1 else (slice(0, M),):
-                nc.vector.tensor_tensor(gated[:, ms], h[j][:].indirect(pos2_sb[:, ms.start // 16 : ms.stop // 16]), gates[j][:, ms], MULT)
-                nc.sync.dma_start(out=out_rows[:, j // PACK, j % PACK, ms], in_=gated[:, ms])
+                fused(j, ms)
+            if ms.stop == M:
+                store(j)
+        for ms in halves:
+            fused(TILES - 1, ms)
+            store(TILES - 1, ms)

@@ -25,8 +25,9 @@ HP = H // HALF
 TILES = H // P
 BANK = 512
 KIB = 1024
-STARTERS = 2
-EARLY = 3
+BANKS = 8
+AHEAD = 5
+EARLY = 2
 LEAD = 5
 
 
@@ -35,7 +36,7 @@ def tile_list_citation_chain_gate_kernel(tc, tab_words, tab_scales, offs, pos1, 
     with ExitStack() as ctx:
         keep = ctx.enter_context(tc.tile_pool(name="keep", bufs=1))
         arena = ctx.enter_context(tc.tile_pool(name="arena", bufs=1))
-        psum = ctx.enter_context(tc.psum_pool(name="psum", bufs=8))
+        psum = ctx.enter_context(tc.psum_pool(name="psum", bufs=1))
 
         def kept(name, shape, dtype, tag=None):
             return keep.tile([P] + shape, dtype, name=name, tag=tag or name, align_bytes=64)
@@ -70,10 +71,10 @@ def tile_list_citation_chain_gate_kernel(tc, tab_words, tab_scales, offs, pos1, 
             for s0 in range(0, S, step):
                 nc.vector.tensor_copy(v_w[a][:, s0 : s0 + step], tab[a][:].bitcast(U32).indirect(offs_sb[:, s0 // 16 : (s0 + step) // 16]))
 
-        def round_w1(copy, tile, raw):
+        def round_w1(copy, tile, raw, quads=slice(0, P)):
             copy(
-                out=tile[:].rearrange("p (t m j) -> p m j t", m=P, j=PACK),
-                in_=raw[:].rearrange("p j (m t) -> p m j t", t=PACK),
+                out=tile[:].rearrange("p (t m j) -> p m j t", m=P, j=PACK)[:, quads],
+                in_=raw[:].rearrange("p j (m t) -> p m j t", t=PACK)[:, quads],
             )
 
         def gpsimd_copy(out, in_):
@@ -91,7 +92,7 @@ def tile_list_citation_chain_gate_kernel(tc, tab_words, tab_scales, offs, pos1, 
         def first_product(bank, a):
             j, s = bank
             if a == 0:
-                acc[bank] = psum.tile([P, BANK], F32, name=f"acc{j}", tag="acc")
+                acc[bank] = psum.tile([P, BANK], F32, name=f"acc{j}{s}", tag=f"bank{len(acc) % BANKS}")
             b, t = divmod(j, PACK)
             nc.tensor.matmul_mx(
                 out=acc[bank][:],
@@ -189,14 +190,18 @@ def tile_list_citation_chain_gate_kernel(tc, tab_words, tab_scales, offs, pos1, 
         quantise_w1(1, 0, rounded10)
         for j in range(PACK - 1):
             gather_cited(j, laid(44 + 2 * j, f"cited{j}", [M], F32)[:])
+        cited[3] = laid(50, "cited3", [M // 2], F32)[:]
+        nc.vector.tensor_copy(cited[3], h[3][:].indirect(pos1_sb[:, : M // 32]))
         for bank in upper_banks:
             first_product(bank, 0)
         rounded11 = laid(72, "rounded11", [HALF * PACK], BF16)
         round_w1(gpsimd_copy, rounded11, raw11)
         quantise_w1(1, 1, rounded11)
-        gather_cited(3, laid(52, "cited3", [M], F32)[:])
         rounded12 = laid(60, "rounded12", [HALF * PACK], BF16)
-        round_w1(nc.scalar.copy, rounded12, raw12)
+        round_w1(nc.scalar.copy, rounded12, raw12, slice(0, P // 2))
+        round_w1(nc.vector.tensor_copy, rounded12, raw12, slice(P // 2, P))
+        rest3 = laid(52, "rest3", [M // 2], F32)
+        nc.vector.tensor_copy(rest3[:], h[3][:].indirect(pos1_sb[:, M // 32 :]))
         quantise_w1(1, 2, rounded12[:, : 2 * HALF], slice(0, 2))
         quantise_w1(1, 2, rounded12[:, 2 * HALF :], slice(2, PACK))
         for bank in upper_banks[:LEAD]:
@@ -208,9 +213,11 @@ def tile_list_citation_chain_gate_kernel(tc, tab_words, tab_scales, offs, pos1, 
 
         gelu_rest = laid(16, "gelu_rest", [PACK - 1, M], F32)
         gelu_lower = [kept("gelu0", [M], F32)[:]] + [gelu_rest[:, t, :] for t in range(PACK - 1)]
-        for t in range(PACK):
+        for t in range(PACK - 1):
             gelu(gelu_lower[t], cited[t])
-        deal_w2(0, slice(0, 1), kept("w2_w00", [2 * HALF], U8))
+        deal_w2(0, slice(0, HP), kept("w2_w0", [2 * H], U8))
+        gelu(gelu_lower[3][:, : M // 2], cited[3])
+        gelu(gelu_lower[3][:, M // 2 :], rest3[:])
         for j in range(EARLY):
             gather_citing(j, laid(22 + 2 * j, f"citing{j}", [M], F32)[:])
         z_slots = laid(62, "z_slots", [PACK, M], BF16)
@@ -219,7 +226,6 @@ def tile_list_citation_chain_gate_kernel(tc, tab_words, tab_scales, offs, pos1, 
         z_lower = kept("z_lower", [M, PACK], BF16)
         nc.gpsimd.tensor_scalar(out=z_lower[:], in0=z_slots[:].rearrange("p t m -> p m t"), scalar1=1.0, scalar2=0.0, op0=MULT, op1=ADD)
         empty(upper_banks)
-        deal_w2(0, slice(1, 2), kept("w2_w01", [2 * HALF], U8, "w1_c12"))
         cited45 = laid(80, "cited45", [2, M], F32)
         for j in range(PACK, TILES):
             gather_cited(j, cited45[:, j - PACK, :] if j < PACK + 2 else kept(f"cited{j}", [M], F32)[:])
@@ -232,7 +238,7 @@ def tile_list_citation_chain_gate_kernel(tc, tab_words, tab_scales, offs, pos1, 
         halves = (slice(0, M // 2), slice(M // 2, M))
         deal_w2(1, slice(0, HP), kept("w2_w1", [2 * H], U8, "cited6"))
         early = laid(82, "early", [M // 2], F32)
-        nc.vector.tensor_copy(early[:], h[EARLY][:].indirect(pos2_sb[:, 0 : M // 32]))
+        nc.vector.tensor_copy(early[:], h[PACK][:].indirect(pos2_sb[:, 0 : M // 32]))
 
         z_upper = kept("z_upper", [M, PACK], BF16)
         z_c[1] = kept("z_c1", [M], U32)
@@ -253,8 +259,6 @@ def tile_list_citation_chain_gate_kernel(tc, tab_words, tab_scales, offs, pos1, 
         quantise_upper(halves[0])
         weave_upper(slice(3 * M // 4, M))
         quantise_upper(halves[1])
-        late = kept("late", [M // 2], F32, "gelu_upper")
-        nc.vector.tensor_copy(late[:], h[EARLY][:].indirect(pos2_sb[:, M // 32 :]))
 
         y = {}
 
@@ -262,7 +266,7 @@ def tile_list_citation_chain_gate_kernel(tc, tab_words, tab_scales, offs, pos1, 
             j, ms = piece
             b, t = divmod(j, PACK)
             if a == 0:
-                y[j, ms.start] = psum.tile([P, ms.stop - ms.start], F32, name=f"y{j}", tag="acc")
+                y[j, ms.start] = psum.tile([P, ms.stop - ms.start], F32, name=f"y{j}", tag=f"bank{len(y) % AHEAD}")
             nc.tensor.matmul_mx(
                 out=y[j, ms.start][:],
                 lhsT=w2_w[a, b][:, 2 * t * P : 2 * (t + 1) * P].bitcast(FP4X4),
@@ -274,42 +278,43 @@ def tile_list_citation_chain_gate_kernel(tc, tab_words, tab_scales, offs, pos1, 
             )
 
         whole = slice(0, M)
-        starters = range(EARLY + 1, EARLY + 1 + STARTERS)
-        front = [(j, halves[0]) for j in starters] + [(j, whole) for j in range(EARLY + 1)]
-        back = [(j, halves[1]) for j in starters]
-        last = [(j, whole) for j in range(starters.stop, TILES)]
-        for piece in front + last:
-            second_product(piece, 0)
-        for piece in front:
-            second_product(piece, 1)
-        for piece in back:
-            second_product(piece, 0)
-            second_product(piece, 1)
-        for piece in last:
-            second_product(piece, 1)
-
+        pieces = [(j, ms) for ms in halves for j in range(EARLY, PACK)] + [(j, whole) for j in (0, 5, 1, 6, 4, 7)]
         out_rows = out.rearrange("(b p t) m -> p b t m", b=HP, t=PACK)
-        gates = [laid(28 + 8 * j, f"gate{j}", [M], F32) for j in range(TILES)]
+        gates = {(j, ms.start): laid(28 + 2 * i, f"gate{i}", [ms.stop - ms.start], F32) for i, (j, ms) in enumerate(pieces)}
         gated = [kept(f"gated{j}", [M], F32) for j in range(TILES)]
-        for j, ms in front + back + last:
-            nc.scalar.activation(out=gates[j][:, ms], in_=y[j, ms.start][:], func=ACT.Sigmoid)
 
-        def fused(j, ms):
-            nc.vector.tensor_tensor(gated[j][:, ms], h[j][:].indirect(pos2_sb[:, ms.start // 16 : ms.stop // 16]), gates[j][:, ms], MULT)
+        def sigmoid(piece):
+            j, ms = piece
+            nc.scalar.activation(out=gates[j, ms.start][:], in_=y[j, ms.start][:], func=ACT.Sigmoid)
+
+        def fused(j, ms, gate):
+            nc.vector.tensor_tensor(gated[j][:, ms], h[j][:].indirect(pos2_sb[:, ms.start // 16 : ms.stop // 16]), gate, MULT)
 
         def store(j, ms=whole):
             nc.sync.dma_start(out=out_rows[:, j // PACK, j % PACK, ms], in_=gated[j][:, ms])
 
-        for j, ms in front + back + last[:-1]:
+        def finish(piece):
+            j, ms = piece
+            gate = gates[j, ms.start]
             if j < EARLY:
-                nc.vector.tensor_tensor(out=gated[j][:], in0=gates[j][:], in1=citing[j], op=MULT)
-            elif j == EARLY:
-                for part, picked in zip(halves, (early, late)):
-                    nc.vector.tensor_tensor(out=gated[j][:, part], in0=gates[j][:, part], in1=picked[:], op=MULT)
+                nc.vector.tensor_tensor(out=gated[j][:], in0=gate[:], in1=citing[j], op=MULT)
+            elif j == PACK:
+                nc.vector.tensor_tensor(out=gated[j][:, halves[0]], in0=gate[:, halves[0]], in1=early[:], op=MULT)
+                fused(j, halves[1], gate[:, halves[1]])
+            elif j == TILES - 1:
+                fused(j, halves[0], gate[:, halves[0]])
+                store(j, halves[0])
+                fused(j, halves[1], gate[:, halves[1]])
             else:
-                fused(j, ms)
+                fused(j, ms, gate[:])
             if ms.stop == M:
-                store(j)
-        for ms in halves:
-            fused(TILES - 1, ms)
-            store(TILES - 1, ms)
+                store(j, halves[1] if j == TILES - 1 else whole)
+
+        for piece in pieces[:AHEAD]:
+            second_product(piece, 0)
+        for i, piece in enumerate(pieces):
+            if i >= AHEAD:
+                second_product(piece, 0)
+            second_product(piece, 1)
+            sigmoid(piece)
+            finish(piece)

@@ -254,11 +254,13 @@ def tile_list_citation_chain_gate_kernel(tc, tab_words, tab_scales, offs, pos1, 
         def quantise_upper(ms):
             nc.vector.quantize_mx(out=z_c[1][:, ms].bitcast(FP8X4), scales=z_s[1][:, ms], in_=z_upper[:, ms, :].rearrange("p m t -> p (m t)"))
 
-        weave_upper(halves[0])
-        weave_upper(slice(M // 2, 3 * M // 4))
-        quantise_upper(halves[0])
-        weave_upper(slice(3 * M // 4, M))
-        quantise_upper(halves[1])
+        for ms in halves:
+            weave_upper(ms)
+        for ms in halves:
+            quantise_upper(ms)
+        late = kept("late", [2, M // 2], F32, "gelu_upper")
+        nc.vector.tensor_copy(late[:, 0, :], h[PACK][:].indirect(pos2_sb[:, M // 32 :]))
+        nc.vector.tensor_copy(late[:, 1, :], h[PACK + 1][:].indirect(pos2_sb[:, 0 : M // 32]))
 
         y = {}
 
@@ -300,6 +302,9 @@ def tile_list_citation_chain_gate_kernel(tc, tab_words, tab_scales, offs, pos1, 
                 nc.vector.tensor_tensor(out=gated[j][:], in0=gate[:], in1=citing[j], op=MULT)
             elif j == PACK:
                 nc.vector.tensor_tensor(out=gated[j][:, halves[0]], in0=gate[:, halves[0]], in1=early[:], op=MULT)
+                nc.vector.tensor_tensor(out=gated[j][:, halves[1]], in0=gate[:, halves[1]], in1=late[:, 0, :], op=MULT)
+            elif j == PACK + 1:
+                nc.vector.tensor_tensor(out=gated[j][:, halves[0]], in0=gate[:, halves[0]], in1=late[:, 1, :], op=MULT)
                 fused(j, halves[1], gate[:, halves[1]])
             elif j == TILES - 1:
                 fused(j, halves[0], gate[:, halves[0]])

@@ -25,6 +25,7 @@ HP = H // HALF
 TILES = H // P
 BANK = 512
 KIB = 1024
+SCALAR_QUADS = 88
 BANKS = 8
 AHEAD = 5
 EARLY = 2
@@ -190,20 +191,20 @@ def tile_list_citation_chain_gate_kernel(tc, tab_words, tab_scales, offs, pos1, 
         quantise_w1(1, 0, rounded10)
         for j in range(PACK - 1):
             gather_cited(j, laid(44 + 2 * j, f"cited{j}", [M], F32)[:])
-        cited[3] = laid(50, "cited3", [M // 2], F32)[:]
-        nc.vector.tensor_copy(cited[3], h[3][:].indirect(pos1_sb[:, : M // 32]))
         for bank in upper_banks:
             first_product(bank, 0)
         rounded11 = laid(72, "rounded11", [HALF * PACK], BF16)
         round_w1(gpsimd_copy, rounded11, raw11)
         quantise_w1(1, 1, rounded11)
         rounded12 = laid(60, "rounded12", [HALF * PACK], BF16)
-        round_w1(nc.scalar.copy, rounded12, raw12, slice(0, P // 2))
-        round_w1(nc.vector.tensor_copy, rounded12, raw12, slice(P // 2, P))
-        rest3 = laid(52, "rest3", [M // 2], F32)
-        nc.vector.tensor_copy(rest3[:], h[3][:].indirect(pos1_sb[:, M // 32 :]))
+        round_w1(nc.scalar.copy, rounded12, raw12, slice(0, SCALAR_QUADS))
+        round_w1(nc.vector.tensor_copy, rounded12, raw12, slice(SCALAR_QUADS, P))
+        cited[3] = laid(52, "cited3", [M], F32)[:]
+        nc.vector.tensor_copy(cited[3][:, : M // 2], h[3][:].indirect(pos1_sb[:, : M // 32]))
         quantise_w1(1, 2, rounded12[:, : 2 * HALF], slice(0, 2))
         quantise_w1(1, 2, rounded12[:, 2 * HALF :], slice(2, PACK))
+        rest3 = laid(26, "rest3", [M // 2], F32)
+        nc.vector.tensor_copy(rest3[:], h[3][:].indirect(pos1_sb[:, M // 32 :]))
         for bank in upper_banks[:LEAD]:
             first_product(bank, 1)
         for i, bank in enumerate(upper_banks):
@@ -216,7 +217,7 @@ def tile_list_citation_chain_gate_kernel(tc, tab_words, tab_scales, offs, pos1, 
         for t in range(PACK - 1):
             gelu(gelu_lower[t], cited[t])
         deal_w2(0, slice(0, HP), kept("w2_w0", [2 * H], U8))
-        gelu(gelu_lower[3][:, : M // 2], cited[3])
+        gelu(gelu_lower[3][:, : M // 2], cited[3][:, : M // 2])
         gelu(gelu_lower[3][:, M // 2 :], rest3[:])
         for j in range(EARLY):
             gather_citing(j, laid(22 + 2 * j, f"citing{j}", [M], F32)[:])

@@ -128,23 +128,35 @@ def tile_list_citation_chain_gate_kernel(tc, tab_words, tab_scales, offs, pos1, 
 
         z_s = [kept(f"z_s{b}", [M], U8) for b in range(HP)]
 
-        nc.vector.memset(tab_sc[:].bitcast(I32), 0)
         w2_s_raw = kept("w2_s_raw", [HP, H], U8)
         nc.vector.memset(w2_s_raw[:].rearrange("p a n -> p (a n)").bitcast(I32), 0)
+        nc.vector.memset(tab_sc[:].bitcast(I32), 0)
         load_tab(0, laid(0, "tab0", [T], I32))
         nc.sync.dma_start(offs_sb[:], offs)
         raw00 = load_w1(0, 0, HALF, laid(20, "raw00", [PACK, HALF], F32))
         raw01 = load_w1(1, 0, HALF, laid(40, "raw01", [PACK, HALF], F32))
         nc.sync.dma_start(pos1_sb[:], pos1)
         nc.sync.dma_start(pos2_sb[:], pos2)
-        for q in range(4):
+
+        def load_tab_scales(q):
             nc.gpsimd.dma_start(
                 out=tab_sc[32 * q + 4 : 32 * q + 4 + 4 * KP, :].bitcast(I32),
                 in_=tab_scales[:, 4 * q : 4 * q + 4, :].bitcast(I32),
             )
-        for q in range(4):
-            rows = w2_scales[:, 4 * q : 4 * q + 4, :]
-            nc.gpsimd.dma_start(out=w2_s_raw[32 * q : 32 * q + 4, :, :].bitcast(I32), in_=rows.rearrange("a r n -> r a n").bitcast(I32))
+
+        def load_w2_scales(q, r0=0, r1=4):
+            rows = w2_scales[:, 4 * q + r0 : 4 * q + r1, :]
+            nc.gpsimd.dma_start(out=w2_s_raw[32 * q + r0 : 32 * q + r1, :, :].bitcast(I32), in_=rows.rearrange("a r n -> r a n").bitcast(I32))
+
+        load_w2_scales(0)
+        load_tab_scales(3)
+        load_w2_scales(1, 0, 2)
+        load_tab_scales(2)
+        load_tab_scales(1)
+        load_w2_scales(1, 2, 4)
+        load_tab_scales(0)
+        load_w2_scales(2)
+        load_w2_scales(3)
 
         warm = kept("warm", [1], F32)
         nc.gpsimd.memset(warm[:], 0.0)

from contextlib import ExitStack

import concourse.mybir as mybir

K, H, T, S, M = 1536, 1024, 4096, 1024, 512
FLOPS = 2 * K * H * S + 2 * H * H * M

F32 = mybir.dt.float32
BF16 = mybir.dt.bfloat16
I32 = mybir.dt.int32
U32 = mybir.dt.uint32
U16 = mybir.dt.uint16
U8 = mybir.dt.uint8
FP8X4 = mybir.dt.float8_e4m3fn_x4
FP4X4 = mybir.dt.float4_e2m1fn_x4
ACT = mybir.ActivationFunctionType
MULT = mybir.AluOpType.mult
ADD = mybir.AluOpType.add

P = 128
PACK = 4
HALF = P * PACK
KP = K // HALF
HP = H // HALF
TILES = H // P
BANK = 512
KIB = 1024
SCALAR_QUADS = 88
BANKS = 8
AHEAD = 5
EARLY = 2
LEAD = 5


def tile_list_citation_chain_gate_kernel(tc, tab_words, tab_scales, offs, pos1, pos2, w1, gain, w2_words, w2_scales, out):
    nc = tc.nc
    with ExitStack() as ctx:
        keep = ctx.enter_context(tc.tile_pool(name="keep", bufs=1))
        arena = ctx.enter_context(tc.tile_pool(name="arena", bufs=1))
        psum = ctx.enter_context(tc.psum_pool(name="psum", bufs=1))

        def kept(name, shape, dtype, tag=None):
            return keep.tile([P] + shape, dtype, name=name, tag=tag or name, align_bytes=64)

        def laid(kib, name, shape, dtype):
            return arena.tile([P] + shape, dtype, name=name, offset=kib * KIB, align_bytes=64)

        offs_sb = kept("offs_sb", [S // 16], U16)
        pos1_sb = kept("pos1_sb", [M // 16], U16)
        pos2_sb = kept("pos2_sb", [M // 16], U16)
        tab_sc = kept("tab_sc", [T], U8)
        v_s = kept("v_s", [S], U8)
        tab, v_w, w1_c, w1_s, w2_raw, w2_w, w2_s = {}, {}, {}, {}, {}, {}, {}
        acc, cited, citing, z_c = {}, {}, {}, {}

        def load_tab(a, tile):
            tab[a] = tile
            nc.sync.dma_start(out=tile[:], in_=tab_words[a].rearrange("p t i -> p (t i)").bitcast(I32))

        def load_w1(a, c0, width, tile):
            rows = w1[a * HALF : (a + 1) * HALF, c0 : c0 + width]
            nc.sync.dma_start(out=tile[:], in_=rows.rearrange("(p j) n -> p j n", j=PACK))
            return tile

        def load_w2(a, tile):
            w2_raw[a] = tile
            nc.sync.dma_start(out=tile[:].bitcast(I32), in_=w2_words[a].bitcast(I32))

        def gather_tab(a, pieces, tag=None):
            v_w[a] = kept(f"v_w{a}", [S], U32, tag)
            step = S // pieces
            for s0 in range(0, S, step):
                nc.vector.tensor_copy(v_w[a][:, s0 : s0 + step], tab[a][:].bitcast(U32).indirect(offs_sb[:, s0 // 16 : (s0 + step) // 16]))

        def round_w1(copy, tile, raw, quads=slice(0, P)):
            copy(
                out=tile[:].rearrange("p (t m j) -> p m j t", m=P, j=PACK)[:, quads],
                in_=raw[:].rearrange("p j (m t) -> p m j t", t=PACK)[:, quads],
            )

        def gpsimd_copy(out, in_):
            nc.gpsimd.tensor_scalar(out=out.rearrange("p m j t -> p m t j"), in0=in_.rearrange("p m j t -> p m t j"), scalar1=1.0, scalar2=0.0, op0=MULT, op1=ADD)

        def quantise_w1(b, a, tile, ts=slice(0, PACK), codes=None):
            if ts.start == 0:
                w1_c[b, a] = kept(f"w1_c{b}{a}", [HALF], U32) if codes is None else codes
                w1_s[b, a] = kept(f"w1_s{b}{a}", [HALF], U8)
            cols = slice(ts.start * P, ts.stop * P)
            nc.vector.quantize_mx(out=w1_c[b, a][:, cols].bitcast(FP8X4), scales=w1_s[b, a][:, cols], in_=tile[:, :])

        h = [kept(f"h{j}", [S], F32) for j in range(TILES)]

        def first_product(bank, a):
            j, s = bank
            if a == 0:
                acc[bank] = psum.tile([P, BANK], F32, name=f"acc{j}{s}", tag=f"bank{len(acc) % BANKS}")
            b, t = divmod(j, PACK)
            nc.tensor.matmul_mx(
                out=acc[bank][:],
                lhsT=w1_c[b, a][:, t * P : (t + 1) * P].bitcast(FP8X4),
                lhsT_scale=w1_s[b, a][:, t * P : (t + 1) * P],
                rhs=v_w[a][:, s * BANK : (s + 1) * BANK].bitcast(FP8X4),
                rhs_scale=v_s[4 + 4 * a :, s * BANK : (s + 1) * BANK],
                start=(a == 0),
                stop=(a == KP - 1),
            )

        def empty(banks):
            for j, s in banks:
                nc.scalar.copy(out=h[j][:, s * BANK : (s + 1) * BANK], in_=acc[j, s][:])

        def gather_cited(j, into):
            cited[j] = into
            nc.vector.tensor_copy(into, h[j][:].indirect(pos1_sb[:]))

        def gather_citing(j, into):
            citing[j] = into
            nc.vector.tensor_copy(into, h[j][:].indirect(pos2_sb[:]))

        def gelu(dst, src):
            nc.scalar.activation(out=dst, in_=src, func=ACT.Gelu_apprx_tanh)

        def deal_w2(a, halves_of_h, tile):
            words = w2_raw[a][:].bitcast(U16).rearrange("p (b m t) -> p b m t", b=HP, t=PACK)
            nc.scalar.copy(out=tile[:].bitcast(U16).rearrange("p (b t m) -> p b m t", t=PACK, m=P), in_=words[:, halves_of_h])
            for b in range(halves_of_h.start, halves_of_h.stop):
                w2_w[a, b] = tile[:, (b - halves_of_h.start) * 2 * HALF : (b - halves_of_h.start + 1) * 2 * HALF]

        z_s = [kept(f"z_s{b}", [M], U8) for b in range(HP)]

        w2_s_raw = kept("w2_s_raw", [HP, H], U8)
        nc.vector.memset(w2_s_raw[:].rearrange("p a n -> p (a n)").bitcast(I32), 0)
        nc.vector.memset(tab_sc[:].bitcast(I32), 0)
        load_tab(0, laid(0, "tab0", [T], I32))
        nc.sync.dma_start(offs_sb[:], offs)
        raw00 = load_w1(0, 0, HALF, laid(20, "raw00", [PACK, HALF], F32))
        raw01 = load_w1(1, 0, HALF, laid(40, "raw01", [PACK, HALF], F32))
        nc.sync.dma_start(pos1_sb[:], pos1)
        nc.sync.dma_start(pos2_sb[:], pos2)

        def load_tab_scales(q):
            nc.gpsimd.dma_start(
                out=tab_sc[32 * q + 4 : 32 * q + 4 + 4 * KP, :].bitcast(I32),
                in_=tab_scales[:, 4 * q : 4 * q + 4, :].bitcast(I32),
            )

        def load_w2_scales(q, r0=0, r1=4):
            rows = w2_scales[:, 4 * q + r0 : 4 * q + r1, :]
            nc.gpsimd.dma_start(out=w2_s_raw[32 * q + r0 : 32 * q + r1, :, :].bitcast(I32), in_=rows.rearrange("a r n -> r a n").bitcast(I32))

        load_w2_scales(0)
        load_tab_scales(3)
        load_w2_scales(1, 0, 2)
        load_tab_scales(2)
        load_tab_scales(1)
        load_w2_scales(1, 2, 4)
        load_tab_scales(0)
        load_w2_scales(2)
        load_w2_scales(3)

        warm = kept("warm", [1], F32)
        nc.gpsimd.memset(warm[:], 0.0)
        nc.scalar.activation(out=warm[:], in_=warm[:], func=ACT.Gelu_apprx_tanh)

        gather_tab(0, 1)
        load_tab(1, laid(0, "tab1", [T], I32))
        rounded00 = kept("rounded00", [HALF * PACK], BF16)
        round_w1(nc.scalar.copy, rounded00, raw00)
        quantise_w1(0, 0, rounded00)
        raw02 = load_w1(2, 0, HALF, laid(20, "raw02", [PACK, HALF], F32))
        rounded01 = laid(52, "rounded01", [HALF * PACK], BF16)
        round_w1(nc.scalar.copy, rounded01, raw01)
        quantise_w1(0, 1, rounded01)
        load_tab(2, laid(28, "tab2", [T], I32))
        raw10 = load_w1(0, HALF, HALF, laid(44, "raw10", [PACK, HALF], F32))
        raw11 = load_w1(1, HALF, HALF, laid(52, "raw11", [PACK, HALF], F32))
        nc.vector.tensor_copy(v_s[:], tab_sc[:].indirect(offs_sb[:]))
        gather_tab(1, 1, "tab_sc")
        for b in range(HP):
            w2_s[b] = laid(2 + b, f"w2_s{b}", [HP, HALF], U8)
            nc.vector.tensor_copy(
                out=w2_s[b][:].rearrange("p a (t m) -> p a t m", t=PACK),
                in_=w2_s_raw[:, :, b * HALF : (b + 1) * HALF].rearrange("p a (m t) -> p a t m", t=PACK),
            )
        rounded02 = laid(90, "rounded02", [HALF * PACK], BF16)
        round_w1(nc.scalar.copy, rounded02, raw02)
        quantise_w1(0, 2, rounded02, codes=laid(0, "w1_c02", [HALF], U32))
        raw12 = load_w1(2, HALF, HALF, laid(20, "raw12", [PACK, HALF], F32))
        gains = laid(91, "gains", [HP, PACK], F32)
        nc.sync.dma_start(out=gains[:], in_=gain.rearrange("(b p t) -> p b t", b=HP, t=PACK))
        load_w2(0, laid(89, "w2_raw0", [2 * H], U8))
        load_w2(1, laid(92, "w2_raw1", [2 * H], U8))
        gather_tab(2, 2)
        lower_banks = [(0, 0), (1, 0), (0, 1), (1, 1), (2, 0), (2, 1), (3, 0), (3, 1)]
        upper_banks = [(j, s) for j in range(PACK, TILES) for s in range(S // BANK)]
        for a in range(KP):
            for bank in lower_banks:
                first_product(bank, a)
        empty(lower_banks)

        rounded10 = laid(72, "rounded10", [HALF * PACK], BF16)
        round_w1(nc.vector.tensor_copy, rounded10, raw10)
        quantise_w1(1, 0, rounded10)
        for j in range(PACK - 1):
            gather_cited(j, laid(44 + 2 * j, f"cited{j}", [M], F32)[:])
        for bank in upper_banks:
            first_product(bank, 0)
        rounded11 = laid(72, "rounded11", [HALF * PACK], BF16)
        round_w1(gpsimd_copy, rounded11, raw11)
        quantise_w1(1, 1, rounded11)
        rounded12 = laid(60, "rounded12", [HALF * PACK], BF16)
        round_w1(nc.scalar.copy, rounded12, raw12, slice(0, SCALAR_QUADS))
        round_w1(nc.vector.tensor_copy, rounded12, raw12, slice(SCALAR_QUADS, P))
        cited[3] = laid(52, "cited3", [M], F32)[:]
        nc.vector.tensor_copy(cited[3][:, : M // 2], h[3][:].indirect(pos1_sb[:, : M // 32]))
        quantise_w1(1, 2, rounded12[:, : 2 * HALF], slice(0, 2))
        quantise_w1(1, 2, rounded12[:, 2 * HALF :], slice(2, PACK))
        rest3 = laid(26, "rest3", [M // 2], F32)
        nc.vector.tensor_copy(rest3[:], h[3][:].indirect(pos1_sb[:, M // 32 :]))
        for bank in upper_banks[:LEAD]:
            first_product(bank, 1)
        for i, bank in enumerate(upper_banks):
            first_product(bank, 2)
            for ahead in upper_banks[i + LEAD : i + LEAD + 1]:
                first_product(ahead, 1)

        gelu_rest = laid(16, "gelu_rest", [PACK - 1, M], F32)
        gelu_lower = [kept("gelu0", [M], F32)[:]] + [gelu_rest[:, t, :] for t in range(PACK - 1)]
        for t in range(PACK - 1):
            gelu(gelu_lower[t], cited[t])
        deal_w2(0, slice(0, HP), kept("w2_w0", [2 * H], U8))
        gelu(gelu_lower[3][:, : M // 2], cited[3][:, : M // 2])
        gelu(gelu_lower[3][:, M // 2 :], rest3[:])
        for j in range(EARLY):
            gather_citing(j, laid(22 + 2 * j, f"citing{j}", [M], F32)[:])
        z_slots = laid(62, "z_slots", [PACK, M], BF16)
        for t in range(PACK):
            nc.gpsimd.tensor_scalar(out=z_slots[:, t, :], in0=gelu_lower[t], scalar1=gains[:, 0, t : t + 1], scalar2=0.0, op0=MULT, op1=ADD)
        z_lower = kept("z_lower", [M, PACK], BF16)
        nc.gpsimd.tensor_scalar(out=z_lower[:], in0=z_slots[:].rearrange("p t m -> p m t"), scalar1=1.0, scalar2=0.0, op0=MULT, op1=ADD)
        empty(upper_banks)
        cited45 = laid(80, "cited45", [2, M], F32)
        for j in range(PACK, TILES):
            gather_cited(j, cited45[:, j - PACK, :] if j < PACK + 2 else kept(f"cited{j}", [M], F32)[:])
        gelu_upper = kept("gelu_upper", [PACK, M], F32)
        gelu(gelu_upper[:, 0:2, :], cited45[:])
        for j in range(PACK + 2, TILES):
            gelu(gelu_upper[:, j - PACK, :], cited[j])
        z_c[0] = laid(80, "z_c0", [M], U32)
        nc.vector.quantize_mx(out=z_c[0][:].bitcast(FP8X4), scales=z_s[0][:], in_=z_lower[:].rearrange("p m t -> p (m t)"))
        halves = (slice(0, M // 2), slice(M // 2, M))
        deal_w2(1, slice(0, HP), kept("w2_w1", [2 * H], U8, "cited6"))
        early = laid(82, "early", [M // 2], F32)
        nc.vector.tensor_copy(early[:], h[PACK][:].indirect(pos2_sb[:, 0 : M // 32]))

        z_upper = kept("z_upper", [M, PACK], BF16)
        z_c[1] = kept("z_c1", [M], U32)

        def weave_upper(ms):
            nc.vector.tensor_tensor(
                out=z_upper[:, ms, :].rearrange("p (g i) t -> p g t i", i=4),
                in0=gelu_upper[:, :, ms].rearrange("p t (g i) -> p g t i", i=4),
                in1=gains[:, 1, :].unsqueeze(1).unsqueeze(3).to_broadcast([P, (ms.stop - ms.start) // 4, PACK, 4]),
                op=MULT,
            )

        def quantise_upper(ms):
            nc.vector.quantize_mx(out=z_c[1][:, ms].bitcast(FP8X4), scales=z_s[1][:, ms], in_=z_upper[:, ms, :].rearrange("p m t -> p (m t)"))

        for ms in halves:
            weave_upper(ms)
        for ms in halves:
            quantise_upper(ms)
        late = kept("late", [2, M // 2], F32, "gelu_upper")
        nc.vector.tensor_copy(late[:, 0, :], h[PACK][:].indirect(pos2_sb[:, M // 32 :]))
        nc.vector.tensor_copy(late[:, 1, :], h[PACK + 1][:].indirect(pos2_sb[:, 0 : M // 32]))

        y = {}

        def second_product(piece, a):
            j, ms = piece
            b, t = divmod(j, PACK)
            if a == 0:
                y[j, ms.start] = psum.tile([P, ms.stop - ms.start], F32, name=f"y{j}", tag=f"bank{len(y) % AHEAD}")
            nc.tensor.matmul_mx(
                out=y[j, ms.start][:],
                lhsT=w2_w[a, b][:, 2 * t * P : 2 * (t + 1) * P].bitcast(FP4X4),
                lhsT_scale=w2_s[b][:, a, t * P : (t + 1) * P],
                rhs=z_c[a][:, ms].bitcast(FP8X4),
                rhs_scale=z_s[a][:, ms],
                start=(a == 0),
                stop=(a == HP - 1),
            )

        whole = slice(0, M)
        pieces = [(j, ms) for ms in halves for j in range(EARLY, PACK)] + [(j, whole) for j in (0, 5, 1, 6, 4, 7)]
        out_rows = out.rearrange("(b p t) m -> p b t m", b=HP, t=PACK)
        gates = {(j, ms.start): laid(28 + 2 * i, f"gate{i}", [ms.stop - ms.start], F32) for i, (j, ms) in enumerate(pieces)}
        gated = [kept(f"gated{j}", [M], F32) for j in range(TILES)]

        def sigmoid(piece):
            j, ms = piece
            nc.scalar.activation(out=gates[j, ms.start][:], in_=y[j, ms.start][:], func=ACT.Sigmoid)

        def fused(j, ms, gate):
            nc.vector.tensor_tensor(gated[j][:, ms], h[j][:].indirect(pos2_sb[:, ms.start // 16 : ms.stop // 16]), gate, MULT)

        def store(j, ms=whole):
            nc.sync.dma_start(out=out_rows[:, j // PACK, j % PACK, ms], in_=gated[j][:, ms])

        def finish(piece):
            j, ms = piece
            gate = gates[j, ms.start]
            if j < EARLY:
                nc.vector.tensor_tensor(out=gated[j][:], in0=gate[:], in1=citing[j], op=MULT)
            elif j == PACK:
                nc.vector.tensor_tensor(out=gated[j][:, halves[0]], in0=gate[:, halves[0]], in1=early[:], op=MULT)
                nc.vector.tensor_tensor(out=gated[j][:, halves[1]], in0=gate[:, halves[1]], in1=late[:, 0, :], op=MULT)
            elif j == PACK + 1:
                nc.vector.tensor_tensor(out=gated[j][:, halves[0]], in0=gate[:, halves[0]], in1=late[:, 1, :], op=MULT)
                fused(j, halves[1], gate[:, halves[1]])
            elif j == TILES - 1:
                fused(j, halves[0], gate[:, halves[0]])
                store(j, halves[0])
                fused(j, halves[1], gate[:, halves[1]])
            else:
                fused(j, ms, gate[:])
            if ms.stop == M:
                store(j, halves[1] if j == TILES - 1 else whole)

        for piece in pieces[:AHEAD]:
            second_product(piece, 0)
        for i, piece in enumerate(pieces):
            if i >= AHEAD:
                second_product(piece, 0)
            second_product(piece, 1)
            sigmoid(piece)
            finish(piece)
